import numpy as np, ml_dtypes
CORES = [83,85,87,115,117,119]
N = 6
BF = ml_dtypes.bfloat16
W, L, S, T, F = 4096, 192, 1, 6, 64
C = W >> S
LEVELS = np.array([800, 900, 1000, 1050, 1100, 1150, 1250, 1400])
def parts(rng):
    d = {"key": rng.integers(0, 256, (N, 8, 16, W)), "em": rng.integers(0, 256, (N, 8, 16, W)), "cl": rng.integers(0, W, (N, 8, 16, C)), "pl": rng.integers(0, W, (N, 8, 16, L)),
         "q": rng.integers(0, 256, (N, 8, 16, L)), "emb": rng.integers(0, 256, (N, 8, 16, 16)), "w": rng.integers(0, 256, (N, 8, 16, 1))}
    base = np.stack([rng.permutation(LEVELS) for r in range(N)]).reshape(N, 8, 1, 1)
    d["th"] = base + rng.integers(-100, 101, (N, 8, 16, 1))
    return d
def pack(d):
    kinds = {"key": BF, "em": BF, "cl": np.int32, "pl": np.int32, "q": BF, "emb": BF, "w": BF, "th": np.float32}
    return {k: np.ascontiguousarray(d[k].reshape(N, 128, -1)).astype(np.float32).astype(t) for k, t in kinds.items()}
def setup_inputs(rng):
    return pack(parts(rng))
def setup_inputs_ties(rng):
    d = parts(rng); o = rng.permutation(8)
    for k in ("key", "q", "emb"): d[k] = 64 * rng.integers(0, 4, d[k].shape)
    d["th"] = 64 * rng.integers(16, 23, (N, 8, 16, 1)) + rng.integers(0, 2, (N, 8, 16, 1))
    d["em"] = rng.integers(0, 2, (N, 8, 16, W)) * rng.choice(np.array([1, 3, 255]), (N, 8, 1, 1))
    d["em"][:, o[0]] = 7; d["em"][:, o[1]] = 0
    for k in ("key", "q", "emb"):
        d[k][:, o[2]] = 0
        d[k][:, o[3]] = rng.integers(0, 32, d[k][:, o[3]].shape)
    d["th"][:, o[2], :, 0] = rng.permutation(np.arange(16) % 3)
    d["th"][:, o[3]] = rng.integers(1, 256, (N, 16, 1))
    return pack(d)
def setup_inputs_ends(rng):
    d = parts(rng); o = rng.permutation(8); ends = np.array([0, 1, W - 2, W - 1])
    d["pl"][:, o[0]] = rng.choice(ends, (N, 16, L)); d["th"][:, o[0]] = 4096
    d["th"][:, o[1]] = 0
    d["pl"][:, o[2]] = rng.integers(0, W, (N, 1, L))
    d["cl"][:, o[3]] = rng.choice(ends, (N, 16, C)); d["th"][:, o[3]] = 1000
    d["cl"][:, o[4]] = rng.integers(0, W, (N, 1, C))
    d["key"][:, o[5]] = d["key"][:, o[5]][:, :, :1]
    d["pl"][:, o[6]] = rng.choice(ends, (N, 16, L))
    d["th"][:, o[7]] = 0; d["w"][:, o[7]] = 0
    return pack(d)
def setup_inputs_lone(rng):
    d = parts(rng); d["th"] = np.zeros((N, 8, 16, 1), np.int64)
    for r in range(N):
        o = rng.permutation(8)
        d["th"][r, o[1], 0] = 4096; d["th"][r, o[2], 15] = 4096; d["th"][r, o[3], 14:] = 4096
        for g in o[4:]: d["th"][r, g, rng.integers(1, 15)] = 4096
    d["th"][rng.integers(0, N)] = 0
    return pack(d)
def setup_inputs_big(rng):
    d = parts(rng); o = rng.permutation(8)
    for k in ("key", "em", "q", "emb"): d[k] = 255 * rng.integers(0, 2, d[k].shape)
    d["w"] = rng.integers(254, 256, d["w"].shape)
    d["th"] = rng.choice(np.array([1785, 1786, 2040, 2041, 2295, 1020, 4080, 4081]), (N, 8, 16, 1))
    d["key"][:, o[0]] = 0; d["q"][:, o[0]] = 255; d["emb"][:, o[0]] = 255; d["w"][:, o[0]] = 255
    d["th"][:, o[0], :, 0] = 4080 + np.arange(16) % 2
    d["em"][:, o[1]] = 255
    d["th"][:, o[2]] = 0
    d["th"][:, o[3]] = 0; d["q"][:, o[3]] = 255; d["emb"][:, o[3]] = 255; d["w"][:, o[3]] = 255
    d["em"][:, o[4]] = 255 - (rng.random((N, 16, W)) < 0.0625)
    return pack(d)
def setup_inputs_spread(rng):
    d = parts(rng)
    for k in ("key", "em", "q", "emb"):
        s = d[k].shape
        d[k] = np.minimum((np.exp2(10 * rng.random(s[:2] + (1, s[3]))) * rng.random(s)).astype(np.int64), 255)
    d["w"] = np.minimum(np.exp2(8 * rng.random(d["w"].shape)).astype(np.int64), 255)
    d["th"] = np.minimum(np.exp2(8 + 4 * rng.random((N, 8, 16, 1))).astype(np.int64), 4096)
    for k in ("pl", "cl"): d[k] = np.minimum((W * rng.random(d[k].shape) ** 3).astype(np.int64), W - 1)
    return pack(d)
def check_inputs(d):
    bad = []
    for k, hi in (("key", 255), ("em", 255), ("cl", W - 1), ("pl", W - 1), ("q", 255), ("emb", 255), ("w", 255), ("th", 4096)):
        a = np.asarray(d[k]).astype(np.float64)
        if not np.all((a >= 0) & (a <= hi) & (a == np.floor(a))): bad.append("whole numbers and range of " + k)
    return bad
def reference(key, em, cl, pl, q, emb, w, th):
    def ints(a): return a.astype(np.float32).astype(np.int32).reshape(N, 8, 16, -1)
    K, E, CL, B, H, TH = ints(key), ints(em), ints(cl), ints(emb), ints(w), ints(th)
    p, x = ints(pl), ints(q)
    toks = [[] for r in range(N)]
    for t in range(T):
        pn, xn = [], []
        for r in range(N):
            at = np.take_along_axis(K[r], p[r].reshape(8, 1, 16 * L), 2).reshape(8, 16, 16, L)
            dist = np.add.reduce(np.abs(at - x[r][:, :, None, :]), axis=1)
            near = dist < TH[r]
            first = np.argmax(near, axis=1)
            lead = np.take_along_axis(p[r], first[:, None, :], 1)[:, 0]
            h = np.add.reduce(H[r] * x[r], axis=1)
            c = np.where(np.any(near, axis=1), lead >> S, h & (C - 1))
            pr = np.where(near, p[r], np.take_along_axis(CL[r], c[:, None, :], 2))
            v = np.add.reduce(np.take_along_axis(E[r], pr.reshape(8, 1, 16 * L), 2).reshape(8, 16, 16, L), axis=2)
            tok = np.argmax(v, axis=1)
            toks[r].append(tok)
            xn.append((x[r] + np.take_along_axis(B[r], tok[:, :, None], 1).transpose(0, 2, 1)) >> 1); pn.append(pr)
        p = np.stack([np.concatenate([(pn[(r - 1) % N][..., :F] + (1 if r == 0 else 0)) & (W - 1), (pn[(r + 1) % N][..., F:] - (1 if r == N - 1 else 0)) & (W - 1)], axis=2) for r in range(N)])
        x = np.stack([np.concatenate([xn[(r - 1) % N][..., :F], xn[(r + 1) % N][..., F:]], axis=2) for r in range(N)])
    yt = np.stack([np.concatenate(a, axis=1) for a in toks])
    return {"yp": p.reshape(N, 128, L).astype(np.float32), "yq": x.reshape(N, 128, L).astype(np.float32).astype(BF), "yt": yt.astype(np.float32)}

@@ -1,0 +1,401 @@
+import numpy as np
+from concourse.mybir import AluOpType, ActivationFunctionType
+
+A = AluOpType
+F = ActivationFunctionType
+NL = 64
+NS = 16
+NC = 3
+STEPS = 6
+PL = 4096
+BIG = 12582912.0
+P = {
+    "K": (("S", 64),),
+    "E": (("S", 48), ("V", 16)),
+    "M": (64,),
+    "look": 0.1, "seed": 0, "noise": 0.0, "stag": (0.0, 0.0, 0.0),
+    "cy": 0.83e-3 * 1.2, "gather": 1.5, "hop": 0.1, "net": 2.6, "pe": 0.55e-3, "fix": 0.02,
+}
+
+BF, F3, I3, U1, H1 = "bfloat16", "float32", "int32", "uint16", "float16"
+SCRATCH = {
+    "key_s": ("sbuf", [128, 4096], BF), "em_s": ("sbuf", [128, 4096], BF), "cl_s": ("sbuf", [128, 2048], I3),
+    "pl_s": ("sbuf", [128, 192], I3), "emb_s": ("sbuf", [128, 16], BF), "w_s": ("sbuf", [128, 1], BF), "th_s": ("sbuf", [128, 1], F3),
+    "pin": ("sbuf", [128, 7 * 192], U1), "qin": ("sbuf", [128, 7 * 192], BF),
+    "pout": ("sbuf", [128, 6 * 192], U1), "pw": ("sbuf", [128, 6 * 192], U1), "qout": ("sbuf", [128, 6 * 192], BF),
+    "yp_s": ("sbuf", [128, 192], F3), "yt_s": ("sbuf", [128, 1152], F3),
+    "wk": ("sbuf", [128, 2048], BF), "w2": ("sbuf", [128, 2048], BF),
+    "tw": ("sbuf", [128, 8], BF), "bdc": ("sbuf", [128, 8], F3),
+    "bdh": ("sbuf", [128, 128], H1), "idh": ("sbuf", [128, 128], H1), "c1023": ("sbuf", [128, 64], H1),
+    "rep": ("sbuf", [128, 64], U1), "rst32": ("sbuf", [128, 128], F3),
+}
+for _n in ("ones", "bd", "idm", "ltm", "gw0", "gw", "sg", "nbd", "bd4k", "i16", "i8k", "ihf", "in2k", "bdw", "eb"):
+    SCRATCH[_n] = ("sbuf", [128, 128], BF)
+for _n in ("mb", "mb2", "cb", "ck", "ckb", "cq"):
+    SCRATCH[_n] = ("sbuf", [128, 64], BF)
+for _n in ("icol", "kint", "gint"):
+    SCRATCH[_n] = ("sbuf", [128, 1], I3)
+for _n in ("kcol", "gcol", "sgcol"):
+    SCRATCH[_n] = ("sbuf", [128, 1], F3)
+for _n, _d in (("rowm", F3), ("rowl", I3), ("rowb", F3), ("zero", F3), ("big16", F3)):
+    SCRATCH[_n] = ("sbuf", [128, 64], _d)
+for _c in range(NC):
+    for _n, _w, _d in (("kg", 1024, BF), ("mx", 1024, BF), ("eg", 1024, BF), ("ph", 64, H1), ("pc", 64, I3), ("nr", 64, BF), ("ar", 64, F3),
+                       ("xx", 64, H1), ("hy", 64, F3), ("hn", 64, BF), ("sc", 128, F3), ("ci", 4, U1), ("pf", 64, I3),
+                       ("s1", 64, I3), ("s2", 64, I3), ("s3", 64, I3), ("vt", 64, F3), ("vs", 80, F3), ("oh", 64, BF), ("ot", 64, BF)):
+        SCRATCH["%s%d" % (_n, _c)] = ("sbuf", [128, _w], _d)
+    SCRATCH["psd%d" % _c] = ("psum", [128, 512], F3)
+    SCRATCH["psx%d" % _c] = ("psum", [128, 512], F3)
+
+SEMAPHORES = (["sV", "sS", "sP", "sG", "lsem", "outs"] + ["ld_" + n for n in ("key", "em", "cl", "pl", "q", "emb", "w", "th")]
+              + ["a%s%d_%d" % (k, c, t) for k in "pq" for c in range(NC) for t in range(1, STEPS + 1)])
+
+
+def plan(ops):
+    n = len(ops)
+    rng = np.random.RandomState(P["seed"])
+    succ = [[] for _ in range(n)]
+    for o in ops:
+        for d in o["deps"] | o["order"]:
+            succ[d].append(o["n"])
+    prio = [0.0] * n
+    for i in range(n - 1, -1, -1):
+        o = ops[i]
+        prio[i] = o["busy"] + o["lat"] + P["hop"] + max([prio[s] for s in succ[i]] + [0.0])
+    prio = [p - P["stag"][o["c"]] for p, o in zip(prio, ops)]
+    if P["noise"]:
+        prio = [p + P["noise"] * float(r) for p, r in zip(prio, rng.standard_normal(n))]
+    missing = [len(o["deps"] | o["order"]) for o in ops]
+    ready = [0.0] * n
+    free = {}
+    start = [0.0] * n
+    cand = [i for i in range(n) if missing[i] == 0]
+    while cand:
+        best, rows = None, []
+        for i in cand:
+            e = ops[i]["eng"]
+            s = ready[i] if e == "NET" else max(free.get(e, 0.0), ready[i])
+            rows.append((s, i, e))
+            if best is None or s < best[0]:
+                best = (s, i, e)
+        lim = best[0] + min(P["look"], ops[best[1]]["busy"])
+        s, i, e = max((r for r in rows if r[2] == best[2] and r[0] <= lim), key=lambda r: (prio[r[1]], -r[1]))
+        o = ops[i]
+        start[i] = s
+        if e != "NET":
+            free[e] = s + o["busy"]
+        fin = s + o["busy"] + o["lat"]
+        cand.remove(i)
+        for j in succ[i]:
+            missing[j] -= 1
+            ready[j] = max(ready[j], fin + P["hop"] if i in ops[j]["deps"] else s)
+            if missing[j] == 0:
+                cand.append(j)
+    return start, max(start[i] + ops[i]["busy"] + ops[i]["lat"] for i in range(n))
+
+
+def build(g, core, T, topo):
+    rank = T.rank_of(core)
+    cores = T.cores
+    N = len(cores)
+    V, S, PE, Y = g.vector, g.scalar, g.tensor, g.sync
+    CY, FIX = P["cy"], P["fix"]
+    ops = []
+    lastw, readers, banks = {}, {}, {}
+    cur = [0]
+
+    def op(eng, emit, reads=(), writes=(), bank=None, busy=0.1, lat=0.0, sem=None, val=0):
+        i = len(ops)
+        deps, order = set(), set()
+        for k in tuple(reads) + tuple(writes):
+            if k in lastw:
+                deps.add(lastw[k])
+        for k in writes:
+            deps.update(readers.get(k, ()))
+        if bank:
+            h = banks.setdefault(bank, {})
+            for e, j in h.items():
+                (order if e == eng else deps).add(j)
+            h[eng] = i
+        for k in reads:
+            readers.setdefault(k, set()).add(i)
+        for k in writes:
+            lastw[k] = i
+            readers[k] = set()
+        ops.append({"n": i, "eng": eng, "emit": emit, "deps": deps, "order": order - deps, "busy": busy, "lat": lat, "sem": sem, "val": val, "c": cur[0]})
+        return i
+
+    def vd(cyc):
+        return max(64, cyc) * CY + FIX
+
+    def vts(out, in0, s1, s2, op0, op1, reads, writes, cyc=64, bank=None):
+        if op1 is None:
+            op("V", lambda: V.tensor_scalar(out, in0, s1, None, op0), reads, writes, bank, vd(cyc))
+        else:
+            op("V", lambda: V.tensor_scalar(out, in0, s1, s2, op0, op1), reads, writes, bank, vd(cyc))
+
+    def vtt(out, in0, in1, o, reads, writes, cyc=64, bank=None):
+        op("V", lambda: V.tensor_tensor(out, in0, in1, o), reads, writes, bank, vd(cyc))
+
+    def vcp(out, in_, reads, writes, cyc=64, bank=None):
+        op("V", lambda: V.tensor_copy(out, in_), reads, writes, bank, vd(cyc))
+
+    def vfill(ap, x, reads, writes, cyc=64):
+        op("V", lambda: V.memset(ap, x), reads, writes, None, vd(cyc))
+
+    def scan(out, d0, d1, o0, o1, reads, writes, cyc=64, bank=None):
+        op("V", lambda: V.tensor_tensor_scan(out, d0, d1, 0.0, o0, o1), reads, writes, bank, vd(cyc))
+
+    def sact(out, in_, f, reads, writes, bank=None, cyc=64, **kw):
+        op("S", lambda: S.activation(out, in_, f, **kw), reads, writes, bank, cyc * CY + 0.04)
+
+    def gc(fn, writes, reads=(), busy=0.45):
+        op("G", fn, reads, writes, None, busy)
+
+    def mms(lst, reads, bank):
+        def emit():
+            r = None
+            for (o, l, x, a, b) in lst:
+                r = PE.matmul(o, l, x, a, b)
+            return r
+        op("P", emit, reads, (), bank, len(lst) * 64 * P["pe"] + 0.05)
+
+    def load(q, out, in_, name, key, lat):
+        op(q, lambda: (Y if q == "Y" else S).dma_start(out, in_), (), (key,), None, 0.1, lat, "ld_" + name, 16)
+
+    load("Y", T.pl_s[:], T.pl[:], "pl", "pl_s", 2.0)
+    load("S", T.qin[:, 0:192], T.q[:], "q", "q0", 2.2)
+    load("Y", T.key_s[:], T.key[:], "key", "key", 5.0)
+    load("S", T.w_s[:], T.w[:], "w", "w", 2.5)
+    load("S", T.th_s[:], T.th[:], "th", "th", 2.5)
+    load("S", T.emb_s[:], T.emb[:], "emb", "emb", 2.5)
+    load("Y", T.cl_s[:], T.cl[:], "cl", "cl", 8.0)
+    load("Y", T.em_s[:], T.em[:], "em", "em", 10.5)
+
+    one64 = T.ones[:, 0:64]
+    vfill(T.ones[:], 1.0, (), ("ones",))
+    gc(lambda: g.iota(T.icol[:], [[0, 1]], 0, 1), ("icol",), (), 0.2)
+    gc(lambda: g.affine_select(T.bd[:], T.ones[:], [[-16, 8], [0, 16]], A.is_ge, 0.0, 0, 1), ("bd",), ("ones",))
+    gc(lambda: g.affine_select(T.bd[:], T.bd[:], [[16, 8], [0, 16]], A.is_ge, 0.0, 15, -1), ("bd",))
+    gc(lambda: g.iota(T.rowl[:], [[1, 64]], 0, 0), ("rowl",), (), 0.3)
+    gc(lambda: g.affine_select(T.idm[:], T.ones[:], [[-1, 128]], A.is_equal, 0.0, 0, 1), ("idm",), ("ones",))
+    gc(lambda: g.affine_select(T.ltm[:], T.bd[:], [[1, 128]], A.is_gt, 0.0, 0, -1), ("ltm",), ("bd",))
+    gc(lambda: g.iota(T.rowm[:], [[0, 4], [1, 16]], 0, 0, allow_small_or_imprecise_dtypes=True), ("rowm",), (), 0.3)
+    vfill(T.wk[:], 0.0, (), ("wk0",), 1024)
+    vfill(T.w2[:], 0.0, (), ("w20",), 1024)
+    for c in range(NC):
+        vcp(T.pin[:, 64 * c:64 * c + 64], T.pl_s[:, 64 * c:64 * c + 64], ("pl_s",), ("p%d_0" % c,))
+    vts(T.kint[:], T.icol[:], 15, None, A.bitwise_and, None, ("icol",), ("kint",))
+    vcp(T.kcol[:], T.kint[:], ("kint",), ("kcol",))
+    vcp(T.rep[:], T.rowl[:], ("rowl",), ("rep",))
+    r8 = range(8)
+    wkk, w2k, ebk = tuple("wk%d" % b for b in r8), tuple("w2_%d" % b for b in r8), tuple("eb%d" % b for b in r8)
+    for b in r8:
+        sl = slice(16 * b, 16 * b + 129 * 15 + 1, 129)
+        sact(T.wk[:, sl], T.bd[:, 16 * b:16 * b + 16], F.Copy, ("bd", "wk0"), (wkk[b],), scale=-1.0)
+        vts(T.w2[:, sl], T.bd[:, 16 * b:16 * b + 16], 2.0, None, A.mult, None, ("bd", "w20"), (w2k[b],))
+    sact(T.nbd[:], T.bd[:], F.Copy, ("bd",), ("nbd",), None, 128, scale=-1.0)
+    vts(T.bdw[:], T.bd[:], T.w_s[:, 0:1], None, A.mult, None, ("bd", "w"), ("bdw",))
+    vcp(T.idh[:], T.idm[:], ("idm",), ("idh",))
+    vts(T.c1023[:], one64, -1023.5, None, A.mult, None, ("ones",), ("c1023",))
+    vfill(T.cb[:], -524288.0, (), ("cb",))
+    sact(T.in2k[:], T.idm[:], F.Copy, ("idm",), ("in2k",), None, 128, scale=-2048.0)
+    sact(T.i8k[:], T.idm[:], F.Copy, ("idm",), ("i8k",), None, 128, scale=8192.0)
+    sact(T.bd4k[:], T.bd[:], F.Copy, ("bd",), ("bd4k",), None, 128, scale=4096.0)
+    vts(T.mb2[:], T.rowm[:], T.kcol[:, 0:1], -8192.0, A.is_equal, A.mult, ("rowm", "kcol"), ("mb2",))
+    vts(T.mb[:], T.mb2[:], 4096.0, None, A.add, None, ("mb2",), ("mb",))
+    vtt(T.gw0[:], T.idm[:], T.ltm[:], A.subtract, ("idm", "ltm"), ("gw0",), 256)
+    sact(T.gw[:], T.gw0[:], F.Copy, ("gw0",), ("gw",), None, 128, scale=4096.0)
+    vts(T.sgcol[:], T.kcol[:], -4096.0, 57344.0, A.mult, A.add, ("kcol",), ("sgcol",))
+    vts(T.sg[:], T.bd[:], T.sgcol[:, 0:1], None, A.mult, None, ("bd", "sgcol"), ("sg",))
+    vcp(T.bdh[:], T.bd[:], ("bd",), ("bdh",))
+    vfill(T.rst32[:], 1.0, (), ("rst32",), 128)
+    vfill(T.rst32[:, 0:128:32], 0.0, (), ("rst32",))
+    sact(T.i16[:], T.idm[:], F.Copy, ("idm",), ("i16",), None, 128, scale=16.0)
+    vts(T.ck[:], one64, T.kcol[:, 0:1], -1.0, A.mult, A.mult, ("ones", "kcol"), ("ck",))
+    vts(T.gint[:], T.icol[:], 4, 1, A.logical_shift_right, A.bitwise_and, ("icol",), ("gint",))
+    vts(T.gcol[:], T.gint[:], 65536.0, None, A.mult, None, ("gint",), ("gcol",))
+    vfill(T.rowb[:, 0:32], 0.0, (), ("rowb0",))
+    vfill(T.rowb[:, 32:64], 131072.0, (), ("rowb1",))
+    vts(T.ckb[:], T.rowb[:], T.gcol[:, 0:1], None, A.add, None, ("rowb0", "rowb1", "gcol"), ("ckb",))
+    vfill(T.zero[:], 0.0, (), ("zero",))
+    vfill(T.big16[:], 0.0, (), ("big16",))
+    vfill(T.big16[:, 0:64:16], 8388608.0, (), ("big16",))
+    for c in range(NC):
+        vfill(T["vs%d" % c][:, 64:80], 4194304.0, (), ("vsp%d" % c,))
+    sact(T.ihf[:], T.idm[:], F.Copy, ("idm",), ("ihf",), None, 128, scale=0.5)
+    vfill(T.cq[:], -0.25, (), ("cq",))
+    vcp(T.bdc[:], T.bd[:, 0:128:16], ("bd",), ("bdc",))
+    vts(T.tw[:], T.bdc[:], T.kcol[:, 0:1], None, A.mult, None, ("bdc", "kcol"), ("tw",))
+    for b in r8:
+        vts(T.eb[:, 16 * b:16 * b + 16], T.emb_s[:], T.bdc[:, b:b + 1], 0.5, A.mult, A.mult, ("emb", "bdc"), (ebk[b],))
+
+    def gather(e, out, win, off, reads, writes, count):
+        fn = (lambda: S.activation(out, win.indirect(off), F.Copy)) if e == "S" else (lambda: V.tensor_copy(out, win.indirect(off)))
+        op(e, fn, reads, writes, None, 0.07 + count * P["gather"] * CY)
+
+    sends = [0]
+
+    def send(dst, out, in_, sem, key, akey):
+        eng = topo.engines(core, dst)[:8]
+        rid, pid, _ = topo.addr(dst)
+        m = sum(1 << x for x in eng)
+        sends[0] += len(eng)
+        i = op("G", lambda: g.remote_dma(out, in_, T.sem[sem], T.sem.lsem, pid, rid, m), (key,), (), None, 0.15)
+        ops[i]["remote"] = True
+        j = op("NET", None, (), (akey,), None, 0.0, P["net"], sem, len(eng))
+        ops[j]["deps"].add(i)
+
+    def step(t, c):
+        cur[0] = c
+        B = lambda n: T["%s%d" % (n, c)]
+        k = lambda n: "%s%d" % (n, c)
+        o0 = t * 192 + NL * c
+        o1 = o0 + 192
+        pin, qin = T.pin[:, o0:o0 + NL], T.qin[:, o0:o0 + NL]
+        pkey = "p%d_%d" % (c, t)
+        qkey = "q%d_%d" % (c, t) if t else "q0"
+        psd, psx = B("psd"), B("psx")
+        bd, bx = "D%d" % c, "X%d" % c
+        kg, mx, eg = B("kg"), B("mx"), B("eg")
+        D, U, AR = psd[:, 0:64], psd[:, 64:128], psd[:, 128:192]
+        CH, C0, C1 = psx[:, 0:128], psx[:, 0:128:2], psx[:, 1:128:2]
+        HA, VO, QO, TK, V2 = psx[:, 128:192], psx[:, 192:256], psx[:, 256:320], psx[0:8, 320:384], psx[:, 384:448]
+        kgk, a = [], 0
+        for e, w in P["K"]:
+            kgk.append("%s_%d" % (k("kg"), a))
+            gather(e, kg[:, 16 * a:16 * (a + w)], T.key_s[:], T.pin[:, o0 + a:o0 + a + w], ("key", pkey), (kgk[-1],), 16 * w)
+            a += w
+        kgk = tuple(kgk)
+        vts(B("pc")[:], pin, 0.5, -0.25, A.mult, A.add, (pkey,), (k("pc"),))
+        vts(B("ph")[:], pin, -2048.0, None, A.add, None, (pkey,), (k("ph"),))
+        mms([(D, T.wk[:, 128 * i:128 * i + 128], kg[:, i:1024:16], i == 0, False) for i in range(NS)], kgk + wkk, bd)
+        mms([(D, T.nbd[:], qin, False, False)], ("nbd", qkey), bd)
+        mxk, a = [], 0
+        for w in P["M"]:
+            mxk.append("%s_%d" % (k("mx"), a))
+            op("V", lambda s=slice(16 * a, 16 * (a + w)), a=a, w=w: V.tensor_tensor(mx[:, s], qin.indirect(T.rep[:, a:a + w]), kg[:, s], A.max),
+               ("rep", qkey) + kgk, (mxk[-1],), None, 0.06 + 16 * w * P["gather"] * CY)
+            a += w
+        mms([(HA, T.bdw[:], qin, True, False), (HA, T.idh[:], T.c1023[:], False, False), (HA, T.idm[:], T.cb[:], False, True)],
+            ("bdw", "idh", "c1023", "idm", "cb", qkey), bx)
+        sact(B("hy")[:], HA, F.Identity, (), (k("hy"),), bx, bias=BIG, scale=1.0 / 2048.0)
+        sact(B("hn")[:], B("hy")[:], F.Identity, (k("hy"),), (k("hn"),), bias=-BIG)
+        mms([(C1, T.bdw[:], qin, True, False), (C1, T.idm[:], T.mb2[:], False, False), (C1, T.idm[:], T.cb[:], False, False),
+             (C1, T.in2k[:], B("hn")[:], False, False)], ("in2k", "mb2", k("hn")), bx)
+        mms([(D, T.w2[:, 128 * i:128 * i + 128], mx[:, i:1024:16], False, i == NS - 1) for i in range(NS)], tuple(mxk) + w2k, bd)
+        vts(B("nr")[:], D, T.th_s[:, 0:1], None, A.is_lt, None, ("th",), (k("nr"),), 64, bd)
+        mms([(U, T.gw[:], B("nr")[:], True, True)], ("gw", k("nr")), bd)
+        mms([(C1, T.bd4k[:], B("nr")[:], False, True), (C0, T.idm[:], T.mb[:], True, False), (C0, T.sg[:], B("nr")[:], False, False)],
+            ("bd4k", "idm", "mb", "sg", k("nr")), bx)
+        mms([(AR, T.idh[:], B("ph")[:], True, False), (AR, T.i8k[:], B("nr")[:], False, True)], ("idh", "i8k", k("nr"), k("ph")), bd)
+        vtt(B("xx")[:], U, B("pc")[:], A.min, (k("pc"),), (k("xx"),), 64, bd)
+        sact(B("ar")[:], AR, F.Identity, (), (k("ar"),), bd, bias=-2048.0)
+        mms([(C0, T.bdh[:], B("xx")[:], False, True)], ("bdh", k("xx")), bx)
+        scan(B("sc")[:], T.rst32[:], CH, A.mult, A.min, ("rst32",), (k("sc"),), 128, bx)
+        vts(B("ci")[:], B("sc")[:, 31:128:32], 8192.0, None, A.add, None, (k("sc"),), (k("ci"),))
+        op("V", lambda: V.tensor_tensor(B("pf")[:], T.cl_s[:].indirect(B("ci")[:, 0:4]), B("ar")[:], A.max),
+           ("cl", k("ci"), k("ar")), (k("pf"),), None, 0.06 + 64 * P["gather"] * CY)
+        vts(B("s2")[:], B("pf")[:], PL - 1, None, A.bitwise_and, None, (k("pf"),), (k("s2"),))
+        pok = "po%d_%d" % (c, t)
+        vcp(T.pout[:, o0:o0 + NL], B("s2")[:], (k("s2"),), (pok,))
+        nxt = cores[(rank + 1) % N if c == 0 else (rank - 1) % N]
+        shift = 1 if (c == 0 and rank == N - 1) else (PL - 1 if (c and rank == 0) else 0)
+        src, sk = T.pout[:, o0:o0 + NL], pok
+        if shift:
+            src, sk = T.pw[:, o0:o0 + NL], "pw%d_%d" % (c, t)
+            vts(B("s1")[:], B("pf")[:], float(shift), None, A.add, None, (k("pf"),), (k("s1"),))
+            vts(B("s3")[:], B("s1")[:], PL - 1, None, A.bitwise_and, None, (k("s1"),), (k("s3"),))
+            vcp(src, B("s3")[:], (k("s3"),), (sk,))
+        send(nxt, T.pin[:, o1:o1 + NL], src, "ap%d_%d" % (c, t + 1), sk, "p%d_%d" % (c, t + 1))
+        egk, a = [], 0
+        for e, w in P["E"]:
+            egk.append("%s_%d" % (k("eg"), a))
+            gather(e, eg[:, 16 * a:16 * (a + w)], T.em_s[:], T.pout[:, o0 + a:o0 + a + w], ("em", pok), (egk[-1],), 16 * w)
+            a += w
+        mms([(VO, T.idm[:], T.ck[:], True, False), (VO, T.idm[:], T.ckb[:], False, False)], ("idm", "ck", "ckb"), bx)
+        mms([(VO, T.i16[:], eg[:, i:1024:16], False, i == NS - 1) for i in range(NS)], tuple(egk) + ("i16",), bx)
+        op("V", lambda: V.transpose(B("vt")[:], VO), (), (k("vt"),), bx, vd(64))
+        mms([(QO, T.idm[:], T.cq[:], True, False), (QO, T.ihf[:], qin, False, False)], ("idm", "cq", "ihf", qkey), bx)
+        scan(B("vs")[:, 0:64], T.zero[:], B("vt")[:], A.max, A.max, ("zero", k("vt")), (k("vs"),))
+        scan(V2, T.big16[:], B("vs")[:, 15:79], A.max, A.min, ("big16", k("vs"), k("vsp")), (k("v2"),), 64, bx)
+        vtt(B("oh")[:], B("vt")[:], V2, A.is_equal, (k("vt"), k("v2")), (k("oh"),), 64, bx)
+        op("V", lambda: V.transpose(B("ot")[:], B("oh")[:]), (k("oh"),), (k("ot"),), None, vd(64))
+        mms([(QO, T.eb[:], B("ot")[:], False, True)], ebk + (k("ot"),), bx)
+        mms([(TK, T.tw[:], B("ot")[:], True, True)], ("tw", k("ot")), bx)
+        qok = "qo%d_%d" % (c, t)
+        vts(T.qout[:, o0:o0 + NL], QO, BIG, BIG, A.add, A.subtract, (), (qok,), 64, bx)
+        sact(T.yt_s[0:8, o0:o0 + NL], TK, F.Copy, (), ("yt%d_%d" % (c, t),), bx)
+        send(nxt, T.qin[:, o1:o1 + NL], T.qout[:, o0:o0 + NL], "aq%d_%d" % (c, t + 1), qok, "q%d_%d" % (c, t + 1))
+
+    for t in range(STEPS):
+        for c in range(NC):
+            step(t, c)
+    nout = [0]
+
+    def store(out, in_, reads):
+        nout[0] += 16
+        op("Y", lambda: Y.dma_start(out, in_), reads, (), None, 0.1, 2.0, "outs", None)
+
+    o6 = STEPS * 192
+    for c in range(NC):
+        a, b = NL * c, NL * c + NL
+        vcp(T.yp_s[:, a:b], T.pin[:, o6 + a:o6 + b], ("p%d_%d" % (c, STEPS),), ("yp%d" % c,))
+        store(T.yp[:, a:b], T.yp_s[:, a:b], ("yp%d" % c,))
+        store(T.yq[:, a:b], T.qin[:, o6 + a:o6 + b], ("q%d_%d" % (c, STEPS),))
+    store(T.yt[:], T.yt_s[0:8, :], tuple("yt%d_%d" % (c, t) for c in range(NC) for t in range(STEPS)))
+    return ops, sends[0], nout[0]
+
+
+def emit_all(g, T, ops, start, nsend, nout):
+    eng = {"V": g.vector, "S": g.scalar, "P": g.tensor, "G": g, "Y": g.sync}
+    esem = {"V": "sV", "S": "sS", "P": "sP", "G": "sG"}
+    count = {e: 0 for e in eng}
+    known = {e: {} for e in eng}
+    fin = {}
+    for i in sorted(range(len(ops)), key=lambda x: (start[x], x)):
+        o = ops[i]
+        e = o["eng"]
+        if e == "NET":
+            fin[i] = (o["sem"], o["val"], {o["sem"]: o["val"]})
+            continue
+        kn = known[e]
+        need = {}
+        for d in o["deps"]:
+            s, v, _ = fin[d]
+            if kn.get(s, 0) < v and need.get(s, (0, None))[0] < v:
+                need[s] = (v, d)
+        for s in list(need):
+            v = need[s][0]
+            if any(s2 != s and fin[need[s2][1]][2].get(s, 0) >= v for s2 in need):
+                del need[s]
+        for s in sorted(need):
+            v, d = need[s]
+            eng[e].wait_ge(T.sem[s], v)
+            for s2, v2 in fin[d][2].items():
+                if kn.get(s2, 0) < v2:
+                    kn[s2] = v2
+        ins = o["emit"]()
+        c = dict(kn)
+        if o["sem"] is not None:
+            ins.then_inc(T.sem[o["sem"]], 16)
+            if o["val"]:
+                c[o["sem"]] = o["val"]
+            fin[i] = (o["sem"], o["val"], c)
+        elif not o.get("remote"):
+            count[e] += 1
+            ins.then_inc(T.sem[esem[e]], 1)
+            c[esem[e]] = count[e]
+            fin[i] = (esem[e], count[e], c)
+    g.wait_ge(T.sem.lsem, nsend)
+    for e in ("V", "S", "P", "G"):
+        g.wait_ge(T.sem[esem[e]], count[e])
+    g.sync.wait_ge(T.sem.outs, nout)
+
+
+def rank_program(g, core, T, topo):
+    if T.rank_of(core) is None:
+        return
+    ops, nsend, nout = build(g, core, T, topo)
+    start, _ = plan(ops)
+    emit_all(g, T, ops, start, nsend, nout)

@@ -1,4 +1,5 @@
 import numpy as np
+from concourse.bass import DstId, RemoteDMATransfer
 from concourse.mybir import AluOpType, ActivationFunctionType
 
 A = AluOpType
@@ -7,47 +8,52 @@ NL = 64
 NS = 16
 NC = 3
 STEPS = 6
-PL = 4096
 BIG = 12582912.0
+MK = 16384.0
 P = {
-    "K": (("S", 64),),
-    "E": (("S", 48), ("V", 16)),
-    "M": (64,),
+    "K": (("S", 32), ("S", 32)),
+    "E": (("S", 40), ("V", 24)),
+    "M": 2,
+    "nr": "V", "z": "V", "ph": "send", "sf16": True, "qeng": 16, "peng": 8, "gate": True, "ka": 1536, "ca": 768,
     "look": 0.1, "seed": 0, "noise": 0.0, "stag": (0.0, 0.0, 0.0),
-    "cy": 0.83e-3 * 1.2, "gather": 1.5, "hop": 0.1, "net": 2.6, "pe": 0.55e-3, "fix": 0.02,
+    "cy": 0.83e-3 * 1.1, "gather": 1.4, "hop": 0.15, "net": 1.3, "row": 0.045, "pe": 0.5e-3, "fix": 0.01, "mb": 4.5,
 }
+P.update({'ph': 'V', 'stag': (0, 1, 2), 'look': 0.1, 'hop': 0.15, 'E': (('S', 40), ('V', 24)), 'K': (('S', 64),), 'M': 2, 'nr': 'S', 'z': 'V', 'gather': 1.5, 'noise': 0.1, 'seed': 16})
 
 BF, F3, I3, U1, H1 = "bfloat16", "float32", "int32", "uint16", "float16"
 SCRATCH = {
     "key_s": ("sbuf", [128, 4096], BF), "em_s": ("sbuf", [128, 4096], BF), "cl_s": ("sbuf", [128, 2048], I3),
     "pl_s": ("sbuf", [128, 192], I3), "emb_s": ("sbuf", [128, 16], BF), "w_s": ("sbuf", [128, 1], BF), "th_s": ("sbuf", [128, 1], F3),
-    "pin": ("sbuf", [128, 7 * 192], U1), "qin": ("sbuf", [128, 7 * 192], BF),
-    "pout": ("sbuf", [128, 6 * 192], U1), "pw": ("sbuf", [128, 6 * 192], U1), "qout": ("sbuf", [128, 6 * 192], BF),
-    "yp_s": ("sbuf", [128, 192], F3), "yt_s": ("sbuf", [128, 1152], F3),
-    "wk": ("sbuf", [128, 2048], BF), "w2": ("sbuf", [128, 2048], BF),
-    "tw": ("sbuf", [128, 8], BF), "bdc": ("sbuf", [128, 8], F3),
-    "bdh": ("sbuf", [128, 128], H1), "idh": ("sbuf", [128, 128], H1), "c1023": ("sbuf", [128, 64], H1),
-    "rep": ("sbuf", [128, 64], U1), "rst32": ("sbuf", [128, 128], F3),
+    "pin": ("sbuf", [128, 6 * 192], U1), "phin": ("sbuf", [128, 6 * 192], H1), "qin": ("sbuf", [128, 7 * 192], BF),
+    "pout": ("sbuf", [128, 6 * 192], U1), "pw": ("sbuf", [128, 6 * 192], U1), "pho": ("sbuf", [128, 6 * 192], H1),
+    "qout": ("sbuf", [128, 6 * 192], BF),
+    "yp_s": ("sbuf", [128, 192], F3), "ypo": ("sbuf", [128, 192], F3), "yt_s": ("sbuf", [128, 384], F3),
+    "wk": ("sbuf", [128, 144], BF), "w2": ("sbuf", [128, 144], BF),
+    "tw": ("sbuf", [128, 32], BF), "bdc": ("sbuf", [128, 8], F3), "id32": ("sbuf", [128, 128], F3),
+    "rep": ("sbuf", [128, 64], U1), "repi": ("sbuf", [128, 64], I3), "repj": ("sbuf", [128, 64], I3), "repk": ("sbuf", [128, 64], I3),
+    "rst": ("sbuf", [128, 128], F3), "seg": ("sbuf", [128, 64], F3), "rowm": ("sbuf", [128, 64], F3), "c1023": ("sbuf", [128, 64], H1),
+    "pst0": ("psum", [128, 512], F3), "pst1": ("psum", [128, 512], F3),
 }
-for _n in ("ones", "bd", "idm", "ltm", "gw0", "gw", "sg", "nbd", "bd4k", "i16", "i8k", "ihf", "in2k", "bdw", "eb"):
+for _n in ("ones", "bd", "idm", "ltm", "gw0", "gw", "sg", "nbd", "bd4k", "i8k", "in4k", "ihf", "bdw", "eb0", "eb", "chc", "shm", "dfm", "in2b"):
     SCRATCH[_n] = ("sbuf", [128, 128], BF)
-for _n in ("mb", "mb2", "cb", "ck", "ckb", "cq"):
+for _n in ("bdh", "idh", "in2k", "dm"):
+    SCRATCH[_n] = ("sbuf", [128, 128], H1)
+for _n in ("cu", "cq"):
     SCRATCH[_n] = ("sbuf", [128, 64], BF)
-for _n in ("icol", "kint", "gint"):
+for _n in ("icol", "kint"):
     SCRATCH[_n] = ("sbuf", [128, 1], I3)
-for _n in ("kcol", "gcol", "sgcol"):
+for _n in ("kcol", "sgcol", "thb", "k15"):
     SCRATCH[_n] = ("sbuf", [128, 1], F3)
-for _n, _d in (("rowm", F3), ("rowl", I3), ("rowb", F3), ("zero", F3), ("big16", F3)):
-    SCRATCH[_n] = ("sbuf", [128, 64], _d)
 for _c in range(NC):
-    for _n, _w, _d in (("kg", 1024, BF), ("mx", 1024, BF), ("eg", 1024, BF), ("ph", 64, H1), ("pc", 64, I3), ("nr", 64, BF), ("ar", 64, F3),
-                       ("xx", 64, H1), ("hy", 64, F3), ("hn", 64, BF), ("sc", 128, F3), ("ci", 4, U1), ("pf", 64, I3),
-                       ("s1", 64, I3), ("s2", 64, I3), ("s3", 64, I3), ("vt", 64, F3), ("vs", 80, F3), ("oh", 64, BF), ("ot", 64, BF)):
+    for _n, _w, _d in (("kg", 1024, BF), ("mx", 1024, BF), ("eg", 1024, BF), ("nr", 64, BF), ("ar", 64, F3),
+                       ("xx", 64, H1), ("hy", 64, F3), ("hn", 64, H1), ("sc", 128, F3), ("ci", 4, U1), ("pf", 64, F3), ("wr", 64, BF),
+                       ("vt", 64, F3), ("rs", 64, H1), ("rt", 64, H1), ("zz", 64, BF)):
         SCRATCH["%s%d" % (_n, _c)] = ("sbuf", [128, _w], _d)
     SCRATCH["psd%d" % _c] = ("psum", [128, 512], F3)
     SCRATCH["psx%d" % _c] = ("psum", [128, 512], F3)
 
-SEMAPHORES = (["sV", "sS", "sP", "sG", "lsem", "outs"] + ["ld_" + n for n in ("key", "em", "cl", "pl", "q", "emb", "w", "th")]
+SEMAPHORES = (["sV", "sS", "sP", "sG", "lsem", "outs"]
+              + ["ld_" + n for n in ("keya", "keyb", "em", "cla", "clb", "pl", "q", "emb", "w", "th")]
               + ["a%s%d_%d" % (k, c, t) for k in "pq" for c in range(NC) for t in range(1, STEPS + 1)])
 
 
@@ -59,7 +65,14 @@ def plan(ops):
         for d in o["deps"] | o["order"]:
             succ[d].append(o["n"])
     prio = [0.0] * n
-    for i in range(n - 1, -1, -1):
+    left = [len(o["deps"] | o["order"]) for o in ops]
+    topo_order = [i for i in range(n) if left[i] == 0]
+    for i in topo_order:
+        for j in succ[i]:
+            left[j] -= 1
+            if left[j] == 0:
+                topo_order.append(j)
+    for i in reversed(topo_order):
         o = ops[i]
         prio[i] = o["busy"] + o["lat"] + P["hop"] + max([prio[s] for s in succ[i]] + [0.0])
     prio = [p - P["stag"][o["c"]] for p, o in zip(prio, ops)]
@@ -91,7 +104,27 @@ def plan(ops):
             ready[j] = max(ready[j], fin + P["hop"] if i in ops[j]["deps"] else s)
             if missing[j] == 0:
                 cand.append(j)
-    return start, max(start[i] + ops[i]["busy"] + ops[i]["lat"] for i in range(n))
+    return start
+
+
+PLANS = {}
+
+
+def plan_all(lists):
+    base, ops, sent = [], [], {}
+    for r, l in enumerate(lists):
+        base.append(len(ops))
+        for o in l:
+            b = base[r]
+            ops.append(dict(o, n=o["n"] + b, deps={d + b for d in o["deps"]}, order={d + b for d in o["order"]},
+                            eng=o["eng"] if o["eng"] == "NET" else o["eng"] + str(r)))
+            if "sends" in o:
+                sent[r, o["sends"]] = o["n"] + b
+    for o in ops:
+        if "from" in o:
+            o["deps"].add(sent[o["from"], o["sem"]])
+    start = plan(ops)
+    return [start[base[r]:base[r] + len(l)] for r, l in enumerate(lists)]
 
 
 def build(g, core, T, topo):
@@ -103,6 +136,11 @@ def build(g, core, T, topo):
     ops = []
     lastw, readers, banks = {}, {}, {}
     cur = [0]
+    lastld = {}
+    na, nb = (1.0, 0.0) if P["nr"] == "V" else (0.5, 0.5)
+    za, zb = (1.0, 0.0) if P["z"] == "V" else (0.5, 0.5)
+    MP = P["M"]
+    MW = 1024 // MP
 
     def op(eng, emit, reads=(), writes=(), bank=None, busy=0.1, lat=0.0, sem=None, val=0):
         i = len(ops)
@@ -152,99 +190,133 @@ def build(g, core, T, topo):
     def gc(fn, writes, reads=(), busy=0.45):
         op("G", fn, reads, writes, None, busy)
 
-    def mms(lst, reads, bank):
+    def mms(lst, reads, bank, writes=(), units=None):
         def emit():
             r = None
             for (o, l, x, a, b) in lst:
                 r = PE.matmul(o, l, x, a, b)
             return r
-        op("P", emit, reads, (), bank, len(lst) * 64 * P["pe"] + 0.05)
+        op("P", emit, reads, writes, bank, (units or len(lst)) * 64 * P["pe"] + 0.02)
 
-    def load(q, out, in_, name, key, lat):
-        op(q, lambda: (Y if q == "Y" else S).dma_start(out, in_), (), (key,), None, 0.1, lat, "ld_" + name, 16)
+    def load(q, out, in_, name, key, lat, after=()):
+        i = op(q, lambda: (Y if q == "Y" else S).dma_start(out, in_), after, (key,), None, 0.1, lat, "ld_" + name, 16)
+        if q in lastld:
+            ops[i]["order"].add(lastld[q])
+        lastld[q] = i
 
-    load("Y", T.pl_s[:], T.pl[:], "pl", "pl_s", 2.0)
+    ka, ca, mb = P["ka"], P["ca"], P["mb"]
+    gate = P["gate"]
+    load("S", T.pl_s[:], T.pl[:], "pl", "pl_s", 2.0)
+    load("Y", T.key_s[:, 0:ka], T.key[:, 0:ka], "keya", "keya", 1.5 + 0.75 * mb)
+    load("Y", T.key_s[:, ka:], T.key[:, ka:], "keyb", "keyb", 1.5 + mb)
     load("S", T.qin[:, 0:192], T.q[:], "q", "q0", 2.2)
-    load("Y", T.key_s[:], T.key[:], "key", "key", 5.0)
     load("S", T.w_s[:], T.w[:], "w", "w", 2.5)
     load("S", T.th_s[:], T.th[:], "th", "th", 2.5)
     load("S", T.emb_s[:], T.emb[:], "emb", "emb", 2.5)
-    load("Y", T.cl_s[:], T.cl[:], "cl", "cl", 8.0)
-    load("Y", T.em_s[:], T.em[:], "em", "em", 10.5)
+    load("Y", T.cl_s[:, 0:ca], T.cl[:, 0:ca], "cla", "cla", 1.5 + 0.75 * mb + (0 if gate else mb), ("keya",) if gate else ())
+    load("Y", T.cl_s[:, ca:], T.cl[:, ca:], "clb", "clb", 1.5 + mb + (0 if gate else mb))
+    load("Y", T.em_s[:], T.em[:], "em", "em", 1.5 + mb + (0 if gate else 2 * mb), ("cla",) if gate else ())
 
     one64 = T.ones[:, 0:64]
     vfill(T.ones[:], 1.0, (), ("ones",))
     gc(lambda: g.iota(T.icol[:], [[0, 1]], 0, 1), ("icol",), (), 0.2)
     gc(lambda: g.affine_select(T.bd[:], T.ones[:], [[-16, 8], [0, 16]], A.is_ge, 0.0, 0, 1), ("bd",), ("ones",))
     gc(lambda: g.affine_select(T.bd[:], T.bd[:], [[16, 8], [0, 16]], A.is_ge, 0.0, 15, -1), ("bd",))
-    gc(lambda: g.iota(T.rowl[:], [[1, 64]], 0, 0), ("rowl",), (), 0.3)
+    gc(lambda: g.iota(T.repi[:], [[16, 64]], 0, 0), ("repi",), (), 0.3)
     gc(lambda: g.affine_select(T.idm[:], T.ones[:], [[-1, 128]], A.is_equal, 0.0, 0, 1), ("idm",), ("ones",))
     gc(lambda: g.affine_select(T.ltm[:], T.bd[:], [[1, 128]], A.is_gt, 0.0, 0, -1), ("ltm",), ("bd",))
     gc(lambda: g.iota(T.rowm[:], [[0, 4], [1, 16]], 0, 0, allow_small_or_imprecise_dtypes=True), ("rowm",), (), 0.3)
-    vfill(T.wk[:], 0.0, (), ("wk0",), 1024)
-    vfill(T.w2[:], 0.0, (), ("w20",), 1024)
+    gc(lambda: g.affine_select(T.shm[:], T.bd[:], [[-1, 128]], A.is_equal, 0.0, -1, 1), ("shm",), ("bd",))
     for c in range(NC):
         vcp(T.pin[:, 64 * c:64 * c + 64], T.pl_s[:, 64 * c:64 * c + 64], ("pl_s",), ("p%d_0" % c,))
+    vts(T.phin[:, 0:192], T.pl_s[:], -2048.0, None, A.add, None, ("pl_s",), ("ph0",), 192)
     vts(T.kint[:], T.icol[:], 15, None, A.bitwise_and, None, ("icol",), ("kint",))
     vcp(T.kcol[:], T.kint[:], ("kint",), ("kcol",))
-    vcp(T.rep[:], T.rowl[:], ("rowl",), ("rep",))
-    r8 = range(8)
-    wkk, w2k, ebk = tuple("wk%d" % b for b in r8), tuple("w2_%d" % b for b in r8), tuple("eb%d" % b for b in r8)
-    for b in r8:
-        sl = slice(16 * b, 16 * b + 129 * 15 + 1, 129)
-        sact(T.wk[:, sl], T.bd[:, 16 * b:16 * b + 16], F.Copy, ("bd", "wk0"), (wkk[b],), scale=-1.0)
-        vts(T.w2[:, sl], T.bd[:, 16 * b:16 * b + 16], 2.0, None, A.mult, None, ("bd", "w20"), (w2k[b],))
+    vts(T.repj[:], T.repi[:], T.kcol[:, 0:1], None, A.add, None, ("repi", "kcol"), ("repj",))
+    vts(T.repk[:], T.repj[:], {1: 4, 2: 3, 4: 2}[MP], None, A.logical_shift_right, None, ("repj",), ("repk",))
+    vcp(T.rep[:], T.repk[:], ("repk",), ("rep",))
+    vfill(T.wk[:], 0.0, (), ("wk",), 72)
+    vfill(T.w2[:], 0.0, (), ("w2",), 72)
+    vts(T.wk[:, 16:144:16], T.bd[:, 0:128:16], -1.0, None, A.mult, None, ("bd",), ("wk",))
+    vts(T.w2[:, 16:144:16], T.bd[:, 0:128:16], 2.0, None, A.mult, None, ("bd",), ("w2",))
     sact(T.nbd[:], T.bd[:], F.Copy, ("bd",), ("nbd",), None, 128, scale=-1.0)
     vts(T.bdw[:], T.bd[:], T.w_s[:, 0:1], None, A.mult, None, ("bd", "w"), ("bdw",))
     vcp(T.idh[:], T.idm[:], ("idm",), ("idh",))
-    vts(T.c1023[:], one64, -1023.5, None, A.mult, None, ("ones",), ("c1023",))
-    vfill(T.cb[:], -524288.0, (), ("cb",))
-    sact(T.in2k[:], T.idm[:], F.Copy, ("idm",), ("in2k",), None, 128, scale=-2048.0)
-    sact(T.i8k[:], T.idm[:], F.Copy, ("idm",), ("i8k",), None, 128, scale=8192.0)
-    sact(T.bd4k[:], T.bd[:], F.Copy, ("bd",), ("bd4k",), None, 128, scale=4096.0)
-    vts(T.mb2[:], T.rowm[:], T.kcol[:, 0:1], -8192.0, A.is_equal, A.mult, ("rowm", "kcol"), ("mb2",))
-    vts(T.mb[:], T.mb2[:], 4096.0, None, A.add, None, ("mb2",), ("mb",))
+    vts(T.in2k[:], T.idm[:], -2048.0, None, A.mult, None, ("idm",), ("in2k",))
+    sact(T.id32[:], T.idm[:], F.Copy, ("idm",), ("id32",), None, 128)
+    sact(T.i8k[:], T.idm[:], F.Copy, ("idm",), ("i8k",), None, 128, scale=8192.0 * na)
+    sact(T.in4k[:], T.idm[:], F.Copy, ("idm",), ("in4k",), None, 128, scale=-4096.0)
+    sact(T.bd4k[:], T.bd[:], F.Copy, ("bd",), ("bd4k",), None, 128, scale=4096.0 * na)
+    if na != 1.0:
+        vts(T.in2b[:], T.idm[:], -2048.0, None, A.mult, None, ("idm",), ("in2b",))
+        vts(T.thb[:], T.th_s[:], -0.5, None, A.add, None, ("th",), ("thb",))
     vtt(T.gw0[:], T.idm[:], T.ltm[:], A.subtract, ("idm", "ltm"), ("gw0",), 256)
-    sact(T.gw[:], T.gw0[:], F.Copy, ("gw0",), ("gw",), None, 128, scale=4096.0)
-    vts(T.sgcol[:], T.kcol[:], -4096.0, 57344.0, A.mult, A.add, ("kcol",), ("sgcol",))
+    sact(T.gw[:], T.gw0[:], F.Copy, ("gw0",), ("gw",), None, 128, scale=4096.0 * na)
+    vts(T.cu[:], one64, T.kcol[:, 0:1], None, A.mult, None, ("ones", "kcol"), ("cu",))
+    vts(T.cu[:], T.cu[:], -4096.0 * nb, 4096.0 * nb - 2048.0, A.mult, A.add, (), ("cu",))
+    vts(T.sgcol[:], T.kcol[:], -2048.0 * na, 28672.0 * na, A.mult, A.add, ("kcol",), ("sgcol",))
     vts(T.sg[:], T.bd[:], T.sgcol[:, 0:1], None, A.mult, None, ("bd", "sgcol"), ("sg",))
-    vcp(T.bdh[:], T.bd[:], ("bd",), ("bdh",))
-    vfill(T.rst32[:], 1.0, (), ("rst32",), 128)
-    vfill(T.rst32[:, 0:128:32], 0.0, (), ("rst32",))
-    sact(T.i16[:], T.idm[:], F.Copy, ("idm",), ("i16",), None, 128, scale=16.0)
-    vts(T.ck[:], one64, T.kcol[:, 0:1], -1.0, A.mult, A.mult, ("ones", "kcol"), ("ck",))
-    vts(T.gint[:], T.icol[:], 4, 1, A.logical_shift_right, A.bitwise_and, ("icol",), ("gint",))
-    vts(T.gcol[:], T.gint[:], 65536.0, None, A.mult, None, ("gint",), ("gcol",))
-    vfill(T.rowb[:, 0:32], 0.0, (), ("rowb0",))
-    vfill(T.rowb[:, 32:64], 131072.0, (), ("rowb1",))
-    vts(T.ckb[:], T.rowb[:], T.gcol[:, 0:1], None, A.add, None, ("rowb0", "rowb1", "gcol"), ("ckb",))
-    vfill(T.zero[:], 0.0, (), ("zero",))
-    vfill(T.big16[:], 0.0, (), ("big16",))
-    vfill(T.big16[:, 0:64:16], 8388608.0, (), ("big16",))
-    for c in range(NC):
-        vfill(T["vs%d" % c][:, 64:80], 4194304.0, (), ("vsp%d" % c,))
+    vts(T.bdh[:], T.bd[:], 0.5, None, A.mult, None, ("bd",), ("bdh",))
+    k0 = 18432.0 + 2048.0 * 104 * nb
+    k1 = (3145728.0 if P["sf16"] else 0.0) + 65536.0 * nb
+    vts(T.seg[:], T.rowm[:], T.kcol[:, 0:1], -MK, A.is_equal, A.mult, ("rowm", "kcol"), ("seg",))
+    vts(T.chc[:, 0:128:2], T.seg[:], k0, None, A.add, None, ("seg",), ("chc0",))
+    vts(T.chc[:, 1:128:2], T.seg[:], k1, None, A.add, None, ("seg",), ("chc1",))
+    vfill(T.rst[:], 0.0, (), ("rst",), 128)
+    vfill(T.rst[:, 0:128:32], 4194304.0, (), ("rst",))
+    vfill(T.rst[:, 31:128:32], -0.25, (), ("rst",))
+    if not P["sf16"]:
+        vts(T.c1023[:], one64, -1023.5, None, A.mult, None, ("ones",), ("c1023",))
+    vfill(T.seg[:], 4096.0, (), ("seg",))
+    vfill(T.seg[:, 0:64:16], -4096.0, (), ("seg",))
+    vts(T.k15[:], T.kcol[:], 15.0, None, A.is_equal, None, ("kcol",), ("k15",))
+    vts(T.dfm[:], T.bd[:], T.k15[:, 0:1], None, A.mult, None, ("bd", "k15"), ("dfm",))
+    vtt(T.dm[:], T.dfm[:], T.idm[:], A.subtract, ("dfm", "idm"), ("dm",), 256)
     sact(T.ihf[:], T.idm[:], F.Copy, ("idm",), ("ihf",), None, 128, scale=0.5)
-    vfill(T.cq[:], -0.25, (), ("cq",))
     vcp(T.bdc[:], T.bd[:, 0:128:16], ("bd",), ("bdc",))
-    vts(T.tw[:], T.bdc[:], T.kcol[:, 0:1], None, A.mult, None, ("bdc", "kcol"), ("tw",))
-    for b in r8:
-        vts(T.eb[:, 16 * b:16 * b + 16], T.emb_s[:], T.bdc[:, b:b + 1], 0.5, A.mult, A.mult, ("emb", "bdc"), (ebk[b],))
+    vfill(T.tw[:], 0.0, (), ("tw",))
+    vcp(T.tw[:, 0:8], T.bd[:, 0:128:16], ("bd",), ("tw",))
+    ebk = tuple("eb%d" % b for b in range(8))
+    for b in range(8):
+        vts(T.eb0[:, 16 * b:16 * b + 16], T.emb_s[:], T.bdc[:, b:b + 1], None, A.mult, None, ("emb", "bdc"), (ebk[b],))
+    vtt(T.dfm[:], T.idm[:], T.shm[:], A.subtract, ("idm", "shm"), ("dfm",), 256)
+    mms([(T.pst1[:, 0:128], T.dfm[:], T.eb0[:], True, True)], ebk + ("dfm",), "T1", (), 2)
+    sact(T.eb[:], T.pst1[:, 0:128], F.Copy, (), ("eb",), "T1", 128, scale=0.5 * za)
+    if zb:
+        mms([(T.pst1[:, 128:192], T.eb[:], one64, True, True)], ("eb", "ones"), "T1")
+        sact(T.cq[:], T.pst1[:, 128:192], F.Identity, (), ("cq",), "T1", bias=-0.25)
+    else:
+        vfill(T.cq[:], -0.25, (), ("cq",))
 
-    def gather(e, out, win, off, reads, writes, count):
-        fn = (lambda: S.activation(out, win.indirect(off), F.Copy)) if e == "S" else (lambda: V.tensor_copy(out, win.indirect(off)))
+    def gather(e, out, win, off, reads, writes, count, bias=None):
+        if e == "S":
+            fn = (lambda: S.activation(out, win.indirect(off), F.Copy)) if bias is None else (lambda: S.activation(out, win.indirect(off), F.Identity, bias=bias))
+        else:
+            fn = (lambda: V.tensor_copy(out, win.indirect(off))) if bias is None else (lambda: V.tensor_scalar(out, win.indirect(off), bias, None, A.add))
         op(e, fn, reads, writes, None, 0.07 + count * P["gather"] * CY)
 
     sends = [0]
 
-    def send(dst, out, in_, sem, key, akey):
-        eng = topo.engines(core, dst)[:8]
+    def send(dst, pairs, sem, keys, akeys, most, last):
+        eng = topo.engines(core, dst)
+        eng = eng[-most:] if last else eng[:most]
         rid, pid, _ = topo.addr(dst)
-        m = sum(1 << x for x in eng)
         sends[0] += len(eng)
-        i = op("G", lambda: g.remote_dma(out, in_, T.sem[sem], T.sem.lsem, pid, rid, m), (key,), (), None, 0.15)
+        if len(pairs) == 1:
+            m = sum(1 << x for x in eng)
+            fn = lambda: g.remote_dma(pairs[0][0], pairs[0][1], T.sem[sem], T.sem.lsem, pid, rid, m)
+        else:
+            h = len(eng) // len(pairs)
+            trs = [RemoteDMATransfer(dst_ids=[DstId(rid=rid, pnc=pid)], dma_engine_mask=sum(1 << x for x in eng[h * j:h * j + h]),
+                                     remote_sem=T.sem[sem], src=s, dst=d) for j, (d, s) in enumerate(pairs)]
+            fn = lambda: g.remote_dma_fused(trs, local_sem=T.sem.lsem)
+        i = op("G", fn, keys, (), None, 0.15)
         ops[i]["remote"] = True
-        j = op("NET", None, (), (akey,), None, 0.0, P["net"], sem, len(eng))
-        ops[j]["deps"].add(i)
+        ops[i]["sends"] = sem
+        frm = (2 * rank - cores.index(dst)) % N
+        ne = min(most, len(topo.engines(cores[frm], core)))
+        j = op("NET", None, (), akeys, None, 0.0, P["net"] + P["row"] * 128 * len(pairs) / ne, sem, ne)
+        ops[j]["from"] = frm
 
     def step(t, c):
         cur[0] = c
@@ -252,81 +324,110 @@ def build(g, core, T, topo):
         k = lambda n: "%s%d" % (n, c)
         o0 = t * 192 + NL * c
         o1 = o0 + 192
-        pin, qin = T.pin[:, o0:o0 + NL], T.qin[:, o0:o0 + NL]
+        ph, qin = T.phin[:, o0:o0 + NL], T.qin[:, o0:o0 + NL]
         pkey = "p%d_%d" % (c, t)
+        hkey = "ph%d_%d" % (c, t) if t else "ph0"
         qkey = "q%d_%d" % (c, t) if t else "q0"
         psd, psx = B("psd"), B("psx")
         bd, bx = "D%d" % c, "X%d" % c
-        kg, mx, eg = B("kg"), B("mx"), B("eg")
-        D, U, AR = psd[:, 0:64], psd[:, 64:128], psd[:, 128:192]
+        kg, mx, eg, nr = B("kg"), B("mx"), B("eg"), B("nr")[:]
+        D, U, AR, PP, P2 = (psd[:, 64 * j:64 * j + 64] for j in range(5))
         CH, C0, C1 = psx[:, 0:128], psx[:, 0:128:2], psx[:, 1:128:2]
-        HA, VO, QO, TK, V2 = psx[:, 128:192], psx[:, 192:256], psx[:, 256:320], psx[0:8, 320:384], psx[:, 384:448]
+        HA, VO, DL, QO = (psx[:, 128 + 64 * j:192 + 64 * j] for j in range(4))
         kgk, a = [], 0
         for e, w in P["K"]:
             kgk.append("%s_%d" % (k("kg"), a))
-            gather(e, kg[:, 16 * a:16 * (a + w)], T.key_s[:], T.pin[:, o0 + a:o0 + a + w], ("key", pkey), (kgk[-1],), 16 * w)
+            gather(e, kg[:, 16 * a:16 * (a + w)], T.key_s[:], T.pin[:, o0 + a:o0 + a + w], ("keya", "keyb", pkey), (kgk[-1],), 16 * w)
             a += w
         kgk = tuple(kgk)
-        vts(B("pc")[:], pin, 0.5, -0.25, A.mult, A.add, (pkey,), (k("pc"),))
-        vts(B("ph")[:], pin, -2048.0, None, A.add, None, (pkey,), (k("ph"),))
-        mms([(D, T.wk[:, 128 * i:128 * i + 128], kg[:, i:1024:16], i == 0, False) for i in range(NS)], kgk + wkk, bd)
+        if t and P["ph"] == "V":
+            vts(ph, T.pin[:, o0:o0 + NL], -2048.0, None, A.add, None, (pkey,), (hkey,))
+        mms([(D, T.wk[:, 16 - i:144 - i], kg[:, i:1024:16], i == 0, False) for i in range(NS)], kgk + ("wk",), bd)
         mms([(D, T.nbd[:], qin, False, False)], ("nbd", qkey), bd)
-        mxk, a = [], 0
-        for w in P["M"]:
-            mxk.append("%s_%d" % (k("mx"), a))
-            op("V", lambda s=slice(16 * a, 16 * (a + w)), a=a, w=w: V.tensor_tensor(mx[:, s], qin.indirect(T.rep[:, a:a + w]), kg[:, s], A.max),
-               ("rep", qkey) + kgk, (mxk[-1],), None, 0.06 + 16 * w * P["gather"] * CY)
-            a += w
-        mms([(HA, T.bdw[:], qin, True, False), (HA, T.idh[:], T.c1023[:], False, False), (HA, T.idm[:], T.cb[:], False, True)],
-            ("bdw", "idh", "c1023", "idm", "cb", qkey), bx)
-        sact(B("hy")[:], HA, F.Identity, (), (k("hy"),), bx, bias=BIG, scale=1.0 / 2048.0)
-        sact(B("hn")[:], B("hy")[:], F.Identity, (k("hy"),), (k("hn"),), bias=-BIG)
-        mms([(C1, T.bdw[:], qin, True, False), (C1, T.idm[:], T.mb2[:], False, False), (C1, T.idm[:], T.cb[:], False, False),
-             (C1, T.in2k[:], B("hn")[:], False, False)], ("in2k", "mb2", k("hn")), bx)
-        mms([(D, T.w2[:, 128 * i:128 * i + 128], mx[:, i:1024:16], False, i == NS - 1) for i in range(NS)], tuple(mxk) + w2k, bd)
-        vts(B("nr")[:], D, T.th_s[:, 0:1], None, A.is_lt, None, ("th",), (k("nr"),), 64, bd)
-        mms([(U, T.gw[:], B("nr")[:], True, True)], ("gw", k("nr")), bd)
-        mms([(C1, T.bd4k[:], B("nr")[:], False, True), (C0, T.idm[:], T.mb[:], True, False), (C0, T.sg[:], B("nr")[:], False, False)],
-            ("bd4k", "idm", "mb", "sg", k("nr")), bx)
-        mms([(AR, T.idh[:], B("ph")[:], True, False), (AR, T.i8k[:], B("nr")[:], False, True)], ("idh", "i8k", k("nr"), k("ph")), bd)
-        vtt(B("xx")[:], U, B("pc")[:], A.min, (k("pc"),), (k("xx"),), 64, bd)
-        sact(B("ar")[:], AR, F.Identity, (), (k("ar"),), bd, bias=-2048.0)
+        for s in range(MP):
+            op("V", lambda s=s: V.tensor_tensor(mx[:, MW * s:MW * s + MW], qin.indirect(T.rep[:, 0:64 // MP]), kg[:, s:1024:MP], A.max),
+               ("rep", qkey) + kgk, ("%s_%d" % (k("mx"), s),), None, 0.06 + MW * P["gather"] * CY)
+        if P["sf16"]:
+            mms([(HA, T.bdw[:], qin, True, True)], ("bdw", qkey), bx)
+            sact(B("hn")[:], HA, F.Identity, (), (k("hn"),), bx, bias=1536.0 - 1023.5 / 2048.0, scale=1.0 / 2048.0)
+        else:
+            mms([(HA, T.bdw[:], qin, True, False), (HA, T.idh[:], T.c1023[:], False, True)], ("bdw", "idh", "c1023", qkey), bx)
+            sact(B("hy")[:], HA, F.Identity, (), (k("hy"),), bx, bias=BIG, scale=1.0 / 2048.0)
+            vts(B("hn")[:], B("hy")[:], -BIG, None, A.add, None, (k("hy"),), (k("hn"),))
+        mms([(CH, T.idm[:], T.chc[:], True, False), (C1, T.bdw[:], qin, False, False), (C1, T.in2k[:], B("hn")[:], False, False)],
+            ("idm", "in2k", "chc0", "chc1", k("hn")), bx, (), 4)
+        for s in range(MP):
+            mms([(D, T.w2[:, 16 - s - MP * r:144 - s - MP * r], mx[:, MW * s + r:MW * s + MW:16 // MP], False, s == MP - 1 and r == 16 // MP - 1)
+                 for r in range(16 // MP)], ("%s_%d" % (k("mx"), s), "w2"), bd)
+        if na == 1.0:
+            vts(nr, D, T.th_s[:, 0:1], None, A.is_lt, None, ("th",), (k("nr"),), 64, bd)
+        else:
+            sact(nr, D, F.Sign, ("thb",), (k("nr"),), bd, bias=T.thb[:, 0:1], scale=-1.0)
+        mms([(U, T.idm[:], T.cu[:], True, False), (U, T.gw[:], nr, False, True)], ("idm", "cu", "gw", k("nr")), bd)
+        mms([(C1, T.bd4k[:], nr, False, False), (C0, T.sg[:], nr, False, False)], ("bd4k", "sg", k("nr")), bx)
+        mms([(AR, T.idh[:], ph, True, False), (AR, T.i8k[:], nr, False, True)], ("idh", "i8k", k("nr"), hkey), bd)
+        vtt(B("xx")[:], U, ph, A.min, (hkey,), (k("xx"),), 64, bd)
+        sact(B("ar")[:], AR, F.Identity, (), (k("ar"),), bd, bias=8192.0 * nb - 2048.0)
         mms([(C0, T.bdh[:], B("xx")[:], False, True)], ("bdh", k("xx")), bx)
-        scan(B("sc")[:], T.rst32[:], CH, A.mult, A.min, ("rst32",), (k("sc"),), 128, bx)
-        vts(B("ci")[:], B("sc")[:, 31:128:32], 8192.0, None, A.add, None, (k("sc"),), (k("ci"),))
+        scan(B("sc")[:], T.rst[:], CH, A.add, A.min, ("rst",), (k("sc"),), 128, bx)
+        vts(B("ci")[:], B("sc")[:, 31:128:32], BIG + MK, BIG, A.add, A.subtract, (k("sc"),), (k("ci"),))
+        i4 = T.in4k[:] if na == 1.0 else T.in2b[:]
+        mms([(PP, i4, nr, True, False)], ("in4k", "in2b", k("nr")), bd)
         op("V", lambda: V.tensor_tensor(B("pf")[:], T.cl_s[:].indirect(B("ci")[:, 0:4]), B("ar")[:], A.max),
-           ("cl", k("ci"), k("ar")), (k("pf"),), None, 0.06 + 64 * P["gather"] * CY)
-        vts(B("s2")[:], B("pf")[:], PL - 1, None, A.bitwise_and, None, (k("pf"),), (k("s2"),))
+           ("cla", "clb", k("ci"), k("ar")), (k("pf"),), None, 0.06 + 64 * P["gather"] * CY)
+        mms([(PP, T.id32[:], B("pf")[:], False, True)], ("id32", k("pf")), bd, (), 4)
+        pb = -4096.0 * nb
         pok = "po%d_%d" % (c, t)
-        vcp(T.pout[:, o0:o0 + NL], B("s2")[:], (k("s2"),), (pok,))
+        vts(T.pout[:, o0:o0 + NL], PP, pb, None, A.add, None, (), (pok,), 64, bd)
         nxt = cores[(rank + 1) % N if c == 0 else (rank - 1) % N]
-        shift = 1 if (c == 0 and rank == N - 1) else (PL - 1 if (c and rank == 0) else 0)
-        src, sk = T.pout[:, o0:o0 + NL], pok
+        shift = 1.0 if (c == 0 and rank == N - 1) else (-1.0 if (c and rank == 0) else 0.0)
+        src, sk, PS = T.pout[:, o0:o0 + NL], pok, PP
         if shift:
-            src, sk = T.pw[:, o0:o0 + NL], "pw%d_%d" % (c, t)
-            vts(B("s1")[:], B("pf")[:], float(shift), None, A.add, None, (k("pf"),), (k("s1"),))
-            vts(B("s3")[:], B("s1")[:], PL - 1, None, A.bitwise_and, None, (k("s1"),), (k("s3"),))
-            vcp(src, B("s3")[:], (k("s3"),), (sk,))
-        send(nxt, T.pin[:, o1:o1 + NL], src, "ap%d_%d" % (c, t + 1), sk, "p%d_%d" % (c, t + 1))
+            if shift > 0:
+                sact(B("wr")[:], PP, F.Relu, (), (k("wr"),), bd, bias=pb - 4094.0)
+            else:
+                sact(B("wr")[:], PP, F.Relu, (), (k("wr"),), bd, bias=1.0 - pb, scale=-1.0)
+            mms([(P2, i4, nr, True, False), (P2, T.id32[:], B("pf")[:], False, False),
+                 (P2, T.in4k[:], B("wr")[:], False, shift > 0)] + ([(P2, T.i8k[:], B("wr")[:], False, na == 1.0)] if shift < 0 else [])
+                + ([(P2, T.i8k[:], B("wr")[:], False, True)] if shift < 0 and na != 1.0 else []), (k("wr"), k("pf"), k("nr")), bd, (), 7)
+            src, sk, PS = T.pw[:, o0:o0 + NL], "pw%d_%d" % (c, t), P2
+            if t < STEPS - 1:
+                vts(src, P2, pb + shift, None, A.add, None, (), (sk,), 64, bd)
+        a1 = "ap%d_%d" % (c, t + 1)
+        if t == STEPS - 1:
+            a, b = NL * c, NL * c + NL
+            sact(T.ypo[:, a:b], PS, F.Identity, (), ("ypo%d" % c,), bd, bias=pb + shift)
+            send(nxt, [(T.yp_s[:, a:b], T.ypo[:, a:b])], a1, ("ypo%d" % c,), ("yp%d" % c,), P["peng"], True)
+        elif P["ph"] == "V":
+            send(nxt, [(T.pin[:, o1:o1 + NL], src)], a1, (sk,), ("p%d_%d" % (c, t + 1),), P["peng"], True)
+        else:
+            hok = "ho%d_%d" % (c, t)
+            sact(T.pho[:, o0:o0 + NL], PS, F.Identity, (), (hok,), bd, bias=pb + shift - 2048.0)
+            send(nxt, [(T.pin[:, o1:o1 + NL], src), (T.phin[:, o1:o1 + NL], T.pho[:, o0:o0 + NL])], a1, (sk, hok),
+                 ("p%d_%d" % (c, t + 1), "ph%d_%d" % (c, t + 1)), P["peng"], True)
         egk, a = [], 0
         for e, w in P["E"]:
             egk.append("%s_%d" % (k("eg"), a))
-            gather(e, eg[:, 16 * a:16 * (a + w)], T.em_s[:], T.pout[:, o0 + a:o0 + a + w], ("em", pok), (egk[-1],), 16 * w)
+            gather(e, eg[:, 16 * a:16 * (a + w)], T.em_s[:], T.pout[:, o0 + a:o0 + a + w], ("em", pok), (egk[-1],), 16 * w, -128.0)
             a += w
-        mms([(VO, T.idm[:], T.ck[:], True, False), (VO, T.idm[:], T.ckb[:], False, False)], ("idm", "ck", "ckb"), bx)
-        mms([(VO, T.i16[:], eg[:, i:1024:16], False, i == NS - 1) for i in range(NS)], tuple(egk) + ("i16",), bx)
+        mms([(VO, T.idm[:], eg[:, i:1024:16], i == 0, i == NS - 1) for i in range(NS)], tuple(egk) + ("idm",), bx)
         op("V", lambda: V.transpose(B("vt")[:], VO), (), (k("vt"),), bx, vd(64))
-        mms([(QO, T.idm[:], T.cq[:], True, False), (QO, T.ihf[:], qin, False, False)], ("idm", "cq", "ihf", qkey), bx)
-        scan(B("vs")[:, 0:64], T.zero[:], B("vt")[:], A.max, A.max, ("zero", k("vt")), (k("vs"),))
-        scan(V2, T.big16[:], B("vs")[:, 15:79], A.max, A.min, ("big16", k("vs"), k("vsp")), (k("v2"),), 64, bx)
-        vtt(B("oh")[:], B("vt")[:], V2, A.is_equal, (k("vt"), k("v2")), (k("oh"),), 64, bx)
-        op("V", lambda: V.transpose(B("ot")[:], B("oh")[:]), (k("oh"),), (k("ot"),), None, vd(64))
-        mms([(QO, T.eb[:], B("ot")[:], False, True)], ebk + (k("ot"),), bx)
-        mms([(TK, T.tw[:], B("ot")[:], True, True)], ("tw", k("ot")), bx)
+        scan(B("rs")[:], T.seg[:], B("vt")[:], A.min, A.max, ("seg", k("vt")), (k("rs"),))
+        op("V", lambda: V.transpose(B("rt")[:], B("rs")[:]), (k("rs"),), (k("rt"),), None, vd(64))
+        mms([(DL, T.dm[:], B("rt")[:], True, True)], ("dm", k("rt")), bx)
+        if za == 1.0:
+            vts(B("zz")[:], DL, 0.5, None, A.is_lt, None, (), (k("zz"),), 64, bx)
+        else:
+            sact(B("zz")[:], DL, F.Sign, (), (k("zz"),), bx, bias=0.5, scale=-1.0)
+        mms([(QO, T.idm[:], T.cq[:], True, False), (QO, T.ihf[:], qin, False, False), (QO, T.eb[:], B("zz")[:], False, True)],
+            ("idm", "cq", "ihf", "eb", qkey, k("zz")), bx)
+        if t < STEPS - 1:
+            mms([(T.pst0[32 * c:32 * c + 32, 64 * t:64 * t + 64], T.tw[:], B("zz")[:], True, True)], ("tw", k("zz")), None, ("tk%d_%d" % (c, t),))
+        else:
+            mms([(T.pst1[32 * c:32 * c + 32, 0:64], T.tw[:], B("zz")[:], True, True)], ("tw", k("zz"), "cq", "eb"), None, ("tk%d_%d" % (c, t),))
         qok = "qo%d_%d" % (c, t)
         vts(T.qout[:, o0:o0 + NL], QO, BIG, BIG, A.add, A.subtract, (), (qok,), 64, bx)
-        sact(T.yt_s[0:8, o0:o0 + NL], TK, F.Copy, (), ("yt%d_%d" % (c, t),), bx)
-        send(nxt, T.qin[:, o1:o1 + NL], T.qout[:, o0:o0 + NL], "aq%d_%d" % (c, t + 1), qok, "q%d_%d" % (c, t + 1))
+        send(nxt, [(T.qin[:, o1:o1 + NL], T.qout[:, o0:o0 + NL])], "aq%d_%d" % (c, t + 1), (qok,), ("q%d_%d" % (c, t + 1),), P["qeng"], False)
 
     for t in range(STEPS):
         for c in range(NC):
@@ -337,13 +438,19 @@ def build(g, core, T, topo):
         nout[0] += 16
         op("Y", lambda: Y.dma_start(out, in_), reads, (), None, 0.1, 2.0, "outs", None)
 
+    last = STEPS - 1
+    sact(T.yt_s[0:96, 0:64 * last], T.pst0[0:96, 0:64 * last], F.Identity, tuple("tk%d_%d" % (c, t) for c in range(NC) for t in range(last)),
+         ("yta",), None, 64 * last, bias=16.0 * (1 - zb), scale=-za)
+    sact(T.yt_s[0:96, 64 * last:64 * STEPS], T.pst1[0:96, 0:64], F.Identity, tuple("tk%d_%d" % (c, last) for c in range(NC)),
+         ("ytb",), None, 64, bias=16.0 * (1 - zb), scale=-za)
     o6 = STEPS * 192
+    for t in range(STEPS):
+        for c in range(NC):
+            store(T.yt[:, 192 * t + 64 * c:192 * t + 64 * c + 64], T.yt_s[32 * c:32 * c + 8, 64 * t:64 * t + 64], ("yta" if t < last else "ytb",))
     for c in range(NC):
         a, b = NL * c, NL * c + NL
-        vcp(T.yp_s[:, a:b], T.pin[:, o6 + a:o6 + b], ("p%d_%d" % (c, STEPS),), ("yp%d" % c,))
         store(T.yp[:, a:b], T.yp_s[:, a:b], ("yp%d" % c,))
         store(T.yq[:, a:b], T.qin[:, o6 + a:o6 + b], ("q%d_%d" % (c, STEPS),))
-    store(T.yt[:], T.yt_s[0:8, :], tuple("yt%d_%d" % (c, t) for c in range(NC) for t in range(STEPS)))
     return ops, sends[0], nout[0]
 
 
@@ -397,5 +504,7 @@ def rank_program(g, core, T, topo):
     if T.rank_of(core) is None:
         return
     ops, nsend, nout = build(g, core, T, topo)
-    start, _ = plan(ops)
-    emit_all(g, T, ops, start, nsend, nout)
+    key = repr(sorted(P.items()))
+    if key not in PLANS:
+        PLANS[key] = plan_all([build(g, c, T, topo)[0] for c in T.cores])
+    emit_all(g, T, ops, PLANS[key][T.rank_of(core)], nsend, nout)

@@ -13,28 +13,30 @@ MK = 16384.0
 P = {
     "K": (("S", 32), ("S", 32)),
     "E": (("S", 40), ("V", 24)),
-    "M": 2,
+    "K0": ((("S", 32), ("V", 32)), (("S", 32), ("S", 32)), (("S", 32), ("S", 32))),
+    "MV": ((0, 2),), "AB": ((1, 2),), "AS": 1, "PO": None, "and": 2,
     "nr": "V", "z": "V", "ph": "send", "sf16": True, "qeng": 16, "peng": 8, "gate": True, "ka": 1536, "ca": 768,
     "look": 0.1, "seed": 0, "noise": 0.0, "stag": (0.0, 0.0, 0.0),
     "cy": 0.83e-3 * 1.1, "gather": 1.4, "hop": 0.15, "net": 1.3, "row": 0.045, "pe": 0.5e-3, "fix": 0.01, "mb": 4.5,
 }
-P.update({'ph': 'V', 'stag': (0, 1, 2), 'look': 0.1, 'hop': 0.15, 'E': (('S', 40), ('V', 24)), 'K': (('S', 64),), 'M': 2, 'nr': 'S', 'z': 'V', 'gather': 1.5, 'noise': 0.1, 'seed': 16})
+P.update({"mb": 1.8, "MV": ((0, 4), (1, 4), (2, 4)), "AB": ((3, 4),), "K": (("S", 64),),
+          "K0": ((("S", 32), ("V", 32)), (("S", 64),), (("S", 64),)), "nr": "V", "E": (("S", 42), ("V", 22))})
 
 BF, F3, I3, U1, H1 = "bfloat16", "float32", "int32", "uint16", "float16"
 SCRATCH = {
-    "key_s": ("sbuf", [128, 4096], BF), "em_s": ("sbuf", [128, 4096], BF), "cl_s": ("sbuf", [128, 2048], I3),
+    "key_s": ("sbuf", [128, 4128], BF), "em_s": ("sbuf", [128, 4096], BF), "cl_s": ("sbuf", [128, 2064], I3),
     "pl_s": ("sbuf", [128, 192], I3), "emb_s": ("sbuf", [128, 16], BF), "w_s": ("sbuf", [128, 1], BF), "th_s": ("sbuf", [128, 1], F3),
     "pin": ("sbuf", [128, 6 * 192], U1), "phin": ("sbuf", [128, 6 * 192], H1), "qin": ("sbuf", [128, 7 * 192], BF),
-    "pout": ("sbuf", [128, 6 * 192], U1), "pw": ("sbuf", [128, 6 * 192], U1), "pho": ("sbuf", [128, 6 * 192], H1),
+    "pout": ("sbuf", [128, 6 * 192], U1), "pw": ("sbuf", [128, 6 * 192], U1),
     "qout": ("sbuf", [128, 6 * 192], BF),
     "yp_s": ("sbuf", [128, 192], F3), "ypo": ("sbuf", [128, 192], F3), "yt_s": ("sbuf", [128, 384], F3),
     "wk": ("sbuf", [128, 144], BF), "w2": ("sbuf", [128, 144], BF),
-    "tw": ("sbuf", [128, 32], BF), "bdc": ("sbuf", [128, 8], F3), "id32": ("sbuf", [128, 128], F3),
-    "rep": ("sbuf", [128, 64], U1), "repi": ("sbuf", [128, 64], I3), "repj": ("sbuf", [128, 64], I3), "repk": ("sbuf", [128, 64], I3),
-    "rst": ("sbuf", [128, 128], F3), "seg": ("sbuf", [128, 64], F3), "rowm": ("sbuf", [128, 64], F3), "c1023": ("sbuf", [128, 64], H1),
+    "tw": ("sbuf", [128, 32], BF), "bdc": ("sbuf", [128, 8], F3),
+    "rep": ("sbuf", [128, 112], U1), "repi": ("sbuf", [128, 64], I3), "repj": ("sbuf", [128, 64], I3), "repk": ("sbuf", [128, 112], I3),
+    "rst": ("sbuf", [128, 128], F3), "seg": ("sbuf", [128, 64], F3), "rowm": ("sbuf", [128, 64], F3), "r2": ("sbuf", [128, 128], F3),
     "pst0": ("psum", [128, 512], F3), "pst1": ("psum", [128, 512], F3),
 }
-for _n in ("ones", "bd", "idm", "ltm", "gw0", "gw", "sg", "nbd", "bd4k", "i8k", "in4k", "ihf", "bdw", "eb0", "eb", "chc", "shm", "dfm", "in2b"):
+for _n in ("ones", "bd", "idm", "ltm", "gw0", "gw", "sg", "nbd", "bd4k", "i8k", "ihf", "bdw", "eb0", "eb", "chc", "shm", "dfm", "nid", "offd"):
     SCRATCH[_n] = ("sbuf", [128, 128], BF)
 for _n in ("bdh", "idh", "in2k", "dm"):
     SCRATCH[_n] = ("sbuf", [128, 128], H1)
@@ -42,18 +44,18 @@ for _n in ("cu", "cq"):
     SCRATCH[_n] = ("sbuf", [128, 64], BF)
 for _n in ("icol", "kint"):
     SCRATCH[_n] = ("sbuf", [128, 1], I3)
-for _n in ("kcol", "sgcol", "thb", "k15"):
+for _n in ("kcol", "sgcol", "thb", "k15", "k16"):
     SCRATCH[_n] = ("sbuf", [128, 1], F3)
 for _c in range(NC):
     for _n, _w, _d in (("kg", 1024, BF), ("mx", 1024, BF), ("eg", 1024, BF), ("nr", 64, BF), ("ar", 64, F3),
-                       ("xx", 64, H1), ("hy", 64, F3), ("hn", 64, H1), ("sc", 128, F3), ("ci", 4, U1), ("pf", 64, F3), ("wr", 64, BF),
+                       ("xx", 64, H1), ("hn", 64, H1), ("sc", 128, F3), ("ci", 4, U1), ("pi", 64, I3), ("s1", 64, I3), ("s2", 64, I3), ("s3", 64, I3),
                        ("vt", 64, F3), ("rs", 64, H1), ("rt", 64, H1), ("zz", 64, BF)):
         SCRATCH["%s%d" % (_n, _c)] = ("sbuf", [128, _w], _d)
     SCRATCH["psd%d" % _c] = ("psum", [128, 512], F3)
     SCRATCH["psx%d" % _c] = ("psum", [128, 512], F3)
 
 SEMAPHORES = (["sV", "sS", "sP", "sG", "lsem", "outs"]
-              + ["ld_" + n for n in ("keya", "keyb", "em", "cla", "clb", "pl", "q", "emb", "w", "th")]
+              + ["ld_" + n for n in ("keya", "keyb", "em", "cla", "clb", "pl", "q", "emb", "w", "th", "kp", "cp")]
               + ["a%s%d_%d" % (k, c, t) for k in "pq" for c in range(NC) for t in range(1, STEPS + 1)])
 
 
@@ -108,9 +110,10 @@ def plan(ops):
 
 
 PLANS = {}
+ORDER = ["020304051a1d1f1h1i2d2f2h0100070e0b0j100v0p1317191q08090m0t1m0l0d140o0s150q1v180x1j1g161b0i0n0h0y0z1e1k1l060a0c2s2v0f0k0r0u1c0g24232k2e2a28292b20120w112w341o1n1r1w1s1t1x1u1y212o2u361z222c2i2l2y3d2z31333g3j3q3t40434749484c4l4n4q4t515355586f5a5b1p262p252g2m2j2n2r35373n2q2t38393c3l3s3m3p3r3u3w41454e4g4s4w4y4j4k4p5254575c5e5h5k6l5p5q27303f2x323e3a3b3i3x3z463h3k3o3v3y424b444a4h4d4f4i4m4o4r4u4z504v4x595d5f5j5m5o5s5u7n5z6056645n5v5r5x625i5t6a6m6o6w5y696b6g6i6s6z6t6u6y74777b7h7m7t7v7w7x81888e8i8l8o8p8q8u938y8z5g63616j67666d65686e707a7g6n6p6r6v727c7k7d7f7j7l7q7u7z84878d8g8h8a8b8k8r8t8x9295989bak9c9d5w5l6c716k6q6x6h73767r7s7y7578797e7i7o827p80868385898c8f8j8w90918m8n8v94979a9e9g9i9ka29p9q8s9h9f9s9m9r9u999ja19la5aa9t9ya0acaeaiasajamawavb0b4b6b9bebibkbjbtbxc4c8cbcfciclcpcudscrcs969x9n9w9za3a69va7abatazbbadahalaqaub1bdb2b7babgbmbpbrbvbyc3c6c7c0c1cacjcmcnctcwczd2dwdzd5d69oa8a4axa9aganafaoaparbfbnayb3b5b8bcbhboblbqbubsbwbzc2c5c9cecgchcccdcocvcyd1d3d7d9dce8eidfdgckcqd4didddhdkd0dadoe2e5eadjdldrdudye3ele4ebecenerevf4f9fefifjfkflfvg2g4g7gbgfgigkgqgngocxd8dedtdqdne0dmdpdvefetf3e6e9egehekeyf7f0f2f6f8fcfhfpfrfufwg0g1fyfzg6geghgjgpgsgvgyhhgzh0dbemdxeoe1e7edeeejepfdfgfmeqeseuf1f5fafnfbfffsfofqftfxg3g5gagcgdg8g9glgrgugxh1h3h5h7iwh8h9gggmgwhihahdhgh2h6hchkhxi8hjhmhnhphsi2idi3i5iaieihilioixj1j6j8j7jcjjjrjvjyk1k5k7k8ljllkbkcgth4hbhqhlhohthfhrhvhzi7iuhuhwibicifiniyiqiritizj4jbjfjijljqjtjujnjojxk6kakdkekkkokrlalxkukvhehyi4iii0i9i6i1igikj0j5jaijimipisivj2jdj3j9jhjejgjkjmjpjsk0k2k3jwjzk9kgkjklknkqktkxlclnl1l2k4khkil6l3kzl5kpkyl9lslzmcl7l8lblglmlymdm0m4m6memhmkmomun0njnmnnn4n5nentnwo0o8odogojooosopoqkfkml0lrlflelhl4lilom8mampltlwm1m7mbmjmsmlmnmrmtmyn3n8nandnsnvo1o4o5ngnlnrnzo3o6o7oboeohokowolomkwksldm9lplvm5lklqlumvmzn2mfmgmimmmqmwn6mxn1nbn7n9ncnfnhnkninpnunxnynonqo2o9oaocofoionorotouoxoyexezewm2m3p1ovp0ozp2"]
 
 
-def plan_all(lists):
+def join(lists):
     base, ops, sent = [], [], {}
     for r, l in enumerate(lists):
         base.append(len(ops))
@@ -123,8 +126,40 @@ def plan_all(lists):
     for o in ops:
         if "from" in o:
             o["deps"].add(sent[o["from"], o["sem"]])
-    start = plan(ops)
+    return base, ops
+
+
+def plan_all(lists):
+    base, ops = join(lists)
+    start = keyed(ops, order_of(ops), {o["name"]: float(int(ORDER[0][2 * j:2 * j + 2], 36)) for j, o in enumerate(lists[0])}) if ORDER[0] else plan(ops)
     return [start[base[r]:base[r] + len(l)] for r, l in enumerate(lists)]
+
+
+def order_of(ops):
+    succ = [[] for _ in ops]
+    for o in ops:
+        for d in o["deps"] | o["order"]:
+            succ[d].append(o["n"])
+    left = [len(o["deps"] | o["order"]) for o in ops]
+    out = [i for i in range(len(ops)) if left[i] == 0]
+    for i in out:
+        for j in succ[i]:
+            left[j] -= 1
+            if left[j] == 0:
+                out.append(j)
+    return out
+
+
+def keyed(ops, order, place):
+    key = [0.0] * len(ops)
+    for i in order:
+        o = ops[i]
+        k = place.get(o["name"], 0.0)
+        for d in o["deps"] | o["order"]:
+            if key[d] + 1e-4 > k:
+                k = key[d] + 1e-4
+        key[i] = k
+    return key
 
 
 def build(g, core, T, topo):
@@ -135,12 +170,14 @@ def build(g, core, T, topo):
     CY, FIX = P["cy"], P["fix"]
     ops = []
     lastw, readers, banks = {}, {}, {}
-    cur = [0]
+    cur = [0, -1]
+    seen = {}
     lastld = {}
     na, nb = (1.0, 0.0) if P["nr"] == "V" else (0.5, 0.5)
     za, zb = (1.0, 0.0) if P["z"] == "V" else (0.5, 0.5)
-    MP = P["M"]
-    MW = 1024 // MP
+    MV, AB = P["MV"], P["AB"]
+    vslots = sorted(i for s, n in MV for i in range(s, NS, n))
+    turn = [0]
 
     def op(eng, emit, reads=(), writes=(), bank=None, busy=0.1, lat=0.0, sem=None, val=0):
         i = len(ops)
@@ -160,7 +197,10 @@ def build(g, core, T, topo):
         for k in writes:
             lastw[k] = i
             readers[k] = set()
-        ops.append({"n": i, "eng": eng, "emit": emit, "deps": deps, "order": order - deps, "busy": busy, "lat": lat, "sem": sem, "val": val, "c": cur[0]})
+        tag = eng + (writes[0][:2] if writes else (bank[0] if bank else reads[0][0]))
+        seen[tag] = seen.get(tag, -1) + 1
+        ops.append({"n": i, "eng": eng, "emit": emit, "deps": deps, "order": order - deps, "busy": busy, "lat": lat, "sem": sem, "val": val,
+                    "c": cur[0], "t": cur[1], "tag": tag + str(seen[tag]), "name": "%s%d.%d%d" % (tag, seen[tag], cur[0], cur[1] + 1)})
         return i
 
     def vd(cyc):
@@ -207,15 +247,21 @@ def build(g, core, T, topo):
     ka, ca, mb = P["ka"], P["ca"], P["mb"]
     gate = P["gate"]
     load("S", T.pl_s[:], T.pl[:], "pl", "pl_s", 2.0)
-    load("Y", T.key_s[:, 0:ka], T.key[:, 0:ka], "keya", "keya", 1.5 + 0.75 * mb)
-    load("Y", T.key_s[:, ka:], T.key[:, ka:], "keyb", "keyb", 1.5 + mb)
+    load("Y", T.key_s[:, 16:16 + ka], T.key[:, 0:ka], "keya", "keya", 1.5 + 0.75 * mb)
+    load("Y", T.key_s[:, 16 + ka:4112], T.key[:, ka:], "keyb", "keyb", 1.5 + mb)
     load("S", T.qin[:, 0:192], T.q[:], "q", "q0", 2.2)
-    load("S", T.w_s[:], T.w[:], "w", "w", 2.5)
-    load("S", T.th_s[:], T.th[:], "th", "th", 2.5)
-    load("S", T.emb_s[:], T.emb[:], "emb", "emb", 2.5)
-    load("Y", T.cl_s[:, 0:ca], T.cl[:, 0:ca], "cla", "cla", 1.5 + 0.75 * mb + (0 if gate else mb), ("keya",) if gate else ())
-    load("Y", T.cl_s[:, ca:], T.cl[:, ca:], "clb", "clb", 1.5 + mb + (0 if gate else mb))
+    load("Y", T.w_s[:], T.w[:], "w", "w", 2.0, ("keya",))
+    load("Y", T.th_s[:], T.th[:], "th", "th", 2.0)
+    load("Y", T.cl_s[:, 8:8 + ca], T.cl[:, 0:ca], "cla", "cla", 1.5 + 0.75 * mb + (0 if gate else mb), ("keya",) if gate else ())
+    load("Y", T.cl_s[:, 8 + ca:2056], T.cl[:, ca:], "clb", "clb", 1.5 + mb + (0 if gate else mb))
+    load("Y", T.emb_s[:], T.emb[:], "emb", "emb", 2.0)
     load("Y", T.em_s[:], T.em[:], "em", "em", 1.5 + mb + (0 if gate else 2 * mb), ("cla",) if gate else ())
+    if rank == 0:
+        load("Y", T.key_s[:, 4112:4128], T.key[:, 0:16], "kp", "kp", 2.0)
+        load("Y", T.cl_s[:, 2056:2064], T.cl[:, 0:8], "cp", "cp", 2.0)
+    if rank == N - 1:
+        load("Y", T.key_s[:, 0:16], T.key[:, 4080:4096], "kp", "kp", 2.0)
+        load("Y", T.cl_s[:, 0:8], T.cl[:, 2040:2048], "cp", "cp", 2.0)
 
     one64 = T.ones[:, 0:64]
     vfill(T.ones[:], 1.0, (), ("ones",))
@@ -233,22 +279,25 @@ def build(g, core, T, topo):
     vts(T.kint[:], T.icol[:], 15, None, A.bitwise_and, None, ("icol",), ("kint",))
     vcp(T.kcol[:], T.kint[:], ("kint",), ("kcol",))
     vts(T.repj[:], T.repi[:], T.kcol[:, 0:1], None, A.add, None, ("repi", "kcol"), ("repj",))
-    vts(T.repk[:], T.repj[:], {1: 4, 2: 3, 4: 2}[MP], None, A.logical_shift_right, None, ("repj",), ("repk",))
-    vcp(T.rep[:], T.repk[:], ("repk",), ("rep",))
+    rep0 = {1: 0, 2: 64, 4: 96}
+    for n in sorted({n for s, n in MV}):
+        a, b = rep0[n], rep0[n] + 64 // n
+        vts(T.repk[:, a:b], T.repj[:, 0:64 // n], {1: 4, 2: 3, 4: 2}[n], None, A.logical_shift_right, None, ("repj",), ("repk%d" % n,))
+        vcp(T.rep[:, a:b], T.repk[:, a:b], ("repk%d" % n,), ("rep%d" % n,))
     vfill(T.wk[:], 0.0, (), ("wk",), 72)
     vfill(T.w2[:], 0.0, (), ("w2",), 72)
     vts(T.wk[:, 16:144:16], T.bd[:, 0:128:16], -1.0, None, A.mult, None, ("bd",), ("wk",))
     vts(T.w2[:, 16:144:16], T.bd[:, 0:128:16], 2.0, None, A.mult, None, ("bd",), ("w2",))
     sact(T.nbd[:], T.bd[:], F.Copy, ("bd",), ("nbd",), None, 128, scale=-1.0)
+    for s, n in AB:
+        vfill(T.nbd[:, s:128:n], 0.0, (), ("nbd",))
+    sact(T.nid[:], T.idm[:], F.Copy, ("idm",), ("nid",), None, 128, scale=-1.0)
     vts(T.bdw[:], T.bd[:], T.w_s[:, 0:1], None, A.mult, None, ("bd", "w"), ("bdw",))
     vcp(T.idh[:], T.idm[:], ("idm",), ("idh",))
     vts(T.in2k[:], T.idm[:], -2048.0, None, A.mult, None, ("idm",), ("in2k",))
-    sact(T.id32[:], T.idm[:], F.Copy, ("idm",), ("id32",), None, 128)
     sact(T.i8k[:], T.idm[:], F.Copy, ("idm",), ("i8k",), None, 128, scale=8192.0 * na)
-    sact(T.in4k[:], T.idm[:], F.Copy, ("idm",), ("in4k",), None, 128, scale=-4096.0)
     sact(T.bd4k[:], T.bd[:], F.Copy, ("bd",), ("bd4k",), None, 128, scale=4096.0 * na)
     if na != 1.0:
-        vts(T.in2b[:], T.idm[:], -2048.0, None, A.mult, None, ("idm",), ("in2b",))
         vts(T.thb[:], T.th_s[:], -0.5, None, A.add, None, ("th",), ("thb",))
     vtt(T.gw0[:], T.idm[:], T.ltm[:], A.subtract, ("idm", "ltm"), ("gw0",), 256)
     sact(T.gw[:], T.gw0[:], F.Copy, ("gw0",), ("gw",), None, 128, scale=4096.0 * na)
@@ -265,8 +314,9 @@ def build(g, core, T, topo):
     vfill(T.rst[:], 0.0, (), ("rst",), 128)
     vfill(T.rst[:, 0:128:32], 4194304.0, (), ("rst",))
     vfill(T.rst[:, 31:128:32], -0.25, (), ("rst",))
-    if not P["sf16"]:
-        vts(T.c1023[:], one64, -1023.5, None, A.mult, None, ("ones",), ("c1023",))
+    if rank == N - 1:
+        vts(T.r2[:], T.rst[:], 0.0, None, A.max, None, ("rst",), ("r2",), 128)
+        vfill(T.r2[:, 31:128:32], 0.25, (), ("r2",))
     vfill(T.seg[:], 4096.0, (), ("seg",))
     vfill(T.seg[:, 0:64:16], -4096.0, (), ("seg",))
     vts(T.k15[:], T.kcol[:], 15.0, None, A.is_equal, None, ("kcol",), ("k15",))
@@ -280,13 +330,17 @@ def build(g, core, T, topo):
     for b in range(8):
         vts(T.eb0[:, 16 * b:16 * b + 16], T.emb_s[:], T.bdc[:, b:b + 1], None, A.mult, None, ("emb", "bdc"), (ebk[b],))
     vtt(T.dfm[:], T.idm[:], T.shm[:], A.subtract, ("idm", "shm"), ("dfm",), 256)
-    mms([(T.pst1[:, 0:128], T.dfm[:], T.eb0[:], True, True)], ebk + ("dfm",), "T1", (), 2)
-    sact(T.eb[:], T.pst1[:, 0:128], F.Copy, (), ("eb",), "T1", 128, scale=0.5 * za)
     if zb:
-        mms([(T.pst1[:, 128:192], T.eb[:], one64, True, True)], ("eb", "ones"), "T1")
-        sact(T.cq[:], T.pst1[:, 128:192], F.Identity, (), ("cq",), "T1", bias=-0.25)
+        mms([(T.psx2[:, 0:128], T.dfm[:], T.eb0[:], True, True)], ebk + ("dfm",), "X2", (), 2)
     else:
-        vfill(T.cq[:], -0.25, (), ("cq",))
+        vts(T.k16[:], T.k15[:], 1.0 / 16, None, A.mult, None, ("k15",), ("k16",))
+        vts(T.offd[:], T.bd[:], -1.0, T.k16[:, 0:1], A.add, A.mult, ("bd", "k16"), ("offd",))
+        mms([(T.psx2[:, 0:128], T.idm[:], T.offd[:], True, False), (T.psx2[:, 0:128], T.dfm[:], T.eb0[:], False, True)],
+            ebk + ("dfm", "idm", "offd"), "X2", (), 4)
+    sact(T.eb[:], T.psx2[:, 0:128], F.Copy, (), ("eb",), "X2", 128, scale=0.5 * za)
+    if zb:
+        mms([(T.psx2[:, 128:192], T.eb[:], one64, True, True)], ("eb", "ones"), "X2")
+        sact(T.cq[:], T.psx2[:, 128:192], F.Identity, (), ("cq",), "X2", bias=-0.25)
 
     def gather(e, out, win, off, reads, writes, count, bias=None):
         if e == "S":
@@ -319,7 +373,8 @@ def build(g, core, T, topo):
         ops[j]["from"] = frm
 
     def step(t, c):
-        cur[0] = c
+        cur[0], cur[1] = c, t
+        seen.clear()
         B = lambda n: T["%s%d" % (n, c)]
         k = lambda n: "%s%d" % (n, c)
         o0 = t * 192 + NL * c
@@ -334,31 +389,47 @@ def build(g, core, T, topo):
         D, U, AR, PP, P2 = (psd[:, 64 * j:64 * j + 64] for j in range(5))
         CH, C0, C1 = psx[:, 0:128], psx[:, 0:128:2], psx[:, 1:128:2]
         HA, VO, DL, QO = (psx[:, 128 + 64 * j:192 + 64 * j] for j in range(4))
+        up, down = t > 0 and c == 0 and rank == 0, t > 0 and c > 0 and rank == N - 1
+        kwin = T.key_s[:, 16:4128] if up else (T.key_s[:, 0:4112] if down else T.key_s[:, 16:4112])
+        cwin = T.cl_s[:, 8:2064] if up else (T.cl_s[:, 0:2056] if down else T.cl_s[:, 8:2056])
+        kp, cp = (("kp",), ("cp",)) if up or down else ((), ())
         kgk, a = [], 0
-        for e, w in P["K"]:
+        for e, w in (P["K"] if t else P["K0"][c]):
             kgk.append("%s_%d" % (k("kg"), a))
-            gather(e, kg[:, 16 * a:16 * (a + w)], T.key_s[:], T.pin[:, o0 + a:o0 + a + w], ("keya", "keyb", pkey), (kgk[-1],), 16 * w)
+            gather(e, kg[:, 16 * a:16 * (a + w)], kwin, T.pin[:, o0 + a:o0 + a + w], ("keya", "keyb", pkey) + kp, (kgk[-1],), 16 * w)
             a += w
         kgk = tuple(kgk)
-        if t and P["ph"] == "V":
-            vts(ph, T.pin[:, o0:o0 + NL], -2048.0, None, A.add, None, (pkey,), (hkey,))
-        mms([(D, T.wk[:, 16 - i:144 - i], kg[:, i:1024:16], i == 0, False) for i in range(NS)], kgk + ("wk",), bd)
-        mms([(D, T.nbd[:], qin, False, False)], ("nbd", qkey), bd)
-        for s in range(MP):
-            op("V", lambda s=s: V.tensor_tensor(mx[:, MW * s:MW * s + MW], qin.indirect(T.rep[:, 0:64 // MP]), kg[:, s:1024:MP], A.max),
-               ("rep", qkey) + kgk, ("%s_%d" % (k("mx"), s),), None, 0.06 + MW * P["gather"] * CY)
-        if P["sf16"]:
-            mms([(HA, T.bdw[:], qin, True, True)], ("bdw", qkey), bx)
-            sact(B("hn")[:], HA, F.Identity, (), (k("hn"),), bx, bias=1536.0 - 1023.5 / 2048.0, scale=1.0 / 2048.0)
-        else:
-            mms([(HA, T.bdw[:], qin, True, False), (HA, T.idh[:], T.c1023[:], False, True)], ("bdw", "idh", "c1023", qkey), bx)
-            sact(B("hy")[:], HA, F.Identity, (), (k("hy"),), bx, bias=BIG, scale=1.0 / 2048.0)
-            vts(B("hn")[:], B("hy")[:], -BIG, None, A.add, None, (k("hy"),), (k("hn"),))
-        mms([(CH, T.idm[:], T.chc[:], True, False), (C1, T.bdw[:], qin, False, False), (C1, T.in2k[:], B("hn")[:], False, False)],
-            ("idm", "in2k", "chc0", "chc1", k("hn")), bx, (), 4)
-        for s in range(MP):
-            mms([(D, T.w2[:, 16 - s - MP * r:144 - s - MP * r], mx[:, MW * s + r:MW * s + MW:16 // MP], False, s == MP - 1 and r == 16 // MP - 1)
-                 for r in range(16 // MP)], ("%s_%d" % (k("mx"), s), "w2"), bd)
+        if t:
+            vts(ph, T.pin[:, o0:o0 + NL], -2063.0 if down else -2048.0, None, A.add, None, (pkey,), (hkey,))
+        if MV:
+            mms([(D, T.wk[:, 16 - i:144 - i], kg[:, i:1024:16], i == vslots[0], False) for i in vslots], kgk + ("wk",), bd)
+            mms([(D, T.nbd[:], qin, False, False)], ("nbd", qkey), bd)
+        pieces, a = [], 0
+        for s, n in MV:
+            w = 1024 // n
+            pieces.append((a, s, n, "%s_%d" % (k("mx"), a)))
+            op("V", lambda a=a, s=s, n=n, w=w: V.tensor_tensor(mx[:, a:a + w], qin.indirect(T.rep[:, rep0[n]:rep0[n] + 64 // n]), kg[:, s:1024:n], A.max),
+               ("rep%d" % n, qkey) + kgk, (pieces[-1][3],), None, 0.06 + w * P["gather"] * CY)
+            a += w
+        for s, n in AB:
+            w, u = 1024 // n, P["AS"]
+            df, bf = T["pst%d" % turn[0]], "F%d" % turn[0]
+            turn[0] = 1 - turn[0]
+            mms([(df[:, 0:w], T.idm[:], kg[:, s:1024:n], True, False)], kgk + ("idm",), bf, (), w // 64)
+            mms([(df[:, r:w:16 // n], T.nid[:], qin, False, r == 16 // n - 1) for r in range(16 // n)], ("nid", qkey), bf)
+            for j in range(u):
+                pieces.append((a, s + n * j, n * u, "%s_%d" % (k("ab"), a)))
+                sact(mx[:, a:a + w // u], df[:, j:w:u], F.Abs, (), (pieces[-1][3],), bf, w // u, scale=0.5)
+                a += w // u
+        mms([(HA, T.bdw[:], qin, True, True)], ("bdw", qkey), bx)
+        sact(B("hn")[:], HA, F.Identity, (), (k("hn"),), bx, bias=1536.0 - 1023.5 / 2048.0, scale=1.0 / 2048.0)
+        mms([(CH, T.idm[:], T.chc[:], True, False), (C1, T.bdw[:], qin, False, False), (C1, T.in2k[:], B("hn")[:], False, False)]
+            + ([(C1, T.idm[:], one64, False, False)] if down else []), ("idm", "in2k", "chc0", "chc1", k("hn")), bx, (), 4)
+        po = P["PO"] or range(len(pieces))
+        for j in po:
+            a, s, n, nm = pieces[j]
+            mms([(D, T.w2[:, 16 - s - n * r:144 - s - n * r], mx[:, a + r:a + 1024 // n:16 // n], not MV and j == po[0] and r == 0,
+                  j == po[-1] and r == 16 // n - 1) for r in range(16 // n)], (nm, "w2"), bd)
         if na == 1.0:
             vts(nr, D, T.th_s[:, 0:1], None, A.is_lt, None, ("th",), (k("nr"),), 64, bd)
         else:
@@ -367,44 +438,34 @@ def build(g, core, T, topo):
         mms([(C1, T.bd4k[:], nr, False, False), (C0, T.sg[:], nr, False, False)], ("bd4k", "sg", k("nr")), bx)
         mms([(AR, T.idh[:], ph, True, False), (AR, T.i8k[:], nr, False, True)], ("idh", "i8k", k("nr"), hkey), bd)
         vtt(B("xx")[:], U, ph, A.min, (hkey,), (k("xx"),), 64, bd)
-        sact(B("ar")[:], AR, F.Identity, (), (k("ar"),), bd, bias=8192.0 * nb - 2048.0)
+        sact(B("ar")[:], AR, F.Identity, (), (k("ar"),), bd, bias=8192.0 * nb - (2049.0 if down else 2048.0))
         mms([(C0, T.bdh[:], B("xx")[:], False, True)], ("bdh", k("xx")), bx)
-        scan(B("sc")[:], T.rst[:], CH, A.add, A.min, ("rst",), (k("sc"),), 128, bx)
-        vts(B("ci")[:], B("sc")[:, 31:128:32], BIG + MK, BIG, A.add, A.subtract, (k("sc"),), (k("ci"),))
-        i4 = T.in4k[:] if na == 1.0 else T.in2b[:]
-        mms([(PP, i4, nr, True, False)], ("in4k", "in2b", k("nr")), bd)
-        op("V", lambda: V.tensor_tensor(B("pf")[:], T.cl_s[:].indirect(B("ci")[:, 0:4]), B("ar")[:], A.max),
-           ("cla", "clb", k("ci"), k("ar")), (k("pf"),), None, 0.06 + 64 * P["gather"] * CY)
-        mms([(PP, T.id32[:], B("pf")[:], False, True)], ("id32", k("pf")), bd, (), 4)
-        pb = -4096.0 * nb
+        scan(B("sc")[:], T.r2[:] if down else T.rst[:], CH, A.add, A.min, ("r2" if down else "rst",), (k("sc"),), 128, bx)
+        vts(B("ci")[:], B("sc")[:, 31:128:32], BIG + MK + (7.0 if down else 0.0), BIG, A.add, A.subtract, (k("sc"),), (k("ci"),))
+        pf = B("pi")[:]
+        op("V", lambda: V.tensor_tensor(pf, cwin.indirect(B("ci")[:, 0:4]), B("ar")[:], A.max),
+           ("cla", "clb", k("ci"), k("ar")) + cp, (k("pf"),), None, 0.06 + 64 * P["gather"] * CY)
         pok = "po%d_%d" % (c, t)
-        vts(T.pout[:, o0:o0 + NL], PP, pb, None, A.add, None, (), (pok,), 64, bd)
+        si, sik = B("s2")[:], k("s2")
+        vts(si, pf, 4095, None, A.bitwise_and, None, (k("pf"),), (sik,))
+        vcp(T.pout[:, o0:o0 + NL], si, (sik,), (pok,))
         nxt = cores[(rank + 1) % N if c == 0 else (rank - 1) % N]
         shift = 1.0 if (c == 0 and rank == N - 1) else (-1.0 if (c and rank == 0) else 0.0)
-        src, sk, PS = T.pout[:, o0:o0 + NL], pok, PP
-        if shift:
-            if shift > 0:
-                sact(B("wr")[:], PP, F.Relu, (), (k("wr"),), bd, bias=pb - 4094.0)
-            else:
-                sact(B("wr")[:], PP, F.Relu, (), (k("wr"),), bd, bias=1.0 - pb, scale=-1.0)
-            mms([(P2, i4, nr, True, False), (P2, T.id32[:], B("pf")[:], False, False),
-                 (P2, T.in4k[:], B("wr")[:], False, shift > 0)] + ([(P2, T.i8k[:], B("wr")[:], False, na == 1.0)] if shift < 0 else [])
-                + ([(P2, T.i8k[:], B("wr")[:], False, True)] if shift < 0 and na != 1.0 else []), (k("wr"), k("pf"), k("nr")), bd, (), 7)
-            src, sk, PS = T.pw[:, o0:o0 + NL], "pw%d_%d" % (c, t), P2
-            if t < STEPS - 1:
-                vts(src, P2, pb + shift, None, A.add, None, (), (sk,), 64, bd)
         a1 = "ap%d_%d" % (c, t + 1)
         if t == STEPS - 1:
             a, b = NL * c, NL * c + NL
-            sact(T.ypo[:, a:b], PS, F.Identity, (), ("ypo%d" % c,), bd, bias=pb + shift)
+            if shift:
+                vts(B("s1")[:], pf, shift + 4096.0, None, A.add, None, (k("pf"),), (k("s1"),))
+                si, sik = B("s3")[:], k("s3")
+                vts(si, B("s1")[:], 4095, None, A.bitwise_and, None, (k("s1"),), (sik,))
+            vcp(T.ypo[:, a:b], si, (sik,), ("ypo%d" % c,))
             send(nxt, [(T.yp_s[:, a:b], T.ypo[:, a:b])], a1, ("ypo%d" % c,), ("yp%d" % c,), P["peng"], True)
-        elif P["ph"] == "V":
-            send(nxt, [(T.pin[:, o1:o1 + NL], src)], a1, (sk,), ("p%d_%d" % (c, t + 1),), P["peng"], True)
         else:
-            hok = "ho%d_%d" % (c, t)
-            sact(T.pho[:, o0:o0 + NL], PS, F.Identity, (), (hok,), bd, bias=pb + shift - 2048.0)
-            send(nxt, [(T.pin[:, o1:o1 + NL], src), (T.phin[:, o1:o1 + NL], T.pho[:, o0:o0 + NL])], a1, (sk, hok),
-                 ("p%d_%d" % (c, t + 1), "ph%d_%d" % (c, t + 1)), P["peng"], True)
+            src, sk = T.pout[:, o0:o0 + NL], pok
+            if shift:
+                src, sk = T.pw[:, o0:o0 + NL], "pw%d_%d" % (c, t)
+                vts(src, si, 1.0 if shift > 0 else 15.0, None, A.add, None, (sik,), (sk,))
+            send(nxt, [(T.pin[:, o1:o1 + NL], src)], a1, (sk,), ("p%d_%d" % (c, t + 1),), P["peng"], True)
         egk, a = [], 0
         for e, w in P["E"]:
             egk.append("%s_%d" % (k("eg"), a))
@@ -419,37 +480,34 @@ def build(g, core, T, topo):
             vts(B("zz")[:], DL, 0.5, None, A.is_lt, None, (), (k("zz"),), 64, bx)
         else:
             sact(B("zz")[:], DL, F.Sign, (), (k("zz"),), bx, bias=0.5, scale=-1.0)
-        mms([(QO, T.idm[:], T.cq[:], True, False), (QO, T.ihf[:], qin, False, False), (QO, T.eb[:], B("zz")[:], False, True)],
+        mms([(QO, T.ihf[:], qin, True, False)] + ([(QO, T.idm[:], T.cq[:], False, False)] if zb else []) + [(QO, T.eb[:], B("zz")[:], False, True)],
             ("idm", "cq", "ihf", "eb", qkey, k("zz")), bx)
-        if t < STEPS - 1:
-            mms([(T.pst0[32 * c:32 * c + 32, 64 * t:64 * t + 64], T.tw[:], B("zz")[:], True, True)], ("tw", k("zz")), None, ("tk%d_%d" % (c, t),))
-        else:
-            mms([(T.pst1[32 * c:32 * c + 32, 0:64], T.tw[:], B("zz")[:], True, True)], ("tw", k("zz"), "cq", "eb"), None, ("tk%d_%d" % (c, t),))
         qok = "qo%d_%d" % (c, t)
         vts(T.qout[:, o0:o0 + NL], QO, BIG, BIG, A.add, A.subtract, (), (qok,), 64, bx)
+        a, b = 32 * (t % 3), 384 + 64 * (t // 3)
+        mms([(psx[a:a + 32, b:b + 64], T.tw[:], B("zz")[:], True, True)], ("tw", k("zz")), bx, (k("tk"),))
+        if t in (2, 4, 5):
+            a, (u, v) = 192 * (t // 3) + 64 * c, {2: (0, 96), 4: (0, 64), 5: (64, 96)}[t]
+            sact(T.yt_s[u:v, a:a + 64], psx[u:v, b:b + 64], F.Identity, (), ("yt%d_%d" % (c, t),), bx, bias=16.0 * (1 - zb), scale=-za)
         send(nxt, [(T.qin[:, o1:o1 + NL], T.qout[:, o0:o0 + NL])], "aq%d_%d" % (c, t + 1), (qok,), ("q%d_%d" % (c, t + 1),), P["qeng"], False)
 
     for t in range(STEPS):
         for c in range(NC):
             step(t, c)
     nout = [0]
+    cur[1] = STEPS
 
     def store(out, in_, reads):
         nout[0] += 16
         op("Y", lambda: Y.dma_start(out, in_), reads, (), None, 0.1, 2.0, "outs", None)
 
-    last = STEPS - 1
-    sact(T.yt_s[0:96, 0:64 * last], T.pst0[0:96, 0:64 * last], F.Identity, tuple("tk%d_%d" % (c, t) for c in range(NC) for t in range(last)),
-         ("yta",), None, 64 * last, bias=16.0 * (1 - zb), scale=-za)
-    sact(T.yt_s[0:96, 64 * last:64 * STEPS], T.pst1[0:96, 0:64], F.Identity, tuple("tk%d_%d" % (c, last) for c in range(NC)),
-         ("ytb",), None, 64, bias=16.0 * (1 - zb), scale=-za)
     o6 = STEPS * 192
     for t in range(STEPS):
-        for c in range(NC):
-            store(T.yt[:, 192 * t + 64 * c:192 * t + 64 * c + 64], T.yt_s[32 * c:32 * c + 8, 64 * t:64 * t + 64], ("yta" if t < last else "ytb",))
+        a, b = 32 * (t % 3), 192 * (t // 3)
+        store(T.yt[:, 192 * t:192 * t + 192], T.yt_s[a:a + 8, b:b + 192], tuple("yt%d_%d" % (c, (2, 2, 2, 4, 4, 5)[t]) for c in range(NC)))
+    store(T.yp[:], T.yp_s[:], tuple("yp%d" % c for c in range(NC)))
     for c in range(NC):
         a, b = NL * c, NL * c + NL
-        store(T.yp[:, a:b], T.yp_s[:, a:b], ("yp%d" % c,))
         store(T.yq[:, a:b], T.qin[:, o6 + a:o6 + b], ("q%d_%d" % (c, STEPS),))
     return ops, sends[0], nout[0]
 
@@ -504,7 +562,7 @@ def rank_program(g, core, T, topo):
     if T.rank_of(core) is None:
         return
     ops, nsend, nout = build(g, core, T, topo)
-    key = repr(sorted(P.items()))
+    key = repr(sorted(P.items())) + ORDER[0]
     if key not in PLANS:
         PLANS[key] = plan_all([build(g, c, T, topo)[0] for c in T.cores])
     emit_all(g, T, ops, PLANS[key][T.rank_of(core)], nsend, nout)

@@ -14,13 +14,13 @@ P = {
     "K": (("S", 32), ("S", 32)),
     "E": (("S", 40), ("V", 24)),
     "K0": ((("S", 32), ("V", 32)), (("S", 32), ("S", 32)), (("S", 32), ("S", 32))),
-    "MV": ((0, 2),), "AB": ((1, 2),), "AS": 1, "PO": None, "and": 2,
+    "MV": ((0, 2),), "AB": ((1, 2),), "AS": 1, "PO": None, "u16": 3, "rev": 1, "sc4": 0,
     "nr": "V", "z": "V", "ph": "send", "sf16": True, "qeng": 16, "peng": 8, "gate": True, "ka": 1536, "ca": 768,
     "look": 0.1, "seed": 0, "noise": 0.0, "stag": (0.0, 0.0, 0.0),
     "cy": 0.83e-3 * 1.1, "gather": 1.4, "hop": 0.15, "net": 1.3, "row": 0.045, "pe": 0.5e-3, "fix": 0.01, "mb": 4.5,
 }
-P.update({"mb": 1.8, "MV": ((0, 4), (1, 4), (2, 4)), "AB": ((3, 4),), "K": (("S", 64),),
-          "K0": ((("S", 32), ("V", 32)), (("S", 64),), (("S", 64),)), "nr": "V", "E": (("S", 42), ("V", 22))})
+P.update({"mb": 1.8, "MV": ((0, 4), (2, 4)), "AB": ((1, 4), (3, 4)), "PO": (0, 2, 1, 3), "K": ((("S", 52), ("V", 12)),) * 3,
+          "K0": ((("S", 32), ("V", 32)), (("S", 64),), (("S", 64),)), "nr": "V", "E": ((("S", 36), ("V", 28)),) * 3})
 
 BF, F3, I3, U1, H1 = "bfloat16", "float32", "int32", "uint16", "float16"
 SCRATCH = {
@@ -36,7 +36,7 @@ SCRATCH = {
     "rst": ("sbuf", [128, 128], F3), "seg": ("sbuf", [128, 64], F3), "rowm": ("sbuf", [128, 64], F3), "r2": ("sbuf", [128, 128], F3),
     "pst0": ("psum", [128, 512], F3), "pst1": ("psum", [128, 512], F3),
 }
-for _n in ("ones", "bd", "idm", "ltm", "gw0", "gw", "sg", "nbd", "bd4k", "i8k", "ihf", "bdw", "eb0", "eb", "chc", "shm", "dfm", "nid", "offd"):
+for _n in ("ones", "bd", "idm", "ltm", "gw0", "gw", "sg", "nbd", "bd4k", "i8k", "ihf", "bdw", "eb0", "eb", "chc", "shm", "dfm", "nid", "offd", "c78"):
     SCRATCH[_n] = ("sbuf", [128, 128], BF)
 for _n in ("bdh", "idh", "in2k", "dm"):
     SCRATCH[_n] = ("sbuf", [128, 128], H1)
@@ -48,14 +48,14 @@ for _n in ("kcol", "sgcol", "thb", "k15", "k16"):
     SCRATCH[_n] = ("sbuf", [128, 1], F3)
 for _c in range(NC):
     for _n, _w, _d in (("kg", 1024, BF), ("mx", 1024, BF), ("eg", 1024, BF), ("nr", 64, BF), ("ar", 64, F3),
-                       ("xx", 64, H1), ("hn", 64, H1), ("sc", 128, F3), ("ci", 4, U1), ("pi", 64, I3), ("s1", 64, I3), ("s2", 64, I3), ("s3", 64, I3),
-                       ("vt", 64, F3), ("rs", 64, H1), ("rt", 64, H1), ("zz", 64, BF)):
+                       ("xx", 64, H1), ("hn", 64, H1), ("sc", 128, F3), ("ci", 128, U1), ("pi", 64, I3) if not P["u16"] else ("pu", 64, F3), ("wf", 64, BF), ("s1", 64, I3), ("s2", 64, I3), ("s3", 64, I3),
+                       ("vt", 64, F3), ("rs", 64, H1), ("rt", 64, H1) if not P["rev"] else ("zt", 64, BF), ("zz", 64, BF)):
         SCRATCH["%s%d" % (_n, _c)] = ("sbuf", [128, _w], _d)
     SCRATCH["psd%d" % _c] = ("psum", [128, 512], F3)
     SCRATCH["psx%d" % _c] = ("psum", [128, 512], F3)
 
 SEMAPHORES = (["sV", "sS", "sP", "sG", "lsem", "outs"]
-              + ["ld_" + n for n in ("keya", "keyb", "em", "cla", "clb", "pl", "q", "emb", "w", "th", "kp", "cp")]
+              + ["ld_" + n for n in ("keya", "keyb", "em", "cl", "pl", "q", "emb", "w", "th", "kp", "cp")]
               + ["a%s%d_%d" % (k, c, t) for k in "pq" for c in range(NC) for t in range(1, STEPS + 1)])
 
 
@@ -110,7 +110,8 @@ def plan(ops):
 
 
 PLANS = {}
-ORDER = ["020304051a1d1f1h1i2d2f2h0100070e0b0j100v0p1317191q08090m0t1m0l0d140o0s150q1v180x1j1g161b0i0n0h0y0z1e1k1l060a0c2s2v0f0k0r0u1c0g24232k2e2a28292b20120w112w341o1n1r1w1s1t1x1u1y212o2u361z222c2i2l2y3d2z31333g3j3q3t40434749484c4l4n4q4t515355586f5a5b1p262p252g2m2j2n2r35373n2q2t38393c3l3s3m3p3r3u3w41454e4g4s4w4y4j4k4p5254575c5e5h5k6l5p5q27303f2x323e3a3b3i3x3z463h3k3o3v3y424b444a4h4d4f4i4m4o4r4u4z504v4x595d5f5j5m5o5s5u7n5z6056645n5v5r5x625i5t6a6m6o6w5y696b6g6i6s6z6t6u6y74777b7h7m7t7v7w7x81888e8i8l8o8p8q8u938y8z5g63616j67666d65686e707a7g6n6p6r6v727c7k7d7f7j7l7q7u7z84878d8g8h8a8b8k8r8t8x9295989bak9c9d5w5l6c716k6q6x6h73767r7s7y7578797e7i7o827p80868385898c8f8j8w90918m8n8v94979a9e9g9i9ka29p9q8s9h9f9s9m9r9u999ja19la5aa9t9ya0acaeaiasajamawavb0b4b6b9bebibkbjbtbxc4c8cbcfciclcpcudscrcs969x9n9w9za3a69va7abatazbbadahalaqaub1bdb2b7babgbmbpbrbvbyc3c6c7c0c1cacjcmcnctcwczd2dwdzd5d69oa8a4axa9aganafaoaparbfbnayb3b5b8bcbhboblbqbubsbwbzc2c5c9cecgchcccdcocvcyd1d3d7d9dce8eidfdgckcqd4didddhdkd0dadoe2e5eadjdldrdudye3ele4ebecenerevf4f9fefifjfkflfvg2g4g7gbgfgigkgqgngocxd8dedtdqdne0dmdpdvefetf3e6e9egehekeyf7f0f2f6f8fcfhfpfrfufwg0g1fyfzg6geghgjgpgsgvgyhhgzh0dbemdxeoe1e7edeeejepfdfgfmeqeseuf1f5fafnfbfffsfofqftfxg3g5gagcgdg8g9glgrgugxh1h3h5h7iwh8h9gggmgwhihahdhgh2h6hchkhxi8hjhmhnhphsi2idi3i5iaieihilioixj1j6j8j7jcjjjrjvjyk1k5k7k8ljllkbkcgth4hbhqhlhohthfhrhvhzi7iuhuhwibicifiniyiqiritizj4jbjfjijljqjtjujnjojxk6kakdkekkkokrlalxkukvhehyi4iii0i9i6i1igikj0j5jaijimipisivj2jdj3j9jhjejgjkjmjpjsk0k2k3jwjzk9kgkjklknkqktkxlclnl1l2k4khkil6l3kzl5kpkyl9lslzmcl7l8lblglmlymdm0m4m6memhmkmomun0njnmnnn4n5nentnwo0o8odogojooosopoqkfkml0lrlflelhl4lilom8mampltlwm1m7mbmjmsmlmnmrmtmyn3n8nandnsnvo1o4o5ngnlnrnzo3o6o7oboeohokowolomkwksldm9lplvm5lklqlumvmzn2mfmgmimmmqmwn6mxn1nbn7n9ncnfnhnkninpnunxnynonqo2o9oaocofoionorotouoxoyexezewm2m3p1ovp0ozp2"]
+ORDER = ["010204051b1c1e1f1h1k1l0300090g0e0l0r0o0w0y11181o0b0d0i0m0z06070n140v1m1v0p1z0s0q0t0x161d0j120h2810131g19080c0f1t200k151a0u1w0a1y2j2m2l2h2c2d2e2b2617212p3c1i1j1p241q221u1x271r1s29232f2v252g2k2n2q2t2w2u2y3a34373h3n3q3y3z40424a4i4n4l4q4u4y525556571n2a322s302r2x312o2z35393e3w333b3g3i3o3s3x3v414943484b4d4j4r4v4w4m4o5158595a5j5p5r5x6g60612i363r383p3d3f3l3k3m3u3j3t4g444546474c4e4h4f4k4s4p4t4x535b5h5m5n5d5e5o5u66656c6e6i6o786u6v4z50545c5v5q5y5g5s5z5f5t625w676m686a6b6d6h6j6n636k6p6r6s6x74757d7h7k7i7j7u85888a8e8h8l8o8w8z905l5k5i646y70766l6t716f6w73727e7v77797b7c7n7r7z7s7x8081868d8f8p8s8x8y8t8u94999e9f9i9n9p9vaca0a1696q836z7q7o7y7a7l7p7g7m7w7f7t8c828487898g8j8m8k8n928q919395989g9k9l9b9c9m9ua3a2aaadafakb4aoap8b8i968r9q9j9x979a9w8v9d9y9sa5aj9ra6a8a9aeagala4ahamaqaraub0b6babdbfbebhbsc1c7c5cbceciclcnd7cocp9h9o9t9zayawb1aiasaxabatazb2bbbob3b5b7b9bgbmbxbnbtbvbyc3c9cdcqcscwcxctcud1d6dcdbdidndpdseberdwdxa7anc8avbkbpbub8bibqbjblbrbcbwc6bzc0c2c4cccfcjchckczcmcyd0d3d5dgdldmdadfdkdrdzdye5eaedegexf8elemcacgd2crdddodtd4d8dvcvd9e0dee2eidue3e6e8eceeeje7efekeoepeteyf1f6f9fbfdfafug5gbgcgeghglgph5gwgxdhdjdqe1euezf2eheqewe9esf5f0fcfvf3f4fefffnfqfwfsfxg0g1g6gdgggogsgygzgtguh2h7hbhchhhnhphuichyhze4eng3evfmfpfyf7flfrfjfoftfifzgag2g4g7g8gfgigmgkgnh1gqh0h3h4h8hghkhlhdhfhmhti1i0i9idifilivirisg9gjh9grhqhohvh6hahxgvhei2hri5ijhwi6i8iaieigiki3ihimioipiuj1j6jajdjfjejjjtk1k6k4kbkekikll3ldkokphihjhsi4izixj3iiiqiyibitj0j2jbjpj4j5j7j9jhjmjqjnjujwjyk2k7kdknkukykzkrksl0l6l9lalflllnlsmdmklwlxi7ink0iwjljojvj8jcjxjijkjrjgjsk9jzk3k5k8kckgkjkhkkkwkmkvkxl1l5leljlkl7lclilrlzlym6mamcmgmyn5mmmnkakfl2kqlolmltl4l8lvktlbm0lpm3mhlum4m7m8mbmemlm2mfmpmqmrn3n8nenjoaofognunwocoloropouoxp0papcpjpdpelglhlqm1mumwn6mimomtm9msmxn0n4nomzn2n7n9ngnlnrnnnvo3nyo2o5o7odomotp3p5p6ohoioqowp1p2pbpgpkpopqpuprpsm5mjo4mvnkninpn1nfnmncnhnsndnqo1ntnxnzo0o6o8obo9oeonojokooosovp4p8p9phpioyozp7pfpmplpnppptpvpwpzpxpyfgfhfknanbq2q1q0q3q4"]
+OLD = ["020304051a1d1f1h1i2d2f2h0100070e0b0j100v0p1317191q08090m0t1m0l0d140o0s150q1v180x1j1g161b0i0n0h0y0z1e1k1l060a0c2s2v0f0k0r0u1c0g24232k2e2a28292b20120w112w341o1n1r1w1s1t1x1u1y212o2u361z222c2i2l2y3d2z31333g3j3q3t40434749484c4l4n4q4t515355586f5a5b1p262p252g2m2j2n2r35373n2q2t38393c3l3s3m3p3r3u3w41454e4g4s4w4y4j4k4p5254575c5e5h5k6l5p5q27303f2x323e3a3b3i3x3z463h3k3o3v3y424b444a4h4d4f4i4m4o4r4u4z504v4x595d5f5j5m5o5s5u7n5z6056645n5v5r5x625i5t6a6m6o6w5y696b6g6i6s6z6t6u6y74777b7h7m7t7v7w7x81888e8i8l8o8p8q8u938y8z5g63616j67666d65686e707a7g6n6p6r6v727c7k7d7f7j7l7q7u7z84878d8g8h8a8b8k8r8t8x9295989bak9c9d5w5l6c716k6q6x6h73767r7s7y7578797e7i7o827p80868385898c8f8j8w90918m8n8v94979a9e9g9i9ka29p9q8s9h9f9s9m9r9u999ja19la5aa9t9ya0acaeaiasajamawavb0b4b6b9bebibkbjbtbxc4c8cbcfciclcpcudscrcs969x9n9w9za3a69va7abatazbbadahalaqaub1bdb2b7babgbmbpbrbvbyc3c6c7c0c1cacjcmcnctcwczd2dwdzd5d69oa8a4axa9aganafaoaparbfbnayb3b5b8bcbhboblbqbubsbwbzc2c5c9cecgchcccdcocvcyd1d3d7d9dce8eidfdgckcqd4didddhdkd0dadoe2e5eadjdldrdudye3ele4ebecenerevf4f9fefifjfkflfvg2g4g7gbgfgigkgqgngocxd8dedtdqdne0dmdpdvefetf3e6e9egehekeyf7f0f2f6f8fcfhfpfrfufwg0g1fyfzg6geghgjgpgsgvgyhhgzh0dbemdxeoe1e7edeeejepfdfgfmeqeseuf1f5fafnfbfffsfofqftfxg3g5gagcgdg8g9glgrgugxh1h3h5h7iwh8h9gggmgwhihahdhgh2h6hchkhxi8hjhmhnhphsi2idi3i5iaieihilioixj1j6j8j7jcjjjrjvjyk1k5k7k8ljllkbkcgth4hbhqhlhohthfhrhvhzi7iuhuhwibicifiniyiqiritizj4jbjfjijljqjtjujnjojxk6kakdkekkkokrlalxkukvhehyi4iii0i9i6i1igikj0j5jaijimipisivj2jdj3j9jhjejgjkjmjpjsk0k2k3jwjzk9kgkjklknkqktkxlclnl1l2k4khkil6l3kzl5kpkyl9lslzmcl7l8lblglmlymdm0m4m6memhmkmomun0njnmnnn4n5nentnwo0o8odogojooosopoqkfkml0lrlflelhl4lilom8mampltlwm1m7mbmjmsmlmnmrmtmyn3n8nandnsnvo1o4o5ngnlnrnzo3o6o7oboeohokowolomkwksldm9lplvm5lklqlumvmzn2mfmgmimmmqmwn6mxn1nbn7n9ncnfnhnkninpnunxnynonqo2o9oaocofoionorotouoxoyexezewm2m3p1ovp0ozp2"]
 
 
 def join(lists):
@@ -154,7 +155,7 @@ def keyed(ops, order, place):
     key = [0.0] * len(ops)
     for i in order:
         o = ops[i]
-        k = place.get(o["name"], 0.0)
+        k = place.get(o["name"], place.get(o["name"].replace("wf", "ph"), 0.0))
         for d in o["deps"] | o["order"]:
             if key[d] + 1e-4 > k:
                 k = key[d] + 1e-4
@@ -244,18 +245,16 @@ def build(g, core, T, topo):
             ops[i]["order"].add(lastld[q])
         lastld[q] = i
 
-    ka, ca, mb = P["ka"], P["ca"], P["mb"]
-    gate = P["gate"]
+    ka, mb = P["ka"], P["mb"]
     load("S", T.pl_s[:], T.pl[:], "pl", "pl_s", 2.0)
     load("Y", T.key_s[:, 16:16 + ka], T.key[:, 0:ka], "keya", "keya", 1.5 + 0.75 * mb)
     load("Y", T.key_s[:, 16 + ka:4112], T.key[:, ka:], "keyb", "keyb", 1.5 + mb)
     load("S", T.qin[:, 0:192], T.q[:], "q", "q0", 2.2)
     load("Y", T.w_s[:], T.w[:], "w", "w", 2.0, ("keya",))
     load("Y", T.th_s[:], T.th[:], "th", "th", 2.0)
-    load("Y", T.cl_s[:, 8:8 + ca], T.cl[:, 0:ca], "cla", "cla", 1.5 + 0.75 * mb + (0 if gate else mb), ("keya",) if gate else ())
-    load("Y", T.cl_s[:, 8 + ca:2056], T.cl[:, ca:], "clb", "clb", 1.5 + mb + (0 if gate else mb))
+    load("Y", T.cl_s[:, 8:2056], T.cl[:], "cl", "cl", 1.5 + 2 * mb)
     load("Y", T.emb_s[:], T.emb[:], "emb", "emb", 2.0)
-    load("Y", T.em_s[:], T.em[:], "em", "em", 1.5 + mb + (0 if gate else 2 * mb), ("cla",) if gate else ())
+    load("Y", T.em_s[:], T.em[:], "em", "em", 1.5 + 2 * mb, ("keyb",))
     if rank == 0:
         load("Y", T.key_s[:, 4112:4128], T.key[:, 0:16], "kp", "kp", 2.0)
         load("Y", T.cl_s[:, 2056:2064], T.cl[:, 0:8], "cp", "cp", 2.0)
@@ -308,7 +307,7 @@ def build(g, core, T, topo):
     vts(T.bdh[:], T.bd[:], 0.5, None, A.mult, None, ("bd",), ("bdh",))
     k0 = 18432.0 + 2048.0 * 104 * nb
     k1 = (3145728.0 if P["sf16"] else 0.0) + 65536.0 * nb
-    vts(T.seg[:], T.rowm[:], T.kcol[:, 0:1], -MK, A.is_equal, A.mult, ("rowm", "kcol"), ("seg",))
+    vts(T.seg[:], T.rowm[:], T.kcol[:, 0:1], MK, A.not_equal, A.mult, ("rowm", "kcol"), ("seg",))
     vts(T.chc[:, 0:128:2], T.seg[:], k0, None, A.add, None, ("seg",), ("chc0",))
     vts(T.chc[:, 1:128:2], T.seg[:], k1, None, A.add, None, ("seg",), ("chc1",))
     vfill(T.rst[:], 0.0, (), ("rst",), 128)
@@ -317,6 +316,8 @@ def build(g, core, T, topo):
     if rank == N - 1:
         vts(T.r2[:], T.rst[:], 0.0, None, A.max, None, ("rst",), ("r2",), 128)
         vfill(T.r2[:, 31:128:32], 0.25, (), ("r2",))
+        vfill(T.c78[:], 7.0, (), ("c78",))
+        vfill(T.c78[:, 1:128:2], 8.0, (), ("c78",))
     vfill(T.seg[:], 4096.0, (), ("seg",))
     vfill(T.seg[:, 0:64:16], -4096.0, (), ("seg",))
     vts(T.k15[:], T.kcol[:], 15.0, None, A.is_equal, None, ("kcol",), ("k15",))
@@ -394,7 +395,7 @@ def build(g, core, T, topo):
         cwin = T.cl_s[:, 8:2064] if up else (T.cl_s[:, 0:2056] if down else T.cl_s[:, 8:2056])
         kp, cp = (("kp",), ("cp",)) if up or down else ((), ())
         kgk, a = [], 0
-        for e, w in (P["K"] if t else P["K0"][c]):
+        for e, w in (P["K"][c] if t else P["K0"][c]):
             kgk.append("%s_%d" % (k("kg"), a))
             gather(e, kg[:, 16 * a:16 * (a + w)], kwin, T.pin[:, o0 + a:o0 + a + w], ("keya", "keyb", pkey) + kp, (kgk[-1],), 16 * w)
             a += w
@@ -424,7 +425,8 @@ def build(g, core, T, topo):
         mms([(HA, T.bdw[:], qin, True, True)], ("bdw", qkey), bx)
         sact(B("hn")[:], HA, F.Identity, (), (k("hn"),), bx, bias=1536.0 - 1023.5 / 2048.0, scale=1.0 / 2048.0)
         mms([(CH, T.idm[:], T.chc[:], True, False), (C1, T.bdw[:], qin, False, False), (C1, T.in2k[:], B("hn")[:], False, False)]
-            + ([(C1, T.idm[:], one64, False, False)] if down else []), ("idm", "in2k", "chc0", "chc1", k("hn")), bx, (), 4)
+            + ([(CH, T.idm[:], T.c78[:], False, False) if P["sc4"] else (C1, T.idm[:], one64, False, False)] if down else []),
+            ("idm", "in2k", "chc0", "chc1", "c78", k("hn")), bx, (), 4)
         po = P["PO"] or range(len(pieces))
         for j in po:
             a, s, n, nm = pieces[j]
@@ -436,26 +438,48 @@ def build(g, core, T, topo):
             sact(nr, D, F.Sign, ("thb",), (k("nr"),), bd, bias=T.thb[:, 0:1], scale=-1.0)
         mms([(U, T.idm[:], T.cu[:], True, False), (U, T.gw[:], nr, False, True)], ("idm", "cu", "gw", k("nr")), bd)
         mms([(C1, T.bd4k[:], nr, False, False), (C0, T.sg[:], nr, False, False)], ("bd4k", "sg", k("nr")), bx)
-        mms([(AR, T.idh[:], ph, True, False), (AR, T.i8k[:], nr, False, True)], ("idh", "i8k", k("nr"), hkey), bd)
+        sab = P["u16"] == 3
+        wrap = []
+        if sab and (up or down):
+            vts(B("wf")[:], T.pin[:, o0:o0 + NL], 4096.0 if up else 15.0, (-0.5 if up else 0.5) / na, A.is_equal, A.mult, (pkey,), (k("wf"),))
+            wrap = [(AR, T.i8k[:], B("wf")[:], False, False)]
+        mms([(AR, T.idh[:], ph, True, False)] + wrap + [(AR, T.i8k[:], nr, False, True)], ("idh", "i8k", k("nr"), hkey, k("wf")), bd)
         vtt(B("xx")[:], U, ph, A.min, (hkey,), (k("xx"),), 64, bd)
-        sact(B("ar")[:], AR, F.Identity, (), (k("ar"),), bd, bias=8192.0 * nb - (2049.0 if down else 2048.0))
+        if sab:
+            sact(B("ar")[:], AR, F.Identity, (), (k("ar"),), bd, bias=8192.0 * (1 - nb) - (2047.0 if down else 2048.0), scale=-1.0)
+        else:
+            sact(B("ar")[:], AR, F.Identity, (), (k("ar"),), bd, bias=8192.0 * nb - (2049.0 if down else 2048.0))
         mms([(C0, T.bdh[:], B("xx")[:], False, True)], ("bdh", k("xx")), bx)
-        scan(B("sc")[:], T.r2[:] if down else T.rst[:], CH, A.add, A.min, ("r2" if down else "rst",), (k("sc"),), 128, bx)
-        vts(B("ci")[:], B("sc")[:, 31:128:32], BIG + MK + (7.0 if down else 0.0), BIG, A.add, A.subtract, (k("sc"),), (k("ci"),))
-        pf = B("pi")[:]
-        op("V", lambda: V.tensor_tensor(pf, cwin.indirect(B("ci")[:, 0:4]), B("ar")[:], A.max),
-           ("cla", "clb", k("ci"), k("ar")) + cp, (k("pf"),), None, 0.06 + 64 * P["gather"] * CY)
+        if P["sc4"]:
+            def four():
+                r = None
+                for h in range(4):
+                    r = V.tensor_tensor_scan(B("ci")[:, h:128:4], (T.r2 if down else T.rst)[:, 0:32], psx[:, 32 * h:32 * h + 32], 0.0, A.add, A.min)
+                return r
+            op("V", four, ("r2" if down else "rst",), (k("ci"),), bx, vd(256))
+            cil = B("ci")[:, 124:128]
+        else:
+            scan(B("sc")[:], T.r2[:] if down else T.rst[:], CH, A.add, A.min, ("r2" if down else "rst",), (k("sc"),), 128, bx)
+            vts(B("ci")[:, 0:4], B("sc")[:, 31:128:32], BIG + (7.0 if down else 0.0), BIG, A.add, A.subtract, (k("sc"),), (k("ci"),))
+            cil = B("ci")[:, 0:4]
+        pf = B("pu")[:] if sab else B("pi")[:]
+        op("V", lambda: V.tensor_tensor(pf, cwin.indirect(cil), B("ar")[:], A.min if sab else A.max),
+           ("cl", k("ci"), k("ar")) + cp, (k("pf"),), None, 0.06 + 64 * P["gather"] * CY)
         pok = "po%d_%d" % (c, t)
         si, sik = B("s2")[:], k("s2")
-        vts(si, pf, 4095, None, A.bitwise_and, None, (k("pf"),), (sik,))
-        vcp(T.pout[:, o0:o0 + NL], si, (sik,), (pok,))
+        if P["u16"]:
+            si, sik = T.pout[:, o0:o0 + NL], pok
+            sact(si, pf, F.Abs, (k("pf"),), (sik,))
+        else:
+            vts(si, pf, 4095, None, A.bitwise_and, None, (k("pf"),), (sik,))
+            vcp(T.pout[:, o0:o0 + NL], si, (sik,), (pok,))
         nxt = cores[(rank + 1) % N if c == 0 else (rank - 1) % N]
         shift = 1.0 if (c == 0 and rank == N - 1) else (-1.0 if (c and rank == 0) else 0.0)
         a1 = "ap%d_%d" % (c, t + 1)
         if t == STEPS - 1:
             a, b = NL * c, NL * c + NL
             if shift:
-                vts(B("s1")[:], pf, shift + 4096.0, None, A.add, None, (k("pf"),), (k("s1"),))
+                vts(B("s1")[:], si, shift + 4096.0, None, A.add, None, (sik,), (k("s1"),))
                 si, sik = B("s3")[:], k("s3")
                 vts(si, B("s1")[:], 4095, None, A.bitwise_and, None, (k("s1"),), (sik,))
             vcp(T.ypo[:, a:b], si, (sik,), ("ypo%d" % c,))
@@ -467,16 +491,23 @@ def build(g, core, T, topo):
                 vts(src, si, 1.0 if shift > 0 else 15.0, None, A.add, None, (sik,), (sk,))
             send(nxt, [(T.pin[:, o1:o1 + NL], src)], a1, (sk,), ("p%d_%d" % (c, t + 1),), P["peng"], True)
         egk, a = [], 0
-        for e, w in P["E"]:
+        for e, w in P["E"][c]:
             egk.append("%s_%d" % (k("eg"), a))
             gather(e, eg[:, 16 * a:16 * (a + w)], T.em_s[:], T.pout[:, o0 + a:o0 + a + w], ("em", pok), (egk[-1],), 16 * w, -128.0)
             a += w
         mms([(VO, T.idm[:], eg[:, i:1024:16], i == 0, i == NS - 1) for i in range(NS)], tuple(egk) + ("idm",), bx)
         op("V", lambda: V.transpose(B("vt")[:], VO), (), (k("vt"),), bx, vd(64))
         scan(B("rs")[:], T.seg[:], B("vt")[:], A.min, A.max, ("seg", k("vt")), (k("rs"),))
-        op("V", lambda: V.transpose(B("rt")[:], B("rs")[:]), (k("rs"),), (k("rt"),), None, vd(64))
-        mms([(DL, T.dm[:], B("rt")[:], True, True)], ("dm", k("rt")), bx)
-        if za == 1.0:
+        if P["rev"]:
+            scan(psx[:, 319:255:-1], T.seg[:], B("vt")[:, ::-1], A.min, A.max, ("seg", k("vt")), (k("sx"),), 64, bx)
+            vtt(B("zt")[:], B("rs")[:], DL, A.is_ge, (k("rs"), k("sx")), (k("zt"),), 64, bx)
+            op("V", lambda: V.transpose(B("zz")[:], B("zt")[:]), (k("zt"),), (k("zz"),), None, vd(64))
+        else:
+            op("V", lambda: V.transpose(B("rt")[:], B("rs")[:]), (k("rs"),), (k("rt"),), None, vd(64))
+            mms([(DL, T.dm[:], B("rt")[:], True, True)], ("dm", k("rt")), bx)
+        if P["rev"]:
+            pass
+        elif za == 1.0:
             vts(B("zz")[:], DL, 0.5, None, A.is_lt, None, (), (k("zz"),), 64, bx)
         else:
             sact(B("zz")[:], DL, F.Sign, (), (k("zz"),), bx, bias=0.5, scale=-1.0)

@@ -14,29 +14,29 @@ P = {
     "K": (("S", 32), ("S", 32)),
     "E": (("S", 40), ("V", 24)),
     "K0": ((("S", 32), ("V", 32)), (("S", 32), ("S", 32)), (("S", 32), ("S", 32))),
-    "MV": ((0, 2),), "AB": ((1, 2),), "AS": 1, "PO": None, "u16": 3, "rev": 1, "sc4": 0,
+    "MV": ((0, 2),), "AB": ((1, 2),), "AS": 1, "PO": None, "u16": 3, "rev": 1, "ha": 0, "sc4": 1, "arl": 1, "dbl": 1, "VS": (0, 0, 0),
     "nr": "V", "z": "V", "ph": "send", "sf16": True, "qeng": 16, "peng": 8, "gate": True, "ka": 1536, "ca": 768,
     "look": 0.1, "seed": 0, "noise": 0.0, "stag": (0.0, 0.0, 0.0),
     "cy": 0.83e-3 * 1.1, "gather": 1.4, "hop": 0.15, "net": 1.3, "row": 0.045, "pe": 0.5e-3, "fix": 0.01, "mb": 4.5,
 }
-P.update({"mb": 1.8, "MV": ((0, 4), (2, 4)), "AB": ((1, 4), (3, 4)), "PO": (0, 2, 1, 3), "K": ((("S", 52), ("V", 12)),) * 3,
-          "K0": ((("S", 32), ("V", 32)), (("S", 64),), (("S", 64),)), "nr": "V", "E": ((("S", 36), ("V", 28)),) * 3})
+P.update({"mb": 1.8, "MV": ((0, 4), (2, 4)), "AB": ((1, 4), (3, 4)), "PO": (0, 2, 1, 3), "K": ((("S", 28), ("S", 28), ("V", 8)),) * 3,
+          "K0": ((("S", 32), ("V", 32)), (("S", 64),), (("S", 64),)), "nr": "V", "peng": 16, "E": ((("S", 38), ("V", 26)),) * 3})
 
 BF, F3, I3, U1, H1 = "bfloat16", "float32", "int32", "uint16", "float16"
 SCRATCH = {
-    "key_s": ("sbuf", [128, 4128], BF), "em_s": ("sbuf", [128, 4096], BF), "cl_s": ("sbuf", [128, 2064], I3),
+    "key_s": ("sbuf", [128, 4128], BF), "em_s": ("sbuf", [128, 8192], BF), "cl_s": ("sbuf", [128, 2064], I3),
     "pl_s": ("sbuf", [128, 192], I3), "emb_s": ("sbuf", [128, 16], BF), "w_s": ("sbuf", [128, 1], BF), "th_s": ("sbuf", [128, 1], F3),
     "pin": ("sbuf", [128, 6 * 192], U1), "phin": ("sbuf", [128, 6 * 192], H1), "qin": ("sbuf", [128, 7 * 192], BF),
     "pout": ("sbuf", [128, 6 * 192], U1), "pw": ("sbuf", [128, 6 * 192], U1),
     "qout": ("sbuf", [128, 6 * 192], BF),
     "yp_s": ("sbuf", [128, 192], F3), "ypo": ("sbuf", [128, 192], F3), "yt_s": ("sbuf", [128, 384], F3),
-    "wk": ("sbuf", [128, 144], BF), "w2": ("sbuf", [128, 144], BF),
+    "sm": ("sbuf", [128, 1024], BF), "wk": ("sbuf", [128, 144], BF), "w2": ("sbuf", [128, 144], BF),
     "tw": ("sbuf", [128, 32], BF), "bdc": ("sbuf", [128, 8], F3),
     "rep": ("sbuf", [128, 112], U1), "repi": ("sbuf", [128, 64], I3), "repj": ("sbuf", [128, 64], I3), "repk": ("sbuf", [128, 112], I3),
     "rst": ("sbuf", [128, 128], F3), "seg": ("sbuf", [128, 64], F3), "rowm": ("sbuf", [128, 64], F3), "r2": ("sbuf", [128, 128], F3),
     "pst0": ("psum", [128, 512], F3), "pst1": ("psum", [128, 512], F3),
 }
-for _n in ("ones", "bd", "idm", "ltm", "gw0", "gw", "sg", "nbd", "bd4k", "i8k", "ihf", "bdw", "eb0", "eb", "chc", "shm", "dfm", "nid", "offd", "c78"):
+for _n in ("ones", "bd", "idm", "ltm", "gw0", "gw", "sg", "nbd", "bd4k", "i8k", "ihf", "bdw", "eb0", "eb", "shm", "dfm", "nid", "offd"):
     SCRATCH[_n] = ("sbuf", [128, 128], BF)
 for _n in ("bdh", "idh", "in2k", "dm"):
     SCRATCH[_n] = ("sbuf", [128, 128], H1)
@@ -44,18 +44,18 @@ for _n in ("cu", "cq"):
     SCRATCH[_n] = ("sbuf", [128, 64], BF)
 for _n in ("icol", "kint"):
     SCRATCH[_n] = ("sbuf", [128, 1], I3)
-for _n in ("kcol", "sgcol", "thb", "k15", "k16"):
+for _n in ("kcol", "sgcol", "thb", "k15", "k16", "cic"):
     SCRATCH[_n] = ("sbuf", [128, 1], F3)
 for _c in range(NC):
     for _n, _w, _d in (("kg", 1024, BF), ("mx", 1024, BF), ("eg", 1024, BF), ("nr", 64, BF), ("ar", 64, F3),
-                       ("xx", 64, H1), ("hn", 64, H1), ("sc", 128, F3), ("ci", 128, U1), ("pi", 64, I3) if not P["u16"] else ("pu", 64, F3), ("wf", 64, BF), ("s1", 64, I3), ("s2", 64, I3), ("s3", 64, I3),
+                       ("xx", 64, H1), ("hn", 64, H1), ("sc", 128, F3), ("ci", 128, U1), ("pu", 64, F3), ("pv", 64, U1), ("wf", 64, BF), ("s1", 64, I3), ("s3", 64, I3),
                        ("vt", 64, F3), ("rs", 64, H1), ("rt", 64, H1) if not P["rev"] else ("zt", 64, BF), ("zz", 64, BF)):
         SCRATCH["%s%d" % (_n, _c)] = ("sbuf", [128, _w], _d)
     SCRATCH["psd%d" % _c] = ("psum", [128, 512], F3)
     SCRATCH["psx%d" % _c] = ("psum", [128, 512], F3)
 
 SEMAPHORES = (["sV", "sS", "sP", "sG", "lsem", "outs"]
-              + ["ld_" + n for n in ("keya", "keyb", "em", "cl", "pl", "q", "emb", "w", "th", "kp", "cp")]
+              + ["ld_" + n for n in ("keya", "keyb", "em", "em2", "cl", "pl", "q", "emb", "w", "th", "kp", "cp")]
               + ["a%s%d_%d" % (k, c, t) for k in "pq" for c in range(NC) for t in range(1, STEPS + 1)])
 
 
@@ -110,7 +110,10 @@ def plan(ops):
 
 
 PLANS = {}
-ORDER = ["010204051b1c1e1f1h1k1l0300090g0e0l0r0o0w0y11181o0b0d0i0m0z06070n140v1m1v0p1z0s0q0t0x161d0j120h2810131g19080c0f1t200k151a0u1w0a1y2j2m2l2h2c2d2e2b2617212p3c1i1j1p241q221u1x271r1s29232f2v252g2k2n2q2t2w2u2y3a34373h3n3q3y3z40424a4i4n4l4q4u4y525556571n2a322s302r2x312o2z35393e3w333b3g3i3o3s3x3v414943484b4d4j4r4v4w4m4o5158595a5j5p5r5x6g60612i363r383p3d3f3l3k3m3u3j3t4g444546474c4e4h4f4k4s4p4t4x535b5h5m5n5d5e5o5u66656c6e6i6o786u6v4z50545c5v5q5y5g5s5z5f5t625w676m686a6b6d6h6j6n636k6p6r6s6x74757d7h7k7i7j7u85888a8e8h8l8o8w8z905l5k5i646y70766l6t716f6w73727e7v77797b7c7n7r7z7s7x8081868d8f8p8s8x8y8t8u94999e9f9i9n9p9vaca0a1696q836z7q7o7y7a7l7p7g7m7w7f7t8c828487898g8j8m8k8n928q919395989g9k9l9b9c9m9ua3a2aaadafakb4aoap8b8i968r9q9j9x979a9w8v9d9y9sa5aj9ra6a8a9aeagala4ahamaqaraub0b6babdbfbebhbsc1c7c5cbceciclcnd7cocp9h9o9t9zayawb1aiasaxabatazb2bbbob3b5b7b9bgbmbxbnbtbvbyc3c9cdcqcscwcxctcud1d6dcdbdidndpdseberdwdxa7anc8avbkbpbub8bibqbjblbrbcbwc6bzc0c2c4cccfcjchckczcmcyd0d3d5dgdldmdadfdkdrdzdye5eaedegexf8elemcacgd2crdddodtd4d8dvcvd9e0dee2eidue3e6e8eceeeje7efekeoepeteyf1f6f9fbfdfafug5gbgcgeghglgph5gwgxdhdjdqe1euezf2eheqewe9esf5f0fcfvf3f4fefffnfqfwfsfxg0g1g6gdgggogsgygzgtguh2h7hbhchhhnhphuichyhze4eng3evfmfpfyf7flfrfjfoftfifzgag2g4g7g8gfgigmgkgnh1gqh0h3h4h8hghkhlhdhfhmhti1i0i9idifilivirisg9gjh9grhqhohvh6hahxgvhei2hri5ijhwi6i8iaieigiki3ihimioipiuj1j6jajdjfjejjjtk1k6k4kbkekikll3ldkokphihjhsi4izixj3iiiqiyibitj0j2jbjpj4j5j7j9jhjmjqjnjujwjyk2k7kdknkukykzkrksl0l6l9lalflllnlsmdmklwlxi7ink0iwjljojvj8jcjxjijkjrjgjsk9jzk3k5k8kckgkjkhkkkwkmkvkxl1l5leljlkl7lclilrlzlym6mamcmgmyn5mmmnkakfl2kqlolmltl4l8lvktlbm0lpm3mhlum4m7m8mbmemlm2mfmpmqmrn3n8nenjoaofognunwocoloropouoxp0papcpjpdpelglhlqm1mumwn6mimomtm9msmxn0n4nomzn2n7n9ngnlnrnnnvo3nyo2o5o7odomotp3p5p6ohoioqowp1p2pbpgpkpopqpuprpsm5mjo4mvnkninpn1nfnmncnhnsndnqo1ntnxnzo0o6o8obo9oeonojokooosovp4p8p9phpioyozp7pfpmplpnppptpvpwpzpxpyfgfhfknanbq2q1q0q3q4"]
+ORDER = ["020304051b1d1f1g1i3i3j3k01000d0n0b0i0q080z1510162g0a0c0h0l1106070u0y0r0x1p0o1v191z0p0w13180f1l0j0s1c0m0t0k171n0e1h1o0g0v14091x282j2m24252e262l1e121a2p391k1j1q1w1r201t1u231s1y27212b2h222a2d2f2k2n2u2q2t2w2v303b3f3l3o3m3n41494c4d4f4k4q4u534x4y1m2i31292r2s2y322o2z362x383e33373a3c3h3q3p3w40433z42464b4g4m4n4h4p4w5557585d5h5j5n665s5t2c353u343x3d3r3y3g3s443t454j3v47484a4e4i4l4o4r504s4v52565a5e5f5b5i5r6064656a6d6i6n6z6q6r4t514z545c5m5u5w5g5l5x595p5v5q686f5y6263676c6g6p616l6t706s6x777a7f7g7b7j7u84898a8d8j8o8s908w8x5k5z5o6h6b6y6o726m6v716k6w736u787e7476797c7h7k7l7n7t7y7s80868c8h8m8n8f8l8v929596999d9h9ka59q9r696j6e82757x7p7v7d7m7r7i7o7w7q7z8g818385878b8e8i8k8q8r8p8u8y979c9f9g919e9p9ya2a3a8abaeakaxapaq888t8z9a949l9s9u989i9o939j9t9na1aa9w9xa0a4a9adam9zaiaoauanasb3b7bcbdb8bgbsc1c6c7cbcgclcpcxdectcu9v9b9mafa6awalayajatazaharb2avb5bbb0b4b6b9bebhbiblbrbvbqbxc2c9cecjckcacicsczd3d4d6d9dddhe3e8dodpa7agacbzb1bpbmbubabjbobfbkbtbnbwcdbyc0c3c5c8cccfchcncocmcrcvd0d7dadccydbdndwe1e0e5eaefekf0fiepeqcqc4cwd8d2dkdjdqd5dgdmd1didrdle2e9dudvdydze6ebejdxegenewemetf3f6fbfcf7fffpg4gag9gdgjgogth0gwgxdsdfdtece4euelezeheoeyeeesf2erevfaexf4f5f8fdfgfhfrfvg0fufzg8gcghgmgngeglgvh2h5h7hahfhhhki6hqhreie7edg5f1fxfkfsf9fjfqfefmftfwg2ggfyg1g3g7gbgfgigkgpgrgqgugyh3h8hbhdh1hghphyi2i3i8icifilitiniogsg6gzhch6hnhshuh9hjhoh4hihthmi1ibhwhxi0i4i9iaihhzijiqixipivj4j7jcjdj8jgjsk1k6k7kakgklkpl3lbktkuhehvhligi7isimiziiiriyikiuj0iwj5jbj1j3j6j9jejijhjkjrjvjqjxk3k9kekjkkkckikskyl1l2l7ldlflgm3m7lnloi5ieidjzj2jojmjtjajjjpjfjljujnjwkdjyk0k2k4k8kbkfkhknkokmkrkvkzl4l8lakxlelmlwlzm0m5mamdmimxn5mnmokqk5kwl9l0lhlplql6lilrl5lklslllum4ltlxlym1m6mcmlm2mgmqmvmmmsn2ngoootoun7n8nso1o5o6oaoeoioqovp1owoxlclvljmem8mrmkmwmhmpmymfmun1mtn4ncmzn3n6n9nfnhninknrnvnqnzo2o9opozp5p8p9o7ogomoyp0p2p6papcplpnprpoppm9mjmbnyn0nlnnntndnjnpnenmnunonwocnxo0o3o4o8obodofojolohokonp3p7pbpepgpiorosp4pdpfphpkpmpqpsptpwpupvflfnfonanbpypxpjpzq0"]
+C6 = ["020304051c1e1g1h1j3g3h3i01000d0m0b0g0r08101611172j0a0c0j0n1206070v0z0s0y1q0p1w1a1z0q0x14190f1m0k0t1d0o0u0l181o0e0h1i1p0i0w15091y292n2l25262f272p1f131b2x3c1l1k1v211s201r1t241u1x28222c2k232b2e2g2i2m2t2r2w302u2y32393f3m3o3n3p424a4e4h4k4o4t4y5752541n2h332a2s2o31372q2v382z3b3q343a3d3e3l3r3s3w41444043464b4g4l4p4q4j4s4z585d5c5g5m5o5t6d5y5z2d363v353y3k3u3z3j3t453x474f48494c4d4i4m4n4r4u514v4x50565a5e5h5j5k5n5w656b6c6g6k6q6v7i7071554w535i5f5r5v605b5p5u5l5q5x5s686l6264676a6f6j6o636n6u6x6r6w75797n7q7r7e7f808a8e8g8j8n8q8w9793945961667b6e726p6y6m6z766s6t7a737d7m747c7g7h7l7o7s7u7z857y84898d8k8p8t8u8h8r92989d9c9g9k9o9tac9y9z696i6h78777x7v817j7w827k7t837p878f86888b8c8i8l8m8o8s8y8v8x95969e9i9m9n999l9wa4abadagalaqatbnazb0918z909h9b9r9va09a9p9u9f9q9x9sa8aka2a3a6aaafajama5aoavb1arawb3b7bmbrbsbfbec0cacfcechclcscvd7dlczd0a19ja7b6aeb2apaxanayb5asaub8b9bdbkbabcbgbhblbobqbubzc2byc4c9cdcgckcqcrctcmd4d9dedddhdndpduedf0dze0aia9ahbbb4bxbvc7bibwc1bjbtc3bpc6coc5c8cbcccjcncpcucyd2cxd1d5d6dbdfdidkd8dodxe5ebecehelerewfnfvf2f3d3cicwdjdcdsdwe1dadqdvdgdrdydte8eme3e4e7eaegekeneeepeveyesexf5fafofsftfjfcg7gggmgkgqgugzh3hdh7h8dme2e6f9eff4eqezeof1f7eteuf8fdfifpfefffgfhfmfqfwfxg5gag3gcgfgjgpgtgxgygngwh5hehkhjhnhshuhziii3i4eje9eifbf6fufzg9fkfrg0flfyg8g1gbglgdgeghgigogrgsgvh1h6h2h4hahchghlhohqhfhti2iaigihimiqiuizjpj5j6h9h0hbhphmhyi1i6hhhwi0hihxi5hvidiri8i9icieilioiwijitj1j7ixj2j9jdjtjwjxjljkk6kgkmklkqkukzl3ldlsl8l9hri7ibjhikj8ivj3isj4jbiyj0jejfjjjsjgjijmjnjqjujvjzk4kbk5kakfkjkpktkxkykokwl6leljlkloltlvm0mmn6m5m6ipifinjcjak3k1k8jok0k7jrjyk9k2kckkkdkekhkiknkrkskvl1l7l2l4lblclglmlplrlflum3mbmimjmnmtmxn2nrnwn8n9lal0l5lqlilym2m7lhlwm1lnlxm4lzmemom9mamdmgmlmrmwmhmun1n4myn3nbnfnvoiooopnnnmo2ogoromouozp3p9pfpmpcpdllm8mcnjmsnamvn5mkn7ndmzn0ngnhnlntninknonpnunzo6o4obojoaoeoloqovpapephpjpkotp1p7plpqpppupyq0q3q5q9q6q7mfmqmpnencnyo5o8nqnxo3nso9odo7okoxocofohonosowoyp0p4p5p2p6p8pbpnprptpvpwpxpgpipopzq2q1q4q8qbqcqdqgqeqfg2g4g6o0o1qhqapsqiqj"]
+C5 = ["020305061f1g1h1i1m3m3o3q04010b0p000c0s0l11131j181e0a0d0e0m0r07080w0v0t141k0g1z0z170j0x161c0f1a0i0u190y120q1b1p0h0o1d1r0k0n15091x2325282b2c2d2e2h1l101s2n3b1n1o1w201t261v1y271u2229242f2p212g2k2l2m2s2x2v2z382y32363e3k3t3v3u3y484c4l4g4m4p4v4x5551521q2a2u2j2o2q2w342r30352t3a3g31393c3d3j3p3w3x41474046494a4e4o4t4u4i4q50585b5c5f5k5n5q6b5y5z2i333r373n3f3h3l3i3s453z4d4h4243444b4f4j4k4n4s4w4r4y53565a5d5h5i5e5l5v64696a6e6h6k6o7m6y6z4z5754595j5s5t5w5m5r5x5g5p60616d6r626667686i6l6w6f6p71757074797d7q7v7w7g7h7y888d8c8g8k8p8t958y8z5o63655u6g6u6q786s6v776t727a6x7b7i737c7e7f7p7t7u7z838782868b8f8n8r90918j8o8x989a9b9e9i9n9pa99q9r6m6n6j6c767n7r807k7l7s7j7o7x818e8h8485898a8i8l8m8q8w938v9296999c9h9l9m9d9j9va4aaabaeaiamaublb0b1948s8u979g9t9w9x9k9u9z9f9sa0a1afaoa2a5a7a8agakaxadatazb5ayb3b9bcbobvbwbgbhbxc9cdccchcjcocxd7dhd1d29oa3a69yahb4alavapawb7aqb2bbasbabib6bdbebfbnbrbsbyc2c8c1c6cbcfckcrcsctcicqd0d9dbdcdldndpdqeaeedudvaranajacb8btbpbzbkbmbqbjbuc0c3cecmc4c5c7cacgclcncpcvd4cucyd3d8dadedidjdgdodxe5ebecegemeperfkfuf2f3d6cwczd5dfdwdsdydkdte0dddre3e1edeue2e7e8e9eleoexejeqf1f6ezf5fbfgfqfxfyfmfng0gegkgjgogsgvh2hdhahbdme4e6dzekf0evfeesewf8etf4fceyf7fifafdfffhfpfrg6ftg8gfg7g9gigmgph3h6h7gqgwh5hfhghhhlhohthvihi1i2efeheneif9fwfsg4flfofvfjg1g5gaghglgbgcgdgggngrgtgugygzgxh4h8hehjhnhrhshihqi3iaieidilioirivjtjbjch0h1hch9hmhzhyi4hpi0i5hkhwi7i9ikixi6icifigimiqj0ijiuj2j9j1j8jgjjjojujvjpjrk4kekjkikokrkvl2lclpl8l9hui8ibhxinj6iwjhiyizjdj3j4jfj5jajmj7jijkjljyk1k3k5k8kdk7kckhklktl1l6l7kpkwl5lflhlilmlslvlwmgmnm6m7isitipiijejwjzk6jqjsk0jnjxk2k9kkknkakbkfkgkmkqkskukyl0kxl3laldlglklqlrljlum1mcmhmimlmpmsmwnxo4n2n3lbkzl4lelolzlxm2ltm0m3lllym5m8mmmxm9mbmemfmqmtn5mkn0n7nen6nanhnlnoohooopnpnvo6ocomojosovp3pbpepkpfpglnmamdm4monbn1ncmyn4ngmzn8njn9ninrndnknmnnnunzo0o3oboloaodonotp6papjpppsptoyp0p7phplpmpqpupxq2q4q8q5q6mumvmrmjnfnyo2o9nqnto1nsnwo5oeorowofogoiokoqouoxozp2p5p1p4p8p9pipnprpwpypzpcpdpopvq0q1q3q7qaqbqdqgqeqffzg2g3o7o8qhqcq9qiqj"]
+BEST3 = ["010204051b1c1e1f1h1k1l0300090g0e0l0r0o0w0y11181o0b0d0i0m0z06070n140v1m1v0p1z0s0q0t0x161d0j120h2810131g19080c0f1t200k151a0u1w0a1y2j2m2l2h2c2d2e2b2617212p3c1i1j1p241q221u1x271r1s29232f2v252g2k2n2q2t2w2u2y3a34373h3n3q3y3z40424a4i4n4l4q4u4y525556571n2a322s302r2x312o2z35393e3w333b3g3i3o3s3x3v414943484b4d4j4r4v4w4m4o5158595a5j5p5r5x6g60612i363r383p3d3f3l3k3m3u3j3t4g444546474c4e4h4f4k4s4p4t4x535b5h5m5n5d5e5o5u66656c6e6i6o786u6v4z50545c5v5q5y5g5s5z5f5t625w676m686a6b6d6h6j6n636k6p6r6s6x74757d7h7k7i7j7u85888a8e8h8l8o8w8z905l5k5i646y70766l6t716f6w73727e7v77797b7c7n7r7z7s7x8081868d8f8p8s8x8y8t8u94999e9f9i9n9p9vaca0a1696q836z7q7o7y7a7l7p7g7m7w7f7t8c828487898g8j8m8k8n928q919395989g9k9l9b9c9m9ua3a2aaadafakb4aoap8b8i968r9q9j9x979a9w8v9d9y9sa5aj9ra6a8a9aeagala4ahamaqaraub0b6babdbfbebhbsc1c7c5cbceciclcnd7cocp9h9o9t9zayawb1aiasaxabatazb2bbbob3b5b7b9bgbmbxbnbtbvbyc3c9cdcqcscwcxctcud1d6dcdbdidndpdseberdwdxa7anc8avbkbpbub8bibqbjblbrbcbwc6bzc0c2c4cccfcjchckczcmcyd0d3d5dgdldmdadfdkdrdzdye5eaedegexf8elemcacgd2crdddodtd4d8dvcvd9e0dee2eidue3e6e8eceeeje7efekeoepeteyf1f6f9fbfdfafug5gbgcgeghglgph5gwgxdhdjdqe1euezf2eheqewe9esf5f0fcfvf3f4fefffnfqfwfsfxg0g1g6gdgggogsgygzgtguh2h7hbhchhhnhphuichyhze4eng3evfmfpfyf7flfrfjfoftfifzgag2g4g7g8gfgigmgkgnh1gqh0h3h4h8hghkhlhdhfhmhti1i0i9idifilivirisg9gjh9grhqhohvh6hahxgvhei2hri5ijhwi6i8iaieigiki3ihimioipiuj1j6jajdjfjejjjtk1k6k4kbkekikll3ldkokphihjhsi4izixj3iiiqiyibitj0j2jbjpj4j5j7j9jhjmjqjnjujwjyk2k7kdknkukykzkrksl0l6l9lalflllnlsmdmklwlxi7ink0iwjljojvj8jcjxjijkjrjgjsk9jzk3k5k8kckgkjkhkkkwkmkvkxl1l5leljlkl7lclilrlzlym6mamcmgmyn5mmmnkakfl2kqlolmltl4l8lvktlbm0lpm3mhlum4m7m8mbmemlm2mfmpmqmrn3n8nenjoaofognunwocoloropouoxp0papcpjpdpelglhlqm1mumwn6mimomtm9msmxn0n4nomzn2n7n9ngnlnrnnnvo3nyo2o5o7odomotp3p5p6ohoioqowp1p2pbpgpkpopqpuprpsm5mjo4mvnkninpn1nfnmncnhnsndnqo1ntnxnzo0o6o8obo9oeonojokooosovp4p8p9phpioyozp7pfpmplpnppptpvpwpzpxpyfgfhfknanbq2q1q0q3q4"]
 OLD = ["020304051a1d1f1h1i2d2f2h0100070e0b0j100v0p1317191q08090m0t1m0l0d140o0s150q1v180x1j1g161b0i0n0h0y0z1e1k1l060a0c2s2v0f0k0r0u1c0g24232k2e2a28292b20120w112w341o1n1r1w1s1t1x1u1y212o2u361z222c2i2l2y3d2z31333g3j3q3t40434749484c4l4n4q4t515355586f5a5b1p262p252g2m2j2n2r35373n2q2t38393c3l3s3m3p3r3u3w41454e4g4s4w4y4j4k4p5254575c5e5h5k6l5p5q27303f2x323e3a3b3i3x3z463h3k3o3v3y424b444a4h4d4f4i4m4o4r4u4z504v4x595d5f5j5m5o5s5u7n5z6056645n5v5r5x625i5t6a6m6o6w5y696b6g6i6s6z6t6u6y74777b7h7m7t7v7w7x81888e8i8l8o8p8q8u938y8z5g63616j67666d65686e707a7g6n6p6r6v727c7k7d7f7j7l7q7u7z84878d8g8h8a8b8k8r8t8x9295989bak9c9d5w5l6c716k6q6x6h73767r7s7y7578797e7i7o827p80868385898c8f8j8w90918m8n8v94979a9e9g9i9ka29p9q8s9h9f9s9m9r9u999ja19la5aa9t9ya0acaeaiasajamawavb0b4b6b9bebibkbjbtbxc4c8cbcfciclcpcudscrcs969x9n9w9za3a69va7abatazbbadahalaqaub1bdb2b7babgbmbpbrbvbyc3c6c7c0c1cacjcmcnctcwczd2dwdzd5d69oa8a4axa9aganafaoaparbfbnayb3b5b8bcbhboblbqbubsbwbzc2c5c9cecgchcccdcocvcyd1d3d7d9dce8eidfdgckcqd4didddhdkd0dadoe2e5eadjdldrdudye3ele4ebecenerevf4f9fefifjfkflfvg2g4g7gbgfgigkgqgngocxd8dedtdqdne0dmdpdvefetf3e6e9egehekeyf7f0f2f6f8fcfhfpfrfufwg0g1fyfzg6geghgjgpgsgvgyhhgzh0dbemdxeoe1e7edeeejepfdfgfmeqeseuf1f5fafnfbfffsfofqftfxg3g5gagcgdg8g9glgrgugxh1h3h5h7iwh8h9gggmgwhihahdhgh2h6hchkhxi8hjhmhnhphsi2idi3i5iaieihilioixj1j6j8j7jcjjjrjvjyk1k5k7k8ljllkbkcgth4hbhqhlhohthfhrhvhzi7iuhuhwibicifiniyiqiritizj4jbjfjijljqjtjujnjojxk6kakdkekkkokrlalxkukvhehyi4iii0i9i6i1igikj0j5jaijimipisivj2jdj3j9jhjejgjkjmjpjsk0k2k3jwjzk9kgkjklknkqktkxlclnl1l2k4khkil6l3kzl5kpkyl9lslzmcl7l8lblglmlymdm0m4m6memhmkmomun0njnmnnn4n5nentnwo0o8odogojooosopoqkfkml0lrlflelhl4lilom8mampltlwm1m7mbmjmsmlmnmrmtmyn3n8nandnsnvo1o4o5ngnlnrnzo3o6o7oboeohokowolomkwksldm9lplvm5lklqlumvmzn2mfmgmimmmqmwn6mxn1nbn7n9ncnfnhnkninpnunxnynonqo2o9oaocofoionorotouoxoyexezewm2m3p1ovp0ozp2"]
 
 
@@ -174,7 +177,7 @@ def build(g, core, T, topo):
     cur = [0, -1]
     seen = {}
     lastld = {}
-    na, nb = (1.0, 0.0) if P["nr"] == "V" else (0.5, 0.5)
+    na, nb = (1.0 / 4096, 0.0) if P["nr"] == "V" else (0.5, 0.5)
     za, zb = (1.0, 0.0) if P["z"] == "V" else (0.5, 0.5)
     MV, AB = P["MV"], P["AB"]
     vslots = sorted(i for s, n in MV for i in range(s, NS, n))
@@ -254,7 +257,9 @@ def build(g, core, T, topo):
     load("Y", T.th_s[:], T.th[:], "th", "th", 2.0)
     load("Y", T.cl_s[:, 8:2056], T.cl[:], "cl", "cl", 1.5 + 2 * mb)
     load("Y", T.emb_s[:], T.emb[:], "emb", "emb", 2.0)
-    load("Y", T.em_s[:], T.em[:], "em", "em", 1.5 + 2 * mb, ("keyb",))
+    load("Y", T.em_s[:, 0:4096], T.em[:], "em", "em", 1.5 + 2 * mb, ("keyb",))
+    if P["dbl"]:
+        load("Y", T.em_s[:, 4096:8192], T.em[:], "em2", "em2", 1.5 + mb, ("em", "cl"))
     if rank == 0:
         load("Y", T.key_s[:, 4112:4128], T.key[:, 0:16], "kp", "kp", 2.0)
         load("Y", T.cl_s[:, 2056:2064], T.cl[:, 0:8], "cp", "cp", 2.0)
@@ -296,7 +301,7 @@ def build(g, core, T, topo):
     vts(T.in2k[:], T.idm[:], -2048.0, None, A.mult, None, ("idm",), ("in2k",))
     sact(T.i8k[:], T.idm[:], F.Copy, ("idm",), ("i8k",), None, 128, scale=8192.0 * na)
     sact(T.bd4k[:], T.bd[:], F.Copy, ("bd",), ("bd4k",), None, 128, scale=4096.0 * na)
-    if na != 1.0:
+    if nb:
         vts(T.thb[:], T.th_s[:], -0.5, None, A.add, None, ("th",), ("thb",))
     vtt(T.gw0[:], T.idm[:], T.ltm[:], A.subtract, ("idm", "ltm"), ("gw0",), 256)
     sact(T.gw[:], T.gw0[:], F.Copy, ("gw0",), ("gw",), None, 128, scale=4096.0 * na)
@@ -307,22 +312,35 @@ def build(g, core, T, topo):
     vts(T.bdh[:], T.bd[:], 0.5, None, A.mult, None, ("bd",), ("bdh",))
     k0 = 18432.0 + 2048.0 * 104 * nb
     k1 = (3145728.0 if P["sf16"] else 0.0) + 65536.0 * nb
-    vts(T.seg[:], T.rowm[:], T.kcol[:, 0:1], MK, A.not_equal, A.mult, ("rowm", "kcol"), ("seg",))
-    vts(T.chc[:, 0:128:2], T.seg[:], k0, None, A.add, None, ("seg",), ("chc0",))
-    vts(T.chc[:, 1:128:2], T.seg[:], k1, None, A.add, None, ("seg",), ("chc1",))
-    vfill(T.rst[:], 0.0, (), ("rst",), 128)
-    vfill(T.rst[:, 0:128:32], 4194304.0, (), ("rst",))
-    vfill(T.rst[:, 31:128:32], -0.25, (), ("rst",))
-    if rank == N - 1:
-        vts(T.r2[:], T.rst[:], 0.0, None, A.max, None, ("rst",), ("r2",), 128)
-        vfill(T.r2[:, 31:128:32], 0.25, (), ("r2",))
-        vfill(T.c78[:], 7.0, (), ("c78",))
-        vfill(T.c78[:, 1:128:2], 8.0, (), ("c78",))
+    ta, tb = T.sc0[:, 0:64], T.sc0[:, 64:128]
+    if P["sc4"]:
+        vts(T.seg[:], T.rowm[:], 1.0, T.kcol[:, 0:1], A.add, A.is_equal, ("rowm", "kcol"), ("seg",))
+        vts(ta, T.seg[:], 8388608.0, None, A.mult, None, ("seg",), ("ta",))
+        vts(tb, T.rowm[:], T.kcol[:, 0:1], -4096.0, A.is_equal, A.mult, ("rowm", "kcol"), ("tb",))
+        vtt(T.rst[:, 1:128:2], ta, tb, A.add, ("ta", "tb", "sc0"), ("rsa",), 128)
+        vts(T.rst[:, 31:32], T.rst[:, 31:32], k1 + 4096.0, None, A.add, None, (), ("rsa",))
+        vts(T.rst[:, 0:128:2], T.rowm[:], T.kcol[:, 0:1], k0 - k1 - 0.25, A.is_equal, A.mult, ("rowm", "kcol"), ("rsb",))
+        if rank == N - 1:
+            vcp(T.r2[:, 1:128:2], T.rst[:, 1:128:2], ("rsa",), ("r2a",))
+            vts(T.r2[:, 31:32], T.r2[:, 31:32], 8.0, None, A.add, None, (), ("r2a",))
+            vts(T.r2[:, 0:128:2], T.rowm[:], T.kcol[:, 0:1], k0 - k1 - 0.75, A.is_equal, A.mult, ("rowm", "kcol"), ("r2b",))
+    else:
+        vts(T.seg[:], T.rowm[:], -1.0, T.kcol[:, 0:1], A.add, A.is_equal, ("rowm", "kcol"), ("seg",))
+        vts(ta, T.seg[:], -4096.0, None, A.mult, None, ("seg",), ("ta",))
+        vts(tb, T.rowm[:], T.kcol[:, 0:1], 8388608.0, A.is_equal, A.mult, ("rowm", "kcol"), ("tb",))
+        vtt(T.rst[:, 0:128:2], ta, tb, A.add, ("ta", "tb", "sc0"), ("rsa",), 128)
+        vts(T.rst[:, 1:128:2], T.rowm[:], T.kcol[:, 0:1], k0 - k1 - 0.25, A.is_equal, A.mult, ("rowm", "kcol"), ("rsb",))
+        vts(T.cic[:], T.kcol[:], 15.0, 4096.0, A.is_lt, A.mult, ("kcol",), ("cic",))
+        vts(T.cic[:], T.cic[:], BIG + k1, None, A.add, None, (), ("cic",))
+        if rank == N - 1:
+            vcp(T.r2[:, 0:128:2], T.rst[:, 0:128:2], ("rsa",), ("r2a",))
+            vts(T.r2[:, 1:128:2], T.rowm[:], T.kcol[:, 0:1], k0 - k1 - 0.75, A.is_equal, A.mult, ("rowm", "kcol"), ("r2b",))
     vfill(T.seg[:], 4096.0, (), ("seg",))
     vfill(T.seg[:, 0:64:16], -4096.0, (), ("seg",))
+    if any(P["VS"]):
+        vfill(T.sm[:], 1.0, (), ("sm",), 512)
+        vfill(T.sm[:, 0:1024:16], 0.0, (), ("sm",))
     vts(T.k15[:], T.kcol[:], 15.0, None, A.is_equal, None, ("kcol",), ("k15",))
-    vts(T.dfm[:], T.bd[:], T.k15[:, 0:1], None, A.mult, None, ("bd", "k15"), ("dfm",))
-    vtt(T.dm[:], T.dfm[:], T.idm[:], A.subtract, ("dfm", "idm"), ("dm",), 256)
     sact(T.ihf[:], T.idm[:], F.Copy, ("idm",), ("ihf",), None, 128, scale=0.5)
     vcp(T.bdc[:], T.bd[:, 0:128:16], ("bd",), ("bdc",))
     vfill(T.tw[:], 0.0, (), ("tw",))
@@ -422,30 +440,32 @@ def build(g, core, T, topo):
                 pieces.append((a, s + n * j, n * u, "%s_%d" % (k("ab"), a)))
                 sact(mx[:, a:a + w // u], df[:, j:w:u], F.Abs, (), (pieces[-1][3],), bf, w // u, scale=0.5)
                 a += w // u
+        HA = C1 if P["ha"] else HA
         mms([(HA, T.bdw[:], qin, True, True)], ("bdw", qkey), bx)
         sact(B("hn")[:], HA, F.Identity, (), (k("hn"),), bx, bias=1536.0 - 1023.5 / 2048.0, scale=1.0 / 2048.0)
-        mms([(CH, T.idm[:], T.chc[:], True, False), (C1, T.bdw[:], qin, False, False), (C1, T.in2k[:], B("hn")[:], False, False)]
-            + ([(CH, T.idm[:], T.c78[:], False, False) if P["sc4"] else (C1, T.idm[:], one64, False, False)] if down else []),
-            ("idm", "in2k", "chc0", "chc1", "c78", k("hn")), bx, (), 4)
+        mms(([] if P["ha"] else [(C1, T.bdw[:], qin, True, False)]) + [(C1, T.in2k[:], B("hn")[:], False, False)], ("in2k", k("hn")), bx)
         po = P["PO"] or range(len(pieces))
         for j in po:
             a, s, n, nm = pieces[j]
             mms([(D, T.w2[:, 16 - s - n * r:144 - s - n * r], mx[:, a + r:a + 1024 // n:16 // n], not MV and j == po[0] and r == 0,
                   j == po[-1] and r == 16 // n - 1) for r in range(16 // n)], (nm, "w2"), bd)
-        if na == 1.0:
-            vts(nr, D, T.th_s[:, 0:1], None, A.is_lt, None, ("th",), (k("nr"),), 64, bd)
+        if not nb:
+            vts(nr, D, T.th_s[:, 0:1], 1.0 / na, A.is_lt, A.mult, ("th",), (k("nr"),), 64, bd)
         else:
             sact(nr, D, F.Sign, ("thb",), (k("nr"),), bd, bias=T.thb[:, 0:1], scale=-1.0)
         mms([(U, T.idm[:], T.cu[:], True, False), (U, T.gw[:], nr, False, True)], ("idm", "cu", "gw", k("nr")), bd)
-        mms([(C1, T.bd4k[:], nr, False, False), (C0, T.sg[:], nr, False, False)], ("bd4k", "sg", k("nr")), bx)
+        mms([(C1, T.bd4k[:], nr, False, True), (C0, T.sg[:], nr, True, False)], ("bd4k", "sg", k("nr")), bx)
         sab = P["u16"] == 3
         wrap = []
         if sab and (up or down):
             vts(B("wf")[:], T.pin[:, o0:o0 + NL], 4096.0 if up else 15.0, (-0.5 if up else 0.5) / na, A.is_equal, A.mult, (pkey,), (k("wf"),))
             wrap = [(AR, T.i8k[:], B("wf")[:], False, False)]
+        if P["arl"]:
+            vtt(B("xx")[:], U, ph, A.min, (hkey,), (k("xx"),), 64, bd)
         mms([(AR, T.idh[:], ph, True, False)] + wrap + [(AR, T.i8k[:], nr, False, True)], ("idh", "i8k", k("nr"), hkey, k("wf")), bd)
-        vtt(B("xx")[:], U, ph, A.min, (hkey,), (k("xx"),), 64, bd)
-        if sab:
+        if not P["arl"]:
+            vtt(B("xx")[:], U, ph, A.min, (hkey,), (k("xx"),), 64, bd)
+        if sab and not P["dbl"]:
             sact(B("ar")[:], AR, F.Identity, (), (k("ar"),), bd, bias=8192.0 * (1 - nb) - (2047.0 if down else 2048.0), scale=-1.0)
         else:
             sact(B("ar")[:], AR, F.Identity, (), (k("ar"),), bd, bias=8192.0 * nb - (2049.0 if down else 2048.0))
@@ -454,22 +474,24 @@ def build(g, core, T, topo):
             def four():
                 r = None
                 for h in range(4):
-                    r = V.tensor_tensor_scan(B("ci")[:, h:128:4], (T.r2 if down else T.rst)[:, 0:32], psx[:, 32 * h:32 * h + 32], 0.0, A.add, A.min)
+                    r = V.tensor_tensor_scan(B("ci")[:, h:128:4], psx[:, 32 * h:32 * h + 32], (T.r2 if down else T.rst)[:, 0:32], 8388608.0, A.min, A.add)
                 return r
-            op("V", four, ("r2" if down else "rst",), (k("ci"),), bx, vd(256))
+            op("V", four, ("r2a", "r2b") if down else ("rsa", "rsb"), (k("ci"),), bx, vd(256))
             cil = B("ci")[:, 124:128]
         else:
-            scan(B("sc")[:], T.r2[:] if down else T.rst[:], CH, A.add, A.min, ("r2" if down else "rst",), (k("sc"),), 128, bx)
-            vts(B("ci")[:, 0:4], B("sc")[:, 31:128:32], BIG + (7.0 if down else 0.0), BIG, A.add, A.subtract, (k("sc"),), (k("ci"),))
+            scan(B("sc")[:], T.r2[:] if down else T.rst[:], CH, A.add, A.min, ("r2a", "r2b") if down else ("rsa", "rsb"), (k("sc"),), 128, bx)
+            vts(B("ci")[:, 0:4], B("sc")[:, 31:128:32], T.cic[:, 0:1], BIG - (8.0 if down else 0.0), A.add, A.subtract, (k("sc"), "cic"), (k("ci"),))
             cil = B("ci")[:, 0:4]
-        pf = B("pu")[:] if sab else B("pi")[:]
-        op("V", lambda: V.tensor_tensor(pf, cwin.indirect(cil), B("ar")[:], A.min if sab else A.max),
+        pf = B("pv")[:] if P["dbl"] else B("pu")[:]
+        op("V", lambda: V.tensor_tensor(pf, cwin.indirect(cil), B("ar")[:], A.max if P["dbl"] else A.min),
            ("cl", k("ci"), k("ar")) + cp, (k("pf"),), None, 0.06 + 64 * P["gather"] * CY)
         pok = "po%d_%d" % (c, t)
-        si, sik = B("s2")[:], k("s2")
         if P["u16"]:
             si, sik = T.pout[:, o0:o0 + NL], pok
-            sact(si, pf, F.Abs, (k("pf"),), (sik,))
+            if P["dbl"]:
+                vtt(si, pf, nr, A.subtract, (k("pf"), k("nr")), (sik,), 128)
+            else:
+                sact(si, pf, F.Abs, (k("pf"),), (sik,))
         else:
             vts(si, pf, 4095, None, A.bitwise_and, None, (k("pf"),), (sik,))
             vcp(T.pout[:, o0:o0 + NL], si, (sik,), (pok,))
@@ -493,13 +515,24 @@ def build(g, core, T, topo):
         egk, a = [], 0
         for e, w in P["E"][c]:
             egk.append("%s_%d" % (k("eg"), a))
-            gather(e, eg[:, 16 * a:16 * (a + w)], T.em_s[:], T.pout[:, o0 + a:o0 + a + w], ("em", pok), (egk[-1],), 16 * w, -128.0)
+            if P["dbl"] and t:
+                gather(e, eg[:, 16 * a:16 * (a + w)], T.em_s[:], B("pv")[:, a:a + w], ("em", "em2", k("pf")), (egk[-1],), 16 * w, -128.0)
+            else:
+                gather(e, eg[:, 16 * a:16 * (a + w)], T.em_s[:, 0:4096], T.pout[:, o0 + a:o0 + a + w], ("em", pok), (egk[-1],), 16 * w, -128.0)
+            if P["VS"][c]:
+                scan(B("vs")[:, 16 * a:16 * (a + w)], T.sm[:, 0:16 * w], eg[:, 16 * a:16 * (a + w)], A.mult, A.add, ("sm", egk[-1]),
+                     ("%s_%d" % (k("vs"), a),), 8 * w)
+                egk[-1] = "%s_%d" % (k("vs"), a)
             a += w
-        mms([(VO, T.idm[:], eg[:, i:1024:16], i == 0, i == NS - 1) for i in range(NS)], tuple(egk) + ("idm",), bx)
-        op("V", lambda: V.transpose(B("vt")[:], VO), (), (k("vt"),), bx, vd(64))
-        scan(B("rs")[:], T.seg[:], B("vt")[:], A.min, A.max, ("seg", k("vt")), (k("rs"),))
+        vn = "vh" if P["VS"][c] else "vt"
+        if P["VS"][c]:
+            op("V", lambda: V.transpose(B("vh")[:], B("vs")[:, 15:1024:16]), tuple(egk), (k("vt"),), None, vd(64))
+        else:
+            mms([(VO, T.idm[:], eg[:, i:1024:16], i == 0, i == NS - 1) for i in range(NS)], tuple(egk) + ("idm",), bx)
+            op("V", lambda: V.transpose(B("vt")[:], VO), (), (k("vt"),), bx, vd(64))
+        scan(B("rs")[:], T.seg[:], B(vn)[:], A.min, A.max, ("seg", k("vt")), (k("rs"),))
         if P["rev"]:
-            scan(psx[:, 319:255:-1], T.seg[:], B("vt")[:, ::-1], A.min, A.max, ("seg", k("vt")), (k("sx"),), 64, bx)
+            scan(psx[:, 319:255:-1], T.seg[:], B(vn)[:, ::-1], A.min, A.max, ("seg", k("vt")), (k("sx"),), 64, bx)
             vtt(B("zt")[:], B("rs")[:], DL, A.is_ge, (k("rs"), k("sx")), (k("zt"),), 64, bx)
             op("V", lambda: V.transpose(B("zz")[:], B("zt")[:]), (k("zt"),), (k("zz"),), None, vd(64))
         else:

import numpy as np
from concourse.bass import DstId, RemoteDMATransfer
from concourse.mybir import AluOpType, ActivationFunctionType

A = AluOpType
F = ActivationFunctionType
NL = 64
NS = 16
NC = 3
STEPS = 6
BIG = 12582912.0
MK = 16384.0
P = {
    "K": (("S", 32), ("S", 32)),
    "E": (("S", 40), ("V", 24)),
    "K0": ((("S", 32), ("V", 32)), (("S", 32), ("S", 32)), (("S", 32), ("S", 32))),
    "MV": ((0, 2),), "AB": ((1, 2),), "AS": 1, "PO": None, "u16": 3, "rev": 1, "ha": 0, "sc4": 1, "arl": 1, "dbl": 1, "VS": (0, 0, 0),
    "nr": "V", "z": "V", "ph": "send", "sf16": True, "qeng": 16, "peng": 8, "gate": True, "ka": 1536, "ca": 768,
    "look": 0.1, "seed": 0, "noise": 0.0, "stag": (0.0, 0.0, 0.0),
    "cy": 0.83e-3 * 1.1, "gather": 1.4, "hop": 0.15, "net": 1.3, "row": 0.045, "pe": 0.5e-3, "fix": 0.01, "mb": 4.5,
}
P.update({"mb": 1.8, "MV": ((0, 4), (2, 4)), "AB": ((1, 4), (3, 4)), "PO": (0, 2, 1, 3), "K": ((("S", 28), ("S", 28), ("V", 8)),) * 3,
          "K0": ((("S", 32), ("V", 32)), (("S", 64),), (("S", 64),)), "nr": "V", "peng": 16, "E": ((("S", 38), ("V", 26)),) * 3})

BF, F3, I3, U1, H1 = "bfloat16", "float32", "int32", "uint16", "float16"
SCRATCH = {
    "key_s": ("sbuf", [128, 4128], BF), "em_s": ("sbuf", [128, 8192], BF), "cl_s": ("sbuf", [128, 2064], I3),
    "pl_s": ("sbuf", [128, 192], I3), "emb_s": ("sbuf", [128, 16], BF), "w_s": ("sbuf", [128, 1], BF), "th_s": ("sbuf", [128, 1], F3),
    "pin": ("sbuf", [128, 6 * 192], U1), "phin": ("sbuf", [128, 6 * 192], H1), "qin": ("sbuf", [128, 7 * 192], BF),
    "pout": ("sbuf", [128, 6 * 192], U1), "pw": ("sbuf", [128, 6 * 192], U1),
    "qout": ("sbuf", [128, 6 * 192], BF),
    "yp_s": ("sbuf", [128, 192], F3), "ypo": ("sbuf", [128, 192], F3), "yt_s": ("sbuf", [128, 384], F3),
    "sm": ("sbuf", [128, 1024], BF), "wk": ("sbuf", [128, 144], BF), "w2": ("sbuf", [128, 144], BF),
    "tw": ("sbuf", [128, 32], BF), "bdc": ("sbuf", [128, 8], F3),
    "rep": ("sbuf", [128, 112], U1), "repi": ("sbuf", [128, 64], I3), "repj": ("sbuf", [128, 64], I3), "repk": ("sbuf", [128, 112], I3),
    "rst": ("sbuf", [128, 128], F3), "seg": ("sbuf", [128, 64], F3), "rowm": ("sbuf", [128, 64], F3), "r2": ("sbuf", [128, 128], F3),
    "pst0": ("psum", [128, 512], F3), "pst1": ("psum", [128, 512], F3),
}
for _n in ("ones", "bd", "idm", "ltm", "gw0", "gw", "sg", "nbd", "bd4k", "i8k", "ihf", "bdw", "eb0", "eb", "shm", "dfm", "nid", "offd"):
    SCRATCH[_n] = ("sbuf", [128, 128], BF)
for _n in ("bdh", "idh", "in2k", "dm"):
    SCRATCH[_n] = ("sbuf", [128, 128], H1)
for _n in ("cu", "cq"):
    SCRATCH[_n] = ("sbuf", [128, 64], BF)
for _n in ("icol", "kint"):
    SCRATCH[_n] = ("sbuf", [128, 1], I3)
for _n in ("kcol", "sgcol", "thb", "k15", "k16", "cic"):
    SCRATCH[_n] = ("sbuf", [128, 1], F3)
for _c in range(NC):
    for _n, _w, _d in (("kg", 1024, BF), ("mx", 1024, BF), ("eg", 1024, BF), ("nr", 64, BF), ("ar", 64, F3),
                       ("xx", 64, H1), ("hn", 64, H1), ("sc", 128, F3), ("ci", 128, U1), ("pu", 64, F3), ("pv", 64, U1), ("wf", 64, BF), ("s1", 64, I3), ("s3", 64, I3),
                       ("vt", 64, F3), ("rs", 64, H1), ("rt", 64, H1) if not P["rev"] else ("zt", 64, BF), ("zz", 64, BF)):
        SCRATCH["%s%d" % (_n, _c)] = ("sbuf", [128, _w], _d)
    SCRATCH["psd%d" % _c] = ("psum", [128, 512], F3)
    SCRATCH["psx%d" % _c] = ("psum", [128, 512], F3)

SEMAPHORES = (["sV", "sS", "sP", "sG", "lsem", "outs"]
              + ["ld_" + n for n in ("keya", "keyb", "em", "em2", "cl", "pl", "q", "emb", "w", "th", "kp", "cp")]
              + ["a%s%d_%d" % (k, c, t) for k in "pq" for c in range(NC) for t in range(1, STEPS + 1)])


def plan(ops):
    n = len(ops)
    rng = np.random.RandomState(P["seed"])
    succ = [[] for _ in range(n)]
    for o in ops:
        for d in o["deps"] | o["order"]:
            succ[d].append(o["n"])
    prio = [0.0] * n
    left = [len(o["deps"] | o["order"]) for o in ops]
    topo_order = [i for i in range(n) if left[i] == 0]
    for i in topo_order:
        for j in succ[i]:
            left[j] -= 1
            if left[j] == 0:
                topo_order.append(j)
    for i in reversed(topo_order):
        o = ops[i]
        prio[i] = o["busy"] + o["lat"] + P["hop"] + max([prio[s] for s in succ[i]] + [0.0])
    prio = [p - P["stag"][o["c"]] for p, o in zip(prio, ops)]
    if P["noise"]:
        prio = [p + P["noise"] * float(r) for p, r in zip(prio, rng.standard_normal(n))]
    missing = [len(o["deps"] | o["order"]) for o in ops]
    ready = [0.0] * n
    free = {}
    start = [0.0] * n
    cand = [i for i in range(n) if missing[i] == 0]
    while cand:
        best, rows = None, []
        for i in cand:
            e = ops[i]["eng"]
            s = ready[i] if e == "NET" else max(free.get(e, 0.0), ready[i])
            rows.append((s, i, e))
            if best is None or s < best[0]:
                best = (s, i, e)
        lim = best[0] + min(P["look"], ops[best[1]]["busy"])
        s, i, e = max((r for r in rows if r[2] == best[2] and r[0] <= lim), key=lambda r: (prio[r[1]], -r[1]))
        o = ops[i]
        start[i] = s
        if e != "NET":
            free[e] = s + o["busy"]
        fin = s + o["busy"] + o["lat"]
        cand.remove(i)
        for j in succ[i]:
            missing[j] -= 1
            ready[j] = max(ready[j], fin + P["hop"] if i in ops[j]["deps"] else s)
            if missing[j] == 0:
                cand.append(j)
    return start


PLANS = {}
ORDER = ["020304051b1d1f1g1i3i3j3k01000d0n0b0i0q080z1510162g0a0c0h0l1106070u0y0r0x1p0o1v191z0p0w13180f1l0j0s1c0m0t0k171n0e1h1o0g0v14091x282j2m24252e262l1e121a2p391k1j1q1w1r201t1u231s1y27212b2h222a2d2f2k2n2u2q2t2w2v303b3f3l3o3m3n41494c4d4f4k4q4u534x4y1m2i31292r2s2y322o2z362x383e33373a3c3h3q3p3w40433z42464b4g4m4n4h4p4w5557585d5h5j5n665s5t2c353u343x3d3r3y3g3s443t454j3v47484a4e4i4l4o4r504s4v52565a5e5f5b5i5r6064656a6d6i6n6z6q6r4t514z545c5m5u5w5g5l5x595p5v5q686f5y6263676c6g6p616l6t706s6x777a7f7g7b7j7u84898a8d8j8o8s908w8x5k5z5o6h6b6y6o726m6v716k6w736u787e7476797c7h7k7l7n7t7y7s80868c8h8m8n8f8l8v929596999d9h9ka59q9r696j6e82757x7p7v7d7m7r7i7o7w7q7z8g818385878b8e8i8k8q8r8p8u8y979c9f9g919e9p9ya2a3a8abaeakaxapaq888t8z9a949l9s9u989i9o939j9t9na1aa9w9xa0a4a9adam9zaiaoauanasb3b7bcbdb8bgbsc1c6c7cbcgclcpcxdectcu9v9b9mafa6awalayajatazaharb2avb5bbb0b4b6b9bebhbiblbrbvbqbxc2c9cecjckcacicsczd3d4d6d9dddhe3e8dodpa7agacbzb1bpbmbubabjbobfbkbtbnbwcdbyc0c3c5c8cccfchcncocmcrcvd0d7dadccydbdndwe1e0e5eaefekf0fiepeqcqc4cwd8d2dkdjdqd5dgdmd1didrdle2e9dudvdydze6ebejdxegenewemetf3f6fbfcf7fffpg4gag9gdgjgogth0gwgxdsdfdtece4euelezeheoeyeeesf2erevfaexf4f5f8fdfgfhfrfvg0fufzg8gcghgmgngeglgvh2h5h7hahfhhhki6hqhreie7edg5f1fxfkfsf9fjfqfefmftfwg2ggfyg1g3g7gbgfgigkgpgrgqgugyh3h8hbhdh1hghphyi2i3i8icifilitiniogsg6gzhch6hnhshuh9hjhoh4hihthmi1ibhwhxi0i4i9iaihhzijiqixipivj4j7jcjdj8jgjsk1k6k7kakgklkpl3lbktkuhehvhligi7isimiziiiriyikiuj0iwj5jbj1j3j6j9jejijhjkjrjvjqjxk3k9kekjkkkckikskyl1l2l7ldlflgm3m7lnloi5ieidjzj2jojmjtjajjjpjfjljujnjwkdjyk0k2k4k8kbkfkhknkokmkrkvkzl4l8lakxlelmlwlzm0m5mamdmimxn5mnmokqk5kwl9l0lhlplql6lilrl5lklslllum4ltlxlym1m6mcmlm2mgmqmvmmmsn2ngoootoun7n8nso1o5o6oaoeoioqovp1owoxlclvljmem8mrmkmwmhmpmymfmun1mtn4ncmzn3n6n9nfnhninknrnvnqnzo2o9opozp5p8p9o7ogomoyp0p2p6papcplpnprpoppm9mjmbnyn0nlnnntndnjnpnenmnunonwocnxo0o3o4o8obodofojolohokonp3p7pbpepgpiorosp4pdpfphpkpmpqpsptpwpupvflfnfonanbpypxpjpzq0"]
C6 = ["020304051c1e1g1h1j3g3h3i01000d0m0b0g0r08101611172j0a0c0j0n1206070v0z0s0y1q0p1w1a1z0q0x14190f1m0k0t1d0o0u0l181o0e0h1i1p0i0w15091y292n2l25262f272p1f131b2x3c1l1k1v211s201r1t241u1x28222c2k232b2e2g2i2m2t2r2w302u2y32393f3m3o3n3p424a4e4h4k4o4t4y5752541n2h332a2s2o31372q2v382z3b3q343a3d3e3l3r3s3w41444043464b4g4l4p4q4j4s4z585d5c5g5m5o5t6d5y5z2d363v353y3k3u3z3j3t453x474f48494c4d4i4m4n4r4u514v4x50565a5e5h5j5k5n5w656b6c6g6k6q6v7i7071554w535i5f5r5v605b5p5u5l5q5x5s686l6264676a6f6j6o636n6u6x6r6w75797n7q7r7e7f808a8e8g8j8n8q8w9793945961667b6e726p6y6m6z766s6t7a737d7m747c7g7h7l7o7s7u7z857y84898d8k8p8t8u8h8r92989d9c9g9k9o9tac9y9z696i6h78777x7v817j7w827k7t837p878f86888b8c8i8l8m8o8s8y8v8x95969e9i9m9n999l9wa4abadagalaqatbnazb0918z909h9b9r9va09a9p9u9f9q9x9sa8aka2a3a6aaafajama5aoavb1arawb3b7bmbrbsbfbec0cacfcechclcscvd7dlczd0a19ja7b6aeb2apaxanayb5asaub8b9bdbkbabcbgbhblbobqbubzc2byc4c9cdcgckcqcrctcmd4d9dedddhdndpduedf0dze0aia9ahbbb4bxbvc7bibwc1bjbtc3bpc6coc5c8cbcccjcncpcucyd2cxd1d5d6dbdfdidkd8dodxe5ebecehelerewfnfvf2f3d3cicwdjdcdsdwe1dadqdvdgdrdydte8eme3e4e7eaegekeneeepeveyesexf5fafofsftfjfcg7gggmgkgqgugzh3hdh7h8dme2e6f9eff4eqezeof1f7eteuf8fdfifpfefffgfhfmfqfwfxg5gag3gcgfgjgpgtgxgygngwh5hehkhjhnhshuhziii3i4eje9eifbf6fufzg9fkfrg0flfyg8g1gbglgdgeghgigogrgsgvh1h6h2h4hahchghlhohqhfhti2iaigihimiqiuizjpj5j6h9h0hbhphmhyi1i6hhhwi0hihxi5hvidiri8i9icieilioiwijitj1j7ixj2j9jdjtjwjxjljkk6kgkmklkqkukzl3ldlsl8l9hri7ibjhikj8ivj3isj4jbiyj0jejfjjjsjgjijmjnjqjujvjzk4kbk5kakfkjkpktkxkykokwl6leljlkloltlvm0mmn6m5m6ipifinjcjak3k1k8jok0k7jrjyk9k2kckkkdkekhkiknkrkskvl1l7l2l4lblclglmlplrlflum3mbmimjmnmtmxn2nrnwn8n9lal0l5lqlilym2m7lhlwm1lnlxm4lzmemom9mamdmgmlmrmwmhmun1n4myn3nbnfnvoiooopnnnmo2ogoromouozp3p9pfpmpcpdllm8mcnjmsnamvn5mkn7ndmzn0ngnhnlntninknonpnunzo6o4obojoaoeoloqovpapephpjpkotp1p7plpqpppupyq0q3q5q9q6q7mfmqmpnencnyo5o8nqnxo3nso9odo7okoxocofohonosowoyp0p4p5p2p6p8pbpnprptpvpwpxpgpipopzq2q1q4q8qbqcqdqgqeqfg2g4g6o0o1qhqapsqiqj"]
C5 = ["020305061f1g1h1i1m3m3o3q04010b0p000c0s0l11131j181e0a0d0e0m0r07080w0v0t141k0g1z0z170j0x161c0f1a0i0u190y120q1b1p0h0o1d1r0k0n15091x2325282b2c2d2e2h1l101s2n3b1n1o1w201t261v1y271u2229242f2p212g2k2l2m2s2x2v2z382y32363e3k3t3v3u3y484c4l4g4m4p4v4x5551521q2a2u2j2o2q2w342r30352t3a3g31393c3d3j3p3w3x41474046494a4e4o4t4u4i4q50585b5c5f5k5n5q6b5y5z2i333r373n3f3h3l3i3s453z4d4h4243444b4f4j4k4n4s4w4r4y53565a5d5h5i5e5l5v64696a6e6h6k6o7m6y6z4z5754595j5s5t5w5m5r5x5g5p60616d6r626667686i6l6w6f6p71757074797d7q7v7w7g7h7y888d8c8g8k8p8t958y8z5o63655u6g6u6q786s6v776t727a6x7b7i737c7e7f7p7t7u7z838782868b8f8n8r90918j8o8x989a9b9e9i9n9pa99q9r6m6n6j6c767n7r807k7l7s7j7o7x818e8h8485898a8i8l8m8q8w938v9296999c9h9l9m9d9j9va4aaabaeaiamaublb0b1948s8u979g9t9w9x9k9u9z9f9sa0a1afaoa2a5a7a8agakaxadatazb5ayb3b9bcbobvbwbgbhbxc9cdccchcjcocxd7dhd1d29oa3a69yahb4alavapawb7aqb2bbasbabib6bdbebfbnbrbsbyc2c8c1c6cbcfckcrcsctcicqd0d9dbdcdldndpdqeaeedudvaranajacb8btbpbzbkbmbqbjbuc0c3cecmc4c5c7cacgclcncpcvd4cucyd3d8dadedidjdgdodxe5ebecegemeperfkfuf2f3d6cwczd5dfdwdsdydkdte0dddre3e1edeue2e7e8e9eleoexejeqf1f6ezf5fbfgfqfxfyfmfng0gegkgjgogsgvh2hdhahbdme4e6dzekf0evfeesewf8etf4fceyf7fifafdfffhfpfrg6ftg8gfg7g9gigmgph3h6h7gqgwh5hfhghhhlhohthvihi1i2efeheneif9fwfsg4flfofvfjg1g5gaghglgbgcgdgggngrgtgugygzgxh4h8hehjhnhrhshihqi3iaieidilioirivjtjbjch0h1hch9hmhzhyi4hpi0i5hkhwi7i9ikixi6icifigimiqj0ijiuj2j9j1j8jgjjjojujvjpjrk4kekjkikokrkvl2lclpl8l9hui8ibhxinj6iwjhiyizjdj3j4jfj5jajmj7jijkjljyk1k3k5k8kdk7kckhklktl1l6l7kpkwl5lflhlilmlslvlwmgmnm6m7isitipiijejwjzk6jqjsk0jnjxk2k9kkknkakbkfkgkmkqkskukyl0kxl3laldlglklqlrljlum1mcmhmimlmpmsmwnxo4n2n3lbkzl4lelolzlxm2ltm0m3lllym5m8mmmxm9mbmemfmqmtn5mkn0n7nen6nanhnlnoohooopnpnvo6ocomojosovp3pbpepkpfpglnmamdm4monbn1ncmyn4ngmzn8njn9ninrndnknmnnnunzo0o3oboloaodonotp6papjpppsptoyp0p7phplpmpqpupxq2q4q8q5q6mumvmrmjnfnyo2o9nqnto1nsnwo5oeorowofogoiokoqouoxozp2p5p1p4p8p9pipnprpwpypzpcpdpopvq0q1q3q7qaqbqdqgqeqffzg2g3o7o8qhqcq9qiqj"]
BEST3 = ["010204051b1c1e1f1h1k1l0300090g0e0l0r0o0w0y11181o0b0d0i0m0z06070n140v1m1v0p1z0s0q0t0x161d0j120h2810131g19080c0f1t200k151a0u1w0a1y2j2m2l2h2c2d2e2b2617212p3c1i1j1p241q221u1x271r1s29232f2v252g2k2n2q2t2w2u2y3a34373h3n3q3y3z40424a4i4n4l4q4u4y525556571n2a322s302r2x312o2z35393e3w333b3g3i3o3s3x3v414943484b4d4j4r4v4w4m4o5158595a5j5p5r5x6g60612i363r383p3d3f3l3k3m3u3j3t4g444546474c4e4h4f4k4s4p4t4x535b5h5m5n5d5e5o5u66656c6e6i6o786u6v4z50545c5v5q5y5g5s5z5f5t625w676m686a6b6d6h6j6n636k6p6r6s6x74757d7h7k7i7j7u85888a8e8h8l8o8w8z905l5k5i646y70766l6t716f6w73727e7v77797b7c7n7r7z7s7x8081868d8f8p8s8x8y8t8u94999e9f9i9n9p9vaca0a1696q836z7q7o7y7a7l7p7g7m7w7f7t8c828487898g8j8m8k8n928q919395989g9k9l9b9c9m9ua3a2aaadafakb4aoap8b8i968r9q9j9x979a9w8v9d9y9sa5aj9ra6a8a9aeagala4ahamaqaraub0b6babdbfbebhbsc1c7c5cbceciclcnd7cocp9h9o9t9zayawb1aiasaxabatazb2bbbob3b5b7b9bgbmbxbnbtbvbyc3c9cdcqcscwcxctcud1d6dcdbdidndpdseberdwdxa7anc8avbkbpbub8bibqbjblbrbcbwc6bzc0c2c4cccfcjchckczcmcyd0d3d5dgdldmdadfdkdrdzdye5eaedegexf8elemcacgd2crdddodtd4d8dvcvd9e0dee2eidue3e6e8eceeeje7efekeoepeteyf1f6f9fbfdfafug5gbgcgeghglgph5gwgxdhdjdqe1euezf2eheqewe9esf5f0fcfvf3f4fefffnfqfwfsfxg0g1g6gdgggogsgygzgtguh2h7hbhchhhnhphuichyhze4eng3evfmfpfyf7flfrfjfoftfifzgag2g4g7g8gfgigmgkgnh1gqh0h3h4h8hghkhlhdhfhmhti1i0i9idifilivirisg9gjh9grhqhohvh6hahxgvhei2hri5ijhwi6i8iaieigiki3ihimioipiuj1j6jajdjfjejjjtk1k6k4kbkekikll3ldkokphihjhsi4izixj3iiiqiyibitj0j2jbjpj4j5j7j9jhjmjqjnjujwjyk2k7kdknkukykzkrksl0l6l9lalflllnlsmdmklwlxi7ink0iwjljojvj8jcjxjijkjrjgjsk9jzk3k5k8kckgkjkhkkkwkmkvkxl1l5leljlkl7lclilrlzlym6mamcmgmyn5mmmnkakfl2kqlolmltl4l8lvktlbm0lpm3mhlum4m7m8mbmemlm2mfmpmqmrn3n8nenjoaofognunwocoloropouoxp0papcpjpdpelglhlqm1mumwn6mimomtm9msmxn0n4nomzn2n7n9ngnlnrnnnvo3nyo2o5o7odomotp3p5p6ohoioqowp1p2pbpgpkpopqpuprpsm5mjo4mvnkninpn1nfnmncnhnsndnqo1ntnxnzo0o6o8obo9oeonojokooosovp4p8p9phpioyozp7pfpmplpnppptpvpwpzpxpyfgfhfknanbq2q1q0q3q4"]
OLD = ["020304051a1d1f1h1i2d2f2h0100070e0b0j100v0p1317191q08090m0t1m0l0d140o0s150q1v180x1j1g161b0i0n0h0y0z1e1k1l060a0c2s2v0f0k0r0u1c0g24232k2e2a28292b20120w112w341o1n1r1w1s1t1x1u1y212o2u361z222c2i2l2y3d2z31333g3j3q3t40434749484c4l4n4q4t515355586f5a5b1p262p252g2m2j2n2r35373n2q2t38393c3l3s3m3p3r3u3w41454e4g4s4w4y4j4k4p5254575c5e5h5k6l5p5q27303f2x323e3a3b3i3x3z463h3k3o3v3y424b444a4h4d4f4i4m4o4r4u4z504v4x595d5f5j5m5o5s5u7n5z6056645n5v5r5x625i5t6a6m6o6w5y696b6g6i6s6z6t6u6y74777b7h7m7t7v7w7x81888e8i8l8o8p8q8u938y8z5g63616j67666d65686e707a7g6n6p6r6v727c7k7d7f7j7l7q7u7z84878d8g8h8a8b8k8r8t8x9295989bak9c9d5w5l6c716k6q6x6h73767r7s7y7578797e7i7o827p80868385898c8f8j8w90918m8n8v94979a9e9g9i9ka29p9q8s9h9f9s9m9r9u999ja19la5aa9t9ya0acaeaiasajamawavb0b4b6b9bebibkbjbtbxc4c8cbcfciclcpcudscrcs969x9n9w9za3a69va7abatazbbadahalaqaub1bdb2b7babgbmbpbrbvbyc3c6c7c0c1cacjcmcnctcwczd2dwdzd5d69oa8a4axa9aganafaoaparbfbnayb3b5b8bcbhboblbqbubsbwbzc2c5c9cecgchcccdcocvcyd1d3d7d9dce8eidfdgckcqd4didddhdkd0dadoe2e5eadjdldrdudye3ele4ebecenerevf4f9fefifjfkflfvg2g4g7gbgfgigkgqgngocxd8dedtdqdne0dmdpdvefetf3e6e9egehekeyf7f0f2f6f8fcfhfpfrfufwg0g1fyfzg6geghgjgpgsgvgyhhgzh0dbemdxeoe1e7edeeejepfdfgfmeqeseuf1f5fafnfbfffsfofqftfxg3g5gagcgdg8g9glgrgugxh1h3h5h7iwh8h9gggmgwhihahdhgh2h6hchkhxi8hjhmhnhphsi2idi3i5iaieihilioixj1j6j8j7jcjjjrjvjyk1k5k7k8ljllkbkcgth4hbhqhlhohthfhrhvhzi7iuhuhwibicifiniyiqiritizj4jbjfjijljqjtjujnjojxk6kakdkekkkokrlalxkukvhehyi4iii0i9i6i1igikj0j5jaijimipisivj2jdj3j9jhjejgjkjmjpjsk0k2k3jwjzk9kgkjklknkqktkxlclnl1l2k4khkil6l3kzl5kpkyl9lslzmcl7l8lblglmlymdm0m4m6memhmkmomun0njnmnnn4n5nentnwo0o8odogojooosopoqkfkml0lrlflelhl4lilom8mampltlwm1m7mbmjmsmlmnmrmtmyn3n8nandnsnvo1o4o5ngnlnrnzo3o6o7oboeohokowolomkwksldm9lplvm5lklqlumvmzn2mfmgmimmmqmwn6mxn1nbn7n9ncnfnhnkninpnunxnynonqo2o9oaocofoionorotouoxoyexezewm2m3p1ovp0ozp2"]


def join(lists):
    base, ops, sent = [], [], {}
    for r, l in enumerate(lists):
        base.append(len(ops))
        for o in l:
            b = base[r]
            ops.append(dict(o, n=o["n"] + b, deps={d + b for d in o["deps"]}, order={d + b for d in o["order"]},
                            eng=o["eng"] if o["eng"] == "NET" else o["eng"] + str(r)))
            if "sends" in o:
                sent[r, o["sends"]] = o["n"] + b
    for o in ops:
        if "from" in o:
            o["deps"].add(sent[o["from"], o["sem"]])
    return base, ops


def plan_all(lists):
    base, ops = join(lists)
    start = keyed(ops, order_of(ops), {o["name"]: float(int(ORDER[0][2 * j:2 * j + 2], 36)) for j, o in enumerate(lists[0])}) if ORDER[0] else plan(ops)
    return [start[base[r]:base[r] + len(l)] for r, l in enumerate(lists)]


def order_of(ops):
    succ = [[] for _ in ops]
    for o in ops:
        for d in o["deps"] | o["order"]:
            succ[d].append(o["n"])
    left = [len(o["deps"] | o["order"]) for o in ops]
    out = [i for i in range(len(ops)) if left[i] == 0]
    for i in out:
        for j in succ[i]:
            left[j] -= 1
            if left[j] == 0:
                out.append(j)
    return out


def keyed(ops, order, place):
    key = [0.0] * len(ops)
    for i in order:
        o = ops[i]
        k = place.get(o["name"], place.get(o["name"].replace("wf", "ph"), 0.0))
        for d in o["deps"] | o["order"]:
            if key[d] + 1e-4 > k:
                k = key[d] + 1e-4
        key[i] = k
    return key


def build(g, core, T, topo):
    rank = T.rank_of(core)
    cores = T.cores
    N = len(cores)
    V, S, PE, Y = g.vector, g.scalar, g.tensor, g.sync
    CY, FIX = P["cy"], P["fix"]
    ops = []
    lastw, readers, banks = {}, {}, {}
    cur = [0, -1]
    seen = {}
    lastld = {}
    na, nb = (1.0 / 4096, 0.0) if P["nr"] == "V" else (0.5, 0.5)
    za, zb = (1.0, 0.0) if P["z"] == "V" else (0.5, 0.5)
    MV, AB = P["MV"], P["AB"]
    vslots = sorted(i for s, n in MV for i in range(s, NS, n))
    turn = [0]

    def op(eng, emit, reads=(), writes=(), bank=None, busy=0.1, lat=0.0, sem=None, val=0):
        i = len(ops)
        deps, order = set(), set()
        for k in tuple(reads) + tuple(writes):
            if k in lastw:
                deps.add(lastw[k])
        for k in writes:
            deps.update(readers.get(k, ()))
        if bank:
            h = banks.setdefault(bank, {})
            for e, j in h.items():
                (order if e == eng else deps).add(j)
            h[eng] = i
        for k in reads:
            readers.setdefault(k, set()).add(i)
        for k in writes:
            lastw[k] = i
            readers[k] = set()
        tag = eng + (writes[0][:2] if writes else (bank[0] if bank else reads[0][0]))
        seen[tag] = seen.get(tag, -1) + 1
        ops.append({"n": i, "eng": eng, "emit": emit, "deps": deps, "order": order - deps, "busy": busy, "lat": lat, "sem": sem, "val": val,
                    "c": cur[0], "t": cur[1], "tag": tag + str(seen[tag]), "name": "%s%d.%d%d" % (tag, seen[tag], cur[0], cur[1] + 1)})
        return i

    def vd(cyc):
        return max(64, cyc) * CY + FIX

    def vts(out, in0, s1, s2, op0, op1, reads, writes, cyc=64, bank=None):
        if op1 is None:
            op("V", lambda: V.tensor_scalar(out, in0, s1, None, op0), reads, writes, bank, vd(cyc))
        else:
            op("V", lambda: V.tensor_scalar(out, in0, s1, s2, op0, op1), reads, writes, bank, vd(cyc))

    def vtt(out, in0, in1, o, reads, writes, cyc=64, bank=None):
        op("V", lambda: V.tensor_tensor(out, in0, in1, o), reads, writes, bank, vd(cyc))

    def vcp(out, in_, reads, writes, cyc=64, bank=None):
        op("V", lambda: V.tensor_copy(out, in_), reads, writes, bank, vd(cyc))

    def vfill(ap, x, reads, writes, cyc=64):
        op("V", lambda: V.memset(ap, x), reads, writes, None, vd(cyc))

    def scan(out, d0, d1, o0, o1, reads, writes, cyc=64, bank=None):
        op("V", lambda: V.tensor_tensor_scan(out, d0, d1, 0.0, o0, o1), reads, writes, bank, vd(cyc))

    def sact(out, in_, f, reads, writes, bank=None, cyc=64, **kw):
        op("S", lambda: S.activation(out, in_, f, **kw), reads, writes, bank, cyc * CY + 0.04)

    def gc(fn, writes, reads=(), busy=0.45):
        op("G", fn, reads, writes, None, busy)

    def mms(lst, reads, bank, writes=(), units=None):
        def emit():
            r = None
            for (o, l, x, a, b) in lst:
                r = PE.matmul(o, l, x, a, b)
            return r
        op("P", emit, reads, writes, bank, (units or len(lst)) * 64 * P["pe"] + 0.02)

    def load(q, out, in_, name, key, lat, after=()):
        i = op(q, lambda: (Y if q == "Y" else S).dma_start(out, in_), after, (key,), None, 0.1, lat, "ld_" + name, 16)
        if q in lastld:
            ops[i]["order"].add(lastld[q])
        lastld[q] = i

    ka, mb = P["ka"], P["mb"]
    load("S", T.pl_s[:], T.pl[:], "pl", "pl_s", 2.0)
    load("Y", T.key_s[:, 16:16 + ka], T.key[:, 0:ka], "keya", "keya", 1.5 + 0.75 * mb)
    load("Y", T.key_s[:, 16 + ka:4112], T.key[:, ka:], "keyb", "keyb", 1.5 + mb)
    load("S", T.qin[:, 0:192], T.q[:], "q", "q0", 2.2)
    load("Y", T.w_s[:], T.w[:], "w", "w", 2.0, ("keya",))
    load("Y", T.th_s[:], T.th[:], "th", "th", 2.0)
    load("Y", T.cl_s[:, 8:2056], T.cl[:], "cl", "cl", 1.5 + 2 * mb)
    load("Y", T.emb_s[:], T.emb[:], "emb", "emb", 2.0)
    load("Y", T.em_s[:, 0:4096], T.em[:], "em", "em", 1.5 + 2 * mb, ("keyb",))
    if P["dbl"]:
        load("Y", T.em_s[:, 4096:8192], T.em[:], "em2", "em2", 1.5 + mb, ("em", "cl"))
    if rank == 0:
        load("Y", T.key_s[:, 4112:4128], T.key[:, 0:16], "kp", "kp", 2.0)
        load("Y", T.cl_s[:, 2056:2064], T.cl[:, 0:8], "cp", "cp", 2.0)
    if rank == N - 1:
        load("Y", T.key_s[:, 0:16], T.key[:, 4080:4096], "kp", "kp", 2.0)
        load("Y", T.cl_s[:, 0:8], T.cl[:, 2040:2048], "cp", "cp", 2.0)

    one64 = T.ones[:, 0:64]
    vfill(T.ones[:], 1.0, (), ("ones",))
    gc(lambda: g.iota(T.icol[:], [[0, 1]], 0, 1), ("icol",), (), 0.2)
    gc(lambda: g.affine_select(T.bd[:], T.ones[:], [[-16, 8], [0, 16]], A.is_ge, 0.0, 0, 1), ("bd",), ("ones",))
    gc(lambda: g.affine_select(T.bd[:], T.bd[:], [[16, 8], [0, 16]], A.is_ge, 0.0, 15, -1), ("bd",))
    gc(lambda: g.iota(T.repi[:], [[16, 64]], 0, 0), ("repi",), (), 0.3)
    gc(lambda: g.affine_select(T.idm[:], T.ones[:], [[-1, 128]], A.is_equal, 0.0, 0, 1), ("idm",), ("ones",))
    gc(lambda: g.affine_select(T.ltm[:], T.bd[:], [[1, 128]], A.is_gt, 0.0, 0, -1), ("ltm",), ("bd",))
    gc(lambda: g.iota(T.rowm[:], [[0, 4], [1, 16]], 0, 0, allow_small_or_imprecise_dtypes=True), ("rowm",), (), 0.3)
    gc(lambda: g.affine_select(T.shm[:], T.bd[:], [[-1, 128]], A.is_equal, 0.0, -1, 1), ("shm",), ("bd",))
    for c in range(NC):
        vcp(T.pin[:, 64 * c:64 * c + 64], T.pl_s[:, 64 * c:64 * c + 64], ("pl_s",), ("p%d_0" % c,))
    vts(T.phin[:, 0:192], T.pl_s[:], -2048.0, None, A.add, None, ("pl_s",), ("ph0",), 192)
    vts(T.kint[:], T.icol[:], 15, None, A.bitwise_and, None, ("icol",), ("kint",))
    vcp(T.kcol[:], T.kint[:], ("kint",), ("kcol",))
    vts(T.repj[:], T.repi[:], T.kcol[:, 0:1], None, A.add, None, ("repi", "kcol"), ("repj",))
    rep0 = {1: 0, 2: 64, 4: 96}
    for n in sorted({n for s, n in MV}):
        a, b = rep0[n], rep0[n] + 64 // n
        vts(T.repk[:, a:b], T.repj[:, 0:64 // n], {1: 4, 2: 3, 4: 2}[n], None, A.logical_shift_right, None, ("repj",), ("repk%d" % n,))
        vcp(T.rep[:, a:b], T.repk[:, a:b], ("repk%d" % n,), ("rep%d" % n,))
    vfill(T.wk[:], 0.0, (), ("wk",), 72)
    vfill(T.w2[:], 0.0, (), ("w2",), 72)
    vts(T.wk[:, 16:144:16], T.bd[:, 0:128:16], -1.0, None, A.mult, None, ("bd",), ("wk",))
    vts(T.w2[:, 16:144:16], T.bd[:, 0:128:16], 2.0, None, A.mult, None, ("bd",), ("w2",))
    sact(T.nbd[:], T.bd[:], F.Copy, ("bd",), ("nbd",), None, 128, scale=-1.0)
    for s, n in AB:
        vfill(T.nbd[:, s:128:n], 0.0, (), ("nbd",))
    sact(T.nid[:], T.idm[:], F.Copy, ("idm",), ("nid",), None, 128, scale=-1.0)
    vts(T.bdw[:], T.bd[:], T.w_s[:, 0:1], None, A.mult, None, ("bd", "w"), ("bdw",))
    vcp(T.idh[:], T.idm[:], ("idm",), ("idh",))
    vts(T.in2k[:], T.idm[:], -2048.0, None, A.mult, None, ("idm",), ("in2k",))
    sact(T.i8k[:], T.idm[:], F.Copy, ("idm",), ("i8k",), None, 128, scale=8192.0 * na)
    sact(T.bd4k[:], T.bd[:], F.Copy, ("bd",), ("bd4k",), None, 128, scale=4096.0 * na)
    if nb:
        vts(T.thb[:], T.th_s[:], -0.5, None, A.add, None, ("th",), ("thb",))
    vtt(T.gw0[:], T.idm[:], T.ltm[:], A.subtract, ("idm", "ltm"), ("gw0",), 256)
    sact(T.gw[:], T.gw0[:], F.Copy, ("gw0",), ("gw",), None, 128, scale=4096.0 * na)
    vts(T.cu[:], one64, T.kcol[:, 0:1], None, A.mult, None, ("ones", "kcol"), ("cu",))
    vts(T.cu[:], T.cu[:], -4096.0 * nb, 4096.0 * nb - 2048.0, A.mult, A.add, (), ("cu",))
    vts(T.sgcol[:], T.kcol[:], -2048.0 * na, 28672.0 * na, A.mult, A.add, ("kcol",), ("sgcol",))
    vts(T.sg[:], T.bd[:], T.sgcol[:, 0:1], None, A.mult, None, ("bd", "sgcol"), ("sg",))
    vts(T.bdh[:], T.bd[:], 0.5, None, A.mult, None, ("bd",), ("bdh",))
    k0 = 18432.0 + 2048.0 * 104 * nb
    k1 = (3145728.0 if P["sf16"] else 0.0) + 65536.0 * nb
    ta, tb = T.sc0[:, 0:64], T.sc0[:, 64:128]
    if P["sc4"]:
        vts(T.seg[:], T.rowm[:], 1.0, T.kcol[:, 0:1], A.add, A.is_equal, ("rowm", "kcol"), ("seg",))
        vts(ta, T.seg[:], 8388608.0, None, A.mult, None, ("seg",), ("ta",))
        vts(tb, T.rowm[:], T.kcol[:, 0:1], -4096.0, A.is_equal, A.mult, ("rowm", "kcol"), ("tb",))
        vtt(T.rst[:, 1:128:2], ta, tb, A.add, ("ta", "tb", "sc0"), ("rsa",), 128)
        vts(T.rst[:, 31:32], T.rst[:, 31:32], k1 + 4096.0, None, A.add, None, (), ("rsa",))
        vts(T.rst[:, 0:128:2], T.rowm[:], T.kcol[:, 0:1], k0 - k1 - 0.25, A.is_equal, A.mult, ("rowm", "kcol"), ("rsb",))
        if rank == N - 1:
            vcp(T.r2[:, 1:128:2], T.rst[:, 1:128:2], ("rsa",), ("r2a",))
            vts(T.r2[:, 31:32], T.r2[:, 31:32], 8.0, None, A.add, None, (), ("r2a",))
            vts(T.r2[:, 0:128:2], T.rowm[:], T.kcol[:, 0:1], k0 - k1 - 0.75, A.is_equal, A.mult, ("rowm", "kcol"), ("r2b",))
    else:
        vts(T.seg[:], T.rowm[:], -1.0, T.kcol[:, 0:1], A.add, A.is_equal, ("rowm", "kcol"), ("seg",))
        vts(ta, T.seg[:], -4096.0, None, A.mult, None, ("seg",), ("ta",))
        vts(tb, T.rowm[:], T.kcol[:, 0:1], 8388608.0, A.is_equal, A.mult, ("rowm", "kcol"), ("tb",))
        vtt(T.rst[:, 0:128:2], ta, tb, A.add, ("ta", "tb", "sc0"), ("rsa",), 128)
        vts(T.rst[:, 1:128:2], T.rowm[:], T.kcol[:, 0:1], k0 - k1 - 0.25, A.is_equal, A.mult, ("rowm", "kcol"), ("rsb",))
        vts(T.cic[:], T.kcol[:], 15.0, 4096.0, A.is_lt, A.mult, ("kcol",), ("cic",))
        vts(T.cic[:], T.cic[:], BIG + k1, None, A.add, None, (), ("cic",))
        if rank == N - 1:
            vcp(T.r2[:, 0:128:2], T.rst[:, 0:128:2], ("rsa",), ("r2a",))
            vts(T.r2[:, 1:128:2], T.rowm[:], T.kcol[:, 0:1], k0 - k1 - 0.75, A.is_equal, A.mult, ("rowm", "kcol"), ("r2b",))
    vfill(T.seg[:], 4096.0, (), ("seg",))
    vfill(T.seg[:, 0:64:16], -4096.0, (), ("seg",))
    if any(P["VS"]):
        vfill(T.sm[:], 1.0, (), ("sm",), 512)
        vfill(T.sm[:, 0:1024:16], 0.0, (), ("sm",))
    vts(T.k15[:], T.kcol[:], 15.0, None, A.is_equal, None, ("kcol",), ("k15",))
    sact(T.ihf[:], T.idm[:], F.Copy, ("idm",), ("ihf",), None, 128, scale=0.5)
    vcp(T.bdc[:], T.bd[:, 0:128:16], ("bd",), ("bdc",))
    vfill(T.tw[:], 0.0, (), ("tw",))
    vcp(T.tw[:, 0:8], T.bd[:, 0:128:16], ("bd",), ("tw",))
    ebk = tuple("eb%d" % b for b in range(8))
    for b in range(8):
        vts(T.eb0[:, 16 * b:16 * b + 16], T.emb_s[:], T.bdc[:, b:b + 1], None, A.mult, None, ("emb", "bdc"), (ebk[b],))
    vtt(T.dfm[:], T.idm[:], T.shm[:], A.subtract, ("idm", "shm"), ("dfm",), 256)
    if zb:
        mms([(T.psx2[:, 0:128], T.dfm[:], T.eb0[:], True, True)], ebk + ("dfm",), "X2", (), 2)
    else:
        vts(T.k16[:], T.k15[:], 1.0 / 16, None, A.mult, None, ("k15",), ("k16",))
        vts(T.offd[:], T.bd[:], -1.0, T.k16[:, 0:1], A.add, A.mult, ("bd", "k16"), ("offd",))
        mms([(T.psx2[:, 0:128], T.idm[:], T.offd[:], True, False), (T.psx2[:, 0:128], T.dfm[:], T.eb0[:], False, True)],
            ebk + ("dfm", "idm", "offd"), "X2", (), 4)
    sact(T.eb[:], T.psx2[:, 0:128], F.Copy, (), ("eb",), "X2", 128, scale=0.5 * za)
    if zb:
        mms([(T.psx2[:, 128:192], T.eb[:], one64, True, True)], ("eb", "ones"), "X2")
        sact(T.cq[:], T.psx2[:, 128:192], F.Identity, (), ("cq",), "X2", bias=-0.25)

    def gather(e, out, win, off, reads, writes, count, bias=None):
        if e == "S":
            fn = (lambda: S.activation(out, win.indirect(off), F.Copy)) if bias is None else (lambda: S.activation(out, win.indirect(off), F.Identity, bias=bias))
        else:
            fn = (lambda: V.tensor_copy(out, win.indirect(off))) if bias is None else (lambda: V.tensor_scalar(out, win.indirect(off), bias, None, A.add))
        op(e, fn, reads, writes, None, 0.07 + count * P["gather"] * CY)

    sends = [0]

    def send(dst, pairs, sem, keys, akeys, most, last):
        eng = topo.engines(core, dst)
        eng = eng[-most:] if last else eng[:most]
        rid, pid, _ = topo.addr(dst)
        sends[0] += len(eng)
        if len(pairs) == 1:
            m = sum(1 << x for x in eng)
            fn = lambda: g.remote_dma(pairs[0][0], pairs[0][1], T.sem[sem], T.sem.lsem, pid, rid, m)
        else:
            h = len(eng) // len(pairs)
            trs = [RemoteDMATransfer(dst_ids=[DstId(rid=rid, pnc=pid)], dma_engine_mask=sum(1 << x for x in eng[h * j:h * j + h]),
                                     remote_sem=T.sem[sem], src=s, dst=d) for j, (d, s) in enumerate(pairs)]
            fn = lambda: g.remote_dma_fused(trs, local_sem=T.sem.lsem)
        i = op("G", fn, keys, (), None, 0.15)
        ops[i]["remote"] = True
        ops[i]["sends"] = sem
        frm = (2 * rank - cores.index(dst)) % N
        ne = min(most, len(topo.engines(cores[frm], core)))
        j = op("NET", None, (), akeys, None, 0.0, P["net"] + P["row"] * 128 * len(pairs) / ne, sem, ne)
        ops[j]["from"] = frm

    def step(t, c):
        cur[0], cur[1] = c, t
        seen.clear()
        B = lambda n: T["%s%d" % (n, c)]
        k = lambda n: "%s%d" % (n, c)
        o0 = t * 192 + NL * c
        o1 = o0 + 192
        ph, qin = T.phin[:, o0:o0 + NL], T.qin[:, o0:o0 + NL]
        pkey = "p%d_%d" % (c, t)
        hkey = "ph%d_%d" % (c, t) if t else "ph0"
        qkey = "q%d_%d" % (c, t) if t else "q0"
        psd, psx = B("psd"), B("psx")
        bd, bx = "D%d" % c, "X%d" % c
        kg, mx, eg, nr = B("kg"), B("mx"), B("eg"), B("nr")[:]
        D, U, AR, PP, P2 = (psd[:, 64 * j:64 * j + 64] for j in range(5))
        CH, C0, C1 = psx[:, 0:128], psx[:, 0:128:2], psx[:, 1:128:2]
        HA, VO, DL, QO = (psx[:, 128 + 64 * j:192 + 64 * j] for j in range(4))
        up, down = t > 0 and c == 0 and rank == 0, t > 0 and c > 0 and rank == N - 1
        kwin = T.key_s[:, 16:4128] if up else (T.key_s[:, 0:4112] if down else T.key_s[:, 16:4112])
        cwin = T.cl_s[:, 8:2064] if up else (T.cl_s[:, 0:2056] if down else T.cl_s[:, 8:2056])
        kp, cp = (("kp",), ("cp",)) if up or down else ((), ())
        kgk, a = [], 0
        for e, w in (P["K"][c] if t else P["K0"][c]):
            kgk.append("%s_%d" % (k("kg"), a))
            gather(e, kg[:, 16 * a:16 * (a + w)], kwin, T.pin[:, o0 + a:o0 + a + w], ("keya", "keyb", pkey) + kp, (kgk[-1],), 16 * w)
            a += w
        kgk = tuple(kgk)
        if t:
            vts(ph, T.pin[:, o0:o0 + NL], -2063.0 if down else -2048.0, None, A.add, None, (pkey,), (hkey,))
        if MV:
            mms([(D, T.wk[:, 16 - i:144 - i], kg[:, i:1024:16], i == vslots[0], False) for i in vslots], kgk + ("wk",), bd)
            mms([(D, T.nbd[:], qin, False, False)], ("nbd", qkey), bd)
        pieces, a = [], 0
        for s, n in MV:
            w = 1024 // n
            pieces.append((a, s, n, "%s_%d" % (k("mx"), a)))
            op("V", lambda a=a, s=s, n=n, w=w: V.tensor_tensor(mx[:, a:a + w], qin.indirect(T.rep[:, rep0[n]:rep0[n] + 64 // n]), kg[:, s:1024:n], A.max),
               ("rep%d" % n, qkey) + kgk, (pieces[-1][3],), None, 0.06 + w * P["gather"] * CY)
            a += w
        for s, n in AB:
            w, u = 1024 // n, P["AS"]
            df, bf = T["pst%d" % turn[0]], "F%d" % turn[0]
            turn[0] = 1 - turn[0]
            mms([(df[:, 0:w], T.idm[:], kg[:, s:1024:n], True, False)], kgk + ("idm",), bf, (), w // 64)
            mms([(df[:, r:w:16 // n], T.nid[:], qin, False, r == 16 // n - 1) for r in range(16 // n)], ("nid", qkey), bf)
            for j in range(u):
                pieces.append((a, s + n * j, n * u, "%s_%d" % (k("ab"), a)))
                sact(mx[:, a:a + w // u], df[:, j:w:u], F.Abs, (), (pieces[-1][3],), bf, w // u, scale=0.5)
                a += w // u
        HA = C1 if P["ha"] else HA
        mms([(HA, T.bdw[:], qin, True, True)], ("bdw", qkey), bx)
        sact(B("hn")[:], HA, F.Identity, (), (k("hn"),), bx, bias=1536.0 - 1023.5 / 2048.0, scale=1.0 / 2048.0)
        mms(([] if P["ha"] else [(C1, T.bdw[:], qin, True, False)]) + [(C1, T.in2k[:], B("hn")[:], False, False)], ("in2k", k("hn")), bx)
        po = P["PO"] or range(len(pieces))
        for j in po:
            a, s, n, nm = pieces[j]
            mms([(D, T.w2[:, 16 - s - n * r:144 - s - n * r], mx[:, a + r:a + 1024 // n:16 // n], not MV and j == po[0] and r == 0,
                  j == po[-1] and r == 16 // n - 1) for r in range(16 // n)], (nm, "w2"), bd)
        if not nb:
            vts(nr, D, T.th_s[:, 0:1], 1.0 / na, A.is_lt, A.mult, ("th",), (k("nr"),), 64, bd)
        else:
            sact(nr, D, F.Sign, ("thb",), (k("nr"),), bd, bias=T.thb[:, 0:1], scale=-1.0)
        mms([(U, T.idm[:], T.cu[:], True, False), (U, T.gw[:], nr, False, True)], ("idm", "cu", "gw", k("nr")), bd)
        mms([(C1, T.bd4k[:], nr, False, True), (C0, T.sg[:], nr, True, False)], ("bd4k", "sg", k("nr")), bx)
        sab = P["u16"] == 3
        wrap = []
        if sab and (up or down):
            vts(B("wf")[:], T.pin[:, o0:o0 + NL], 4096.0 if up else 15.0, (-0.5 if up else 0.5) / na, A.is_equal, A.mult, (pkey,), (k("wf"),))
            wrap = [(AR, T.i8k[:], B("wf")[:], False, False)]
        if P["arl"]:
            vtt(B("xx")[:], U, ph, A.min, (hkey,), (k("xx"),), 64, bd)
        mms([(AR, T.idh[:], ph, True, False)] + wrap + [(AR, T.i8k[:], nr, False, True)], ("idh", "i8k", k("nr"), hkey, k("wf")), bd)
        if not P["arl"]:
            vtt(B("xx")[:], U, ph, A.min, (hkey,), (k("xx"),), 64, bd)
        if sab and not P["dbl"]:
            sact(B("ar")[:], AR, F.Identity, (), (k("ar"),), bd, bias=8192.0 * (1 - nb) - (2047.0 if down else 2048.0), scale=-1.0)
        else:
            sact(B("ar")[:], AR, F.Identity, (), (k("ar"),), bd, bias=8192.0 * nb - (2049.0 if down else 2048.0))
        mms([(C0, T.bdh[:], B("xx")[:], False, True)], ("bdh", k("xx")), bx)
        if P["sc4"]:
            def four():
                r = None
                for h in range(4):
                    r = V.tensor_tensor_scan(B("ci")[:, h:128:4], psx[:, 32 * h:32 * h + 32], (T.r2 if down else T.rst)[:, 0:32], 8388608.0, A.min, A.add)
                return r
            op("V", four, ("r2a", "r2b") if down else ("rsa", "rsb"), (k("ci"),), bx, vd(256))
            cil = B("ci")[:, 124:128]
        else:
            scan(B("sc")[:], T.r2[:] if down else T.rst[:], CH, A.add, A.min, ("r2a", "r2b") if down else ("rsa", "rsb"), (k("sc"),), 128, bx)
            vts(B("ci")[:, 0:4], B("sc")[:, 31:128:32], T.cic[:, 0:1], BIG - (8.0 if down else 0.0), A.add, A.subtract, (k("sc"), "cic"), (k("ci"),))
            cil = B("ci")[:, 0:4]
        pf = B("pv")[:] if P["dbl"] else B("pu")[:]
        op("V", lambda: V.tensor_tensor(pf, cwin.indirect(cil), B("ar")[:], A.max if P["dbl"] else A.min),
           ("cl", k("ci"), k("ar")) + cp, (k("pf"),), None, 0.06 + 64 * P["gather"] * CY)
        pok = "po%d_%d" % (c, t)
        if P["u16"]:
            si, sik = T.pout[:, o0:o0 + NL], pok
            if P["dbl"]:
                vtt(si, pf, nr, A.subtract, (k("pf"), k("nr")), (sik,), 128)
            else:
                sact(si, pf, F.Abs, (k("pf"),), (sik,))
        else:
            vts(si, pf, 4095, None, A.bitwise_and, None, (k("pf"),), (sik,))
            vcp(T.pout[:, o0:o0 + NL], si, (sik,), (pok,))
        nxt = cores[(rank + 1) % N if c == 0 else (rank - 1) % N]
        shift = 1.0 if (c == 0 and rank == N - 1) else (-1.0 if (c and rank == 0) else 0.0)
        a1 = "ap%d_%d" % (c, t + 1)
        if t == STEPS - 1:
            a, b = NL * c, NL * c + NL
            if shift:
                vts(B("s1")[:], si, shift + 4096.0, None, A.add, None, (sik,), (k("s1"),))
                si, sik = B("s3")[:], k("s3")
                vts(si, B("s1")[:], 4095, None, A.bitwise_and, None, (k("s1"),), (sik,))
            vcp(T.ypo[:, a:b], si, (sik,), ("ypo%d" % c,))
            send(nxt, [(T.yp_s[:, a:b], T.ypo[:, a:b])], a1, ("ypo%d" % c,), ("yp%d" % c,), P["peng"], True)
        else:
            src, sk = T.pout[:, o0:o0 + NL], pok
            if shift:
                src, sk = T.pw[:, o0:o0 + NL], "pw%d_%d" % (c, t)
                vts(src, si, 1.0 if shift > 0 else 15.0, None, A.add, None, (sik,), (sk,))
            send(nxt, [(T.pin[:, o1:o1 + NL], src)], a1, (sk,), ("p%d_%d" % (c, t + 1),), P["peng"], True)
        egk, a = [], 0
        for e, w in P["E"][c]:
            egk.append("%s_%d" % (k("eg"), a))
            if P["dbl"] and t:
                gather(e, eg[:, 16 * a:16 * (a + w)], T.em_s[:], B("pv")[:, a:a + w], ("em", "em2", k("pf")), (egk[-1],), 16 * w, -128.0)
            else:
                gather(e, eg[:, 16 * a:16 * (a + w)], T.em_s[:, 0:4096], T.pout[:, o0 + a:o0 + a + w], ("em", pok), (egk[-1],), 16 * w, -128.0)
            if P["VS"][c]:
                scan(B("vs")[:, 16 * a:16 * (a + w)], T.sm[:, 0:16 * w], eg[:, 16 * a:16 * (a + w)], A.mult, A.add, ("sm", egk[-1]),
                     ("%s_%d" % (k("vs"), a),), 8 * w)
                egk[-1] = "%s_%d" % (k("vs"), a)
            a += w
        vn = "vh" if P["VS"][c] else "vt"
        if P["VS"][c]:
            op("V", lambda: V.transpose(B("vh")[:], B("vs")[:, 15:1024:16]), tuple(egk), (k("vt"),), None, vd(64))
        else:
            mms([(VO, T.idm[:], eg[:, i:1024:16], i == 0, i == NS - 1) for i in range(NS)], tuple(egk) + ("idm",), bx)
            op("V", lambda: V.transpose(B("vt")[:], VO), (), (k("vt"),), bx, vd(64))
        scan(B("rs")[:], T.seg[:], B(vn)[:], A.min, A.max, ("seg", k("vt")), (k("rs"),))
        if P["rev"]:
            scan(psx[:, 319:255:-1], T.seg[:], B(vn)[:, ::-1], A.min, A.max, ("seg", k("vt")), (k("sx"),), 64, bx)
            vtt(B("zt")[:], B("rs")[:], DL, A.is_ge, (k("rs"), k("sx")), (k("zt"),), 64, bx)
            op("V", lambda: V.transpose(B("zz")[:], B("zt")[:]), (k("zt"),), (k("zz"),), None, vd(64))
        else:
            op("V", lambda: V.transpose(B("rt")[:], B("rs")[:]), (k("rs"),), (k("rt"),), None, vd(64))
            mms([(DL, T.dm[:], B("rt")[:], True, True)], ("dm", k("rt")), bx)
        if P["rev"]:
            pass
        elif za == 1.0:
            vts(B("zz")[:], DL, 0.5, None, A.is_lt, None, (), (k("zz"),), 64, bx)
        else:
            sact(B("zz")[:], DL, F.Sign, (), (k("zz"),), bx, bias=0.5, scale=-1.0)
        mms([(QO, T.ihf[:], qin, True, False)] + ([(QO, T.idm[:], T.cq[:], False, False)] if zb else []) + [(QO, T.eb[:], B("zz")[:], False, True)],
            ("idm", "cq", "ihf", "eb", qkey, k("zz")), bx)
        qok = "qo%d_%d" % (c, t)
        vts(T.qout[:, o0:o0 + NL], QO, BIG, BIG, A.add, A.subtract, (), (qok,), 64, bx)
        a, b = 32 * (t % 3), 384 + 64 * (t // 3)
        mms([(psx[a:a + 32, b:b + 64], T.tw[:], B("zz")[:], True, True)], ("tw", k("zz")), bx, (k("tk"),))
        if t in (2, 4, 5):
            a, (u, v) = 192 * (t // 3) + 64 * c, {2: (0, 96), 4: (0, 64), 5: (64, 96)}[t]
            sact(T.yt_s[u:v, a:a + 64], psx[u:v, b:b + 64], F.Identity, (), ("yt%d_%d" % (c, t),), bx, bias=16.0 * (1 - zb), scale=-za)
        send(nxt, [(T.qin[:, o1:o1 + NL], T.qout[:, o0:o0 + NL])], "aq%d_%d" % (c, t + 1), (qok,), ("q%d_%d" % (c, t + 1),), P["qeng"], False)

    for t in range(STEPS):
        for c in range(NC):
            step(t, c)
    nout = [0]
    cur[1] = STEPS

    def store(out, in_, reads):
        nout[0] += 16
        op("Y", lambda: Y.dma_start(out, in_), reads, (), None, 0.1, 2.0, "outs", None)

    o6 = STEPS * 192
    for t in range(STEPS):
        a, b = 32 * (t % 3), 192 * (t // 3)
        store(T.yt[:, 192 * t:192 * t + 192], T.yt_s[a:a + 8, b:b + 192], tuple("yt%d_%d" % (c, (2, 2, 2, 4, 4, 5)[t]) for c in range(NC)))
    store(T.yp[:], T.yp_s[:], tuple("yp%d" % c for c in range(NC)))
    for c in range(NC):
        a, b = NL * c, NL * c + NL
        store(T.yq[:, a:b], T.qin[:, o6 + a:o6 + b], ("q%d_%d" % (c, STEPS),))
    return ops, sends[0], nout[0]


def emit_all(g, T, ops, start, nsend, nout):
    eng = {"V": g.vector, "S": g.scalar, "P": g.tensor, "G": g, "Y": g.sync}
    esem = {"V": "sV", "S": "sS", "P": "sP", "G": "sG"}
    count = {e: 0 for e in eng}
    known = {e: {} for e in eng}
    fin = {}
    for i in sorted(range(len(ops)), key=lambda x: (start[x], x)):
        o = ops[i]
        e = o["eng"]
        if e == "NET":
            fin[i] = (o["sem"], o["val"], {o["sem"]: o["val"]})
            continue
        kn = known[e]
        need = {}
        for d in o["deps"]:
            s, v, _ = fin[d]
            if kn.get(s, 0) < v and need.get(s, (0, None))[0] < v:
                need[s] = (v, d)
        for s in list(need):
            v = need[s][0]
            if any(s2 != s and fin[need[s2][1]][2].get(s, 0) >= v for s2 in need):
                del need[s]
        for s in sorted(need):
            v, d = need[s]
            eng[e].wait_ge(T.sem[s], v)
            for s2, v2 in fin[d][2].items():
                if kn.get(s2, 0) < v2:
                    kn[s2] = v2
        ins = o["emit"]()
        c = dict(kn)
        if o["sem"] is not None:
            ins.then_inc(T.sem[o["sem"]], 16)
            if o["val"]:
                c[o["sem"]] = o["val"]
            fin[i] = (o["sem"], o["val"], c)
        elif not o.get("remote"):
            count[e] += 1
            ins.then_inc(T.sem[esem[e]], 1)
            c[esem[e]] = count[e]
            fin[i] = (esem[e], count[e], c)
    g.wait_ge(T.sem.lsem, nsend)
    for e in ("V", "S", "P", "G"):
        g.wait_ge(T.sem[esem[e]], count[e])
    g.sync.wait_ge(T.sem.outs, nout)


def rank_program(g, core, T, topo):
    if T.rank_of(core) is None:
        return
    ops, nsend, nout = build(g, core, T, topo)
    key = repr(sorted(P.items())) + ORDER[0]
    if key not in PLANS:
        PLANS[key] = plan_all([build(g, c, T, topo)[0] for c in T.cores])
    emit_all(g, T, ops, PLANS[key][T.rank_of(core)], nsend, nout)
